import numpy as np
import ml_dtypes


def mxq(x, axis, fmt="e4m3"):
    dtype, down = {"e4m3": (ml_dtypes.float8_e4m3fn, 7), "e5m2": (ml_dtypes.float8_e5m2, 14)}[fmt]
    v = np.moveaxis(np.asarray(x, np.float32).astype(ml_dtypes.bfloat16).astype(np.float64), axis, -1)
    blocks = v.reshape(v.shape[:-1] + (-1, 32))
    amax = np.abs(blocks).max(-1, keepdims=True)
    byte = np.maximum(np.where(amax > 0, np.frexp(amax)[1] - 1 + 127, 0) - down, 1)
    scale = np.exp2(byte - 127.0)
    codes = (blocks / scale).astype(np.float32).astype(dtype).astype(np.float64)
    return np.moveaxis((codes * scale).reshape(v.shape), -1, axis)


WIDE = False


def mx_kscale(k):
    if not WIDE:
        return np.ones(k)
    levels = np.array([10, -10, 5, -5, 0])
    if k % 512:
        return np.exp2(np.random.permutation(np.resize(levels, k // 32))).repeat(32)
    a = np.empty((k // 512, 16))
    for p in range(k // 512):
        a[p, :8] = np.random.permutation(np.resize(levels, 8))
        for g in range(8):
            far = levels[np.abs(levels - a[p, g]) >= 10]
            a[p, g + 8] = far[np.random.randint(len(far))]
    return np.exp2(a.ravel()).repeat(32)


def f64(x):
    return np.asarray(x).astype(np.float64)


def striped(idx):
    return np.tile(np.asarray(idx).reshape(-1, 16).T, (8, 1)).astype(np.uint16)


def unstriped(offs):
    return offs[:16].T.reshape(-1).astype(np.int64)


E2M1 = np.array([0.0, 0.5, 1.0, 1.5, 2.0, 3.0, 4.0, 6.0, -0.0, -0.5, -1.0, -1.5, -2.0, -3.0, -4.0, -6.0])


def pack_weight(w, fmt):
    k, n = w.shape
    w = f64(np.asarray(w, np.float32).astype(ml_dtypes.bfloat16)).reshape(k // 32, 32, n)
    amax = np.abs(w).max(1)
    if fmt == "e4m3":
        byte = np.frexp(amax)[1] - 1 + 127 - 7
    else:
        mant, ex = np.frexp(amax / 6.0)
        byte = np.where(mant > 0.5, ex, ex - 1) + 127
    byte = np.clip(np.where(amax > 0, byte, 1), 1, 254)
    scaled = (w * np.exp2(127.0 - byte)[:, None, :]).reshape(k, n).astype(np.float32)
    by_word = np.ascontiguousarray(scaled.reshape(k // 512, 128, 4, n).transpose(0, 1, 3, 2))
    if fmt == "e4m3":
        words = by_word.astype(ml_dtypes.float8_e4m3fn).view(np.uint8)
    else:
        c = by_word.astype(ml_dtypes.float4_e2m1fn).view(np.uint8) & 0xF
        words = (c[..., 0::2] | (c[..., 1::2] << 4)).reshape(k // 512, 128, 2 * n)
    return np.ascontiguousarray(words), np.ascontiguousarray(byte.astype(np.uint8).reshape(k // 512, 16, n))


def unpack_weight(words, scales, fmt):
    g, _, n = scales.shape
    words = np.ascontiguousarray(words).reshape(g, 128, n, -1)
    if fmt == "e4m3":
        vals = words.view(ml_dtypes.float8_e4m3fn).astype(np.float64)
    else:
        nib = np.empty((g, 128, n, 4), np.uint8)
        nib[..., 0::2] = words & 0xF
        nib[..., 1::2] = words >> 4
        vals = E2M1[nib]
    vals = vals * np.repeat(np.exp2(scales.astype(np.float64) - 127.0), 8, axis=1)[..., None]
    return vals.transpose(0, 1, 3, 2).reshape(g * 512, n)


B, N, T, D, DV, NQ = 2, 512, 2048, 1024, 256, 256
DRAFT = 128


def setup_inputs():
    n = np.random.standard_normal
    seg = T // B
    idx = np.concatenate([b * seg + np.random.permutation(seg)[:N] for b in range(B)])
    s = mx_kscale(D)[:, None]
    u = np.ones(T)
    u[idx] = mx_kscale(B * N)
    r = np.random.uniform(0.5, 2.0, T)
    qp = [pack_weight(x, "e4m3") for x in n((B, D, NQ)) * s * (0.80 / np.sqrt(D))]
    k = n((D, T)) / s
    v = n((DV, T)) / (u * r)
    kp = pack_weight(k, "e2m1")
    when = np.zeros(T)
    when[idx] = np.concatenate([np.concatenate([np.arange(N - DRAFT), N - DRAFT + np.random.randint(0, 16, DRAFT)]) for b in range(B)])
    return {
        "q_words": np.stack([x[0] for x in qp]),
        "q_scales": np.stack([x[1] for x in qp]),
        "k_words": np.ascontiguousarray(kp[0].reshape(D // 1024, 2, 128, T, 2).transpose(0, 2, 3, 1, 4)).reshape(D // 1024, 128, T, 4),
        "k_scales": kp[1],
        "vT": v.astype(np.float32),
        "vs": np.tile(u * r, (128, 1)).astype(np.float32),
        "pos": np.tile(when, (128, 1)).astype(np.float32),
        "qpos": np.random.randint(N - DRAFT, N - DRAFT + 16, (B, NQ, 1)).astype(np.float32),
        "offs": striped(idx),
    }


def reference(q_words, q_scales, k_words, k_scales, vT, vs, pos, qpos, offs):
    idx = unstriped(offs)
    k = unpack_weight(k_words.reshape(D // 1024, 128, T, 2, 2).transpose(0, 3, 1, 2, 4).reshape(D // 512, 128, 2 * T), k_scales, "e2m1")
    v = f64(vT)
    pick = lambda x: x[:, idx].reshape(x.shape[0], B, N).transpose(1, 0, 2)
    q = np.stack([unpack_weight(q_words[b], q_scales[b], "e4m3") for b in range(B)])
    score = q.transpose(0, 2, 1) @ pick(k)
    score = np.where(pick(f64(pos))[:, :1, :] <= f64(qpos), score, -30000.0)
    m = score.max(-1, keepdims=True)
    p = np.exp(score - m)
    total = p.sum(-1, keepdims=True)
    w = p * pick(f64(vs))[:, :1, :]
    y = mxq(w, 2, "e4m3") @ mxq(pick(v).transpose(0, 2, 1), 1, "e4m3")
    y = y / total
    return y

@@ -1,0 +1,237 @@
+from contextlib import ExitStack
+
+import concourse.mybir as mybir
+from concourse.masks import make_identity
+
+B, N, T, D, DV, NQ = 2, 512, 2048, 1024, 256, 256
+FLOPS = 2 * B * NQ * N * (D + DV)
+BYTES = B * D * NQ + B * D * NQ // 32 + D * T // 2 + D * T // 32 + 4 * DV * T + 2 * 4 * T + 4 * B * NQ + 2 * 128 * 64 + 4 * B * NQ * DV
+
+F32 = mybir.dt.float32
+BF16 = mybir.dt.bfloat16
+I32 = mybir.dt.int32
+U32 = mybir.dt.uint32
+U16 = mybir.dt.uint16
+U8 = mybir.dt.uint8
+FP8X4 = mybir.dt.float8_e4m3fn_x4
+FP4X4 = mybir.dt.float4_e2m1fn_x4
+ALU = mybir.AluOpType
+ACT = mybir.ActivationFunctionType
+
+P = 128
+PACK = 4
+PASSES = D // (P * PACK)
+SEG = T // B
+QT = NQ // P
+LIST_COLS = N // 16
+MASKED = 30000.0
+STEEP = 2.0 ** 60
+
+
+def tile_attend_soft_draft_segb2q256n512t2048_kernel(tc, q_words, q_scales, k_words, k_scales, vT, vs, pos, qpos, offs, out):
+    nc = tc.nc
+    with ExitStack() as ctx:
+        keep = ctx.enter_context(tc.tile_pool(name="keep", bufs=1))
+        work = ctx.enter_context(tc.tile_pool(name="work", bufs=2))
+        psum = ctx.enter_context(tc.psum_pool(name="psum", bufs=2))
+        banks = ctx.enter_context(tc.psum_pool(name="banks", bufs=1))
+        rows = ctx.enter_context(tc.tile_pool(name="rows", bufs=B * QT))
+
+        offsets = keep.tile([P, B * LIST_COLS], U16, name="offsets")
+        k_pool = keep.tile([P, T], I32, name="k_pool", align_bytes=64)
+        ks_pool = keep.tile([P, T], U8, name="ks_pool", align_bytes=64)
+        q_codes = [keep.tile([P, PASSES, NQ], I32, name=f"q_codes{b}", align_bytes=64) for b in range(B)]
+        q_planes = keep.tile([P, B * PASSES * NQ], U8, name="q_planes", align_bytes=64)
+        pos_pool = keep.tile([P, T], F32, name="pos_pool")
+        vs_pool = keep.tile([P, T], F32, name="vs_pool")
+        v_raw = [keep.tile([P, 2, SEG], F32, name=f"v_raw{b}") for b in range(B)]
+        v_pool = keep.tile([P, T], I32, name="v_pool", tag="v_pool", align_bytes=64)
+        q_place = keep.tile([P, B * QT], F32, name="q_place")
+        q_bias = keep.tile([P, B * QT], F32, name="q_bias")
+        ks_got = keep.tile([P, B * N], U8, name="ks_got", align_bytes=64)
+        k_planes = keep.tile([P, PASSES * B * N], U8, name="k_planes", align_bytes=64)
+        vs_got = keep.tile([P, B * N], F32, name="vs_got")
+        ident = keep.tile([P, P], F32, name="ident")
+        warm = keep.tile([P, 1], F32, name="warm")
+
+        nc.vector.memset(q_planes[:].bitcast(I32), 0)
+        nc.vector.memset(warm[:], 0.0)
+        nc.vector.memset(ks_pool[0:96, :].bitcast(I32), 0)
+        nc.vector.memset(k_planes[:].bitcast(I32), 0)
+        nc.scalar.activation(warm[:], warm[:], ACT.Exp)
+        make_identity(nc, ident[:])
+        nc.gpsimd.memset(vs_pool[0 : P - 1, :], 0.0)
+
+        k_hbm = k_words[0].rearrange("p t r -> p (t r)").bitcast(I32)
+        nc.sync.dma_start(offsets[:], offs)
+        nc.sync.dma_start(ks_pool[96:P, :].bitcast(I32), k_scales.rearrange("o f t -> f o t").bitcast(I32))
+
+        def stretch(b):
+            return slice(b * SEG, (b + 1) * SEG)
+
+        def load_queries(b):
+            nc.sync.dma_start(q_codes[b][:], q_words[b].rearrange("o p q r -> p o (q r)").bitcast(I32))
+
+        def load_values(b):
+            nc.sync.dma_start(v_raw[b][:], vT[:, stretch(b)].rearrange("(c h) t -> c h t", h=2))
+
+        nc.sync.dma_start(vs_pool[P - 1 : P, :], vs[0:1, :])
+        for b in range(B):
+            load_values(b)
+            nc.sync.dma_start(k_pool[:, stretch(b)], k_hbm[:, stretch(b)])
+        for b in range(B):
+            nc.sync.dma_start(pos_pool[:, stretch(b)], pos[:, stretch(b)])
+        with nc.allow_non_contiguous_dma(reason="one place a partition"):
+            nc.sync.dma_start(q_place[:], qpos.rearrange("b (j p) o -> p (b j o)", p=P))
+        for b in range(B):
+            load_queries(b)
+        for quad in range(4):
+            nc.sync.dma_start(
+                q_planes[32 * quad : 32 * quad + 4, :].bitcast(I32).rearrange("j (g q) -> j g q", g=B * PASSES),
+                q_scales[:, :, 4 * quad : 4 * quad + 4, :].rearrange("b o j q -> j (b o) q").bitcast(I32),
+            )
+
+        nc.vector.tensor_copy(ks_got[:], ks_pool[:].indirect(offsets[:]))
+        for quad in range(4):
+            nc.sync.dma_start(k_planes[32 * quad : 32 * quad + 4, :].bitcast(I32), ks_got[96 + 8 * quad : 96 + 8 * quad + 8, :].bitcast(I32))
+        nc.vector.tensor_copy(vs_got[:], vs_pool[:].indirect(offsets[:]))
+        nc.vector.tensor_scalar(q_bias[:], q_place[:], -STEEP, None, ALU.mult)
+
+        def window(pool, b):
+            return pool[:, 0 : (b + 1) * SEG]
+
+        def listed(b):
+            return offsets[:, b * LIST_COLS : (b + 1) * LIST_COLS]
+
+        def keys(b):
+            both = work.tile([P, N], U32, name="k_both")
+            nc.vector.tensor_copy(both[:], window(k_pool, b).bitcast(U32).indirect(listed(b)))
+            parted = work.tile([P, PASSES * 2 * N], U8, name="k_parted", align_bytes=64)
+            nc.vector.tensor_copy(
+                parted[:].bitcast(U16).rearrange("p (o n) -> p o n", o=PASSES),
+                both[:].bitcast(U16).rearrange("p (n o) -> p o n", o=PASSES),
+            )
+            return parted
+
+        def places(b):
+            got = work.tile([P, N], F32, name="pos_got")
+            nc.vector.tensor_copy(got[:], window(pos_pool, b).indirect(listed(b)))
+            return got
+
+        def scores(b, j, parted):
+            bank = banks.tile([P, N], F32, name="scores", tag=f"bank{b * QT + j}")
+            for o in range(PASSES):
+                first = (b * PASSES + o) * NQ + j * P
+                nc.tensor.matmul_mx(
+                    out=bank[:],
+                    lhsT=q_codes[b][:, o, j * P : (j + 1) * P].bitcast(FP8X4),
+                    lhsT_scale=q_planes[:, first : first + P],
+                    rhs=parted[:, o * 2 * N : (o + 1) * 2 * N].bitcast(FP4X4),
+                    rhs_scale=k_planes[:, (o * B + b) * N : (o * B + b + 1) * N],
+                    start=(o == 0),
+                    stop=(o == PASSES - 1),
+                )
+            return bank
+
+        def penalty(b, j, pos_got):
+            tile = rows.tile([P, N], F32, name="penalty")
+            nc.scalar.activation(
+                tile[:].rearrange("p (t c i) -> p c t i", t=PACK, i=4),
+                pos_got[:].rearrange("p (c i t) -> p c t i", t=PACK, i=4),
+                ACT.Relu, bias=q_bias[:, b * QT + j : b * QT + j + 1], scale=STEEP,
+            )
+            return tile
+
+        def mask(negated, bank, pen):
+            nc.vector.tensor_tensor(
+                negated.rearrange("p (t s) -> p t s", t=PACK), pen[:].rearrange("p (t s) -> p t s", t=PACK),
+                bank[:].rearrange("p (s t) -> p t s", t=PACK), ALU.subtract,
+            )
+
+        def softmax(u, negated):
+            capped = rows.tile([P, N], F32, name="capped")
+            low = rows.tile([P, 1], F32, name="low")
+            nc.vector.tensor_scalar(capped[:], negated, MASKED, None, ALU.min, ALU.min, accum_out=low[:])
+            p = rows.tile([P, PACK, P], F32, name="p")
+            total = rows.tile([P, 1], F32, name="total")
+            nc.scalar.activation(p[:].rearrange("p t s -> p (t s)"), capped[:], ACT.Exp, bias=low[:], scale=-1.0, accum_out=total[:])
+            turned = banks.tile([P, PACK, P], F32, name="p_turned", tag=f"bank{u}")
+            for t in range(PACK):
+                nc.tensor.transpose(turned[:, t, :], p[:, t, :], ident[:])
+            return turned, total
+
+        def token_scales(b):
+            turned = psum.tile([P, PACK, P], F32, name="turned")
+            for t in range(PACK):
+                nc.tensor.transpose(turned[:, t, :], vs_got[:, b * N + t : (b + 1) * N : PACK], ident[:])
+            cols = work.tile([P, PACK], F32, name="vs_cols")
+            nc.scalar.copy(cols[:], turned[:, :, P - 1])
+            return cols
+
+        def cast_values(b):
+            nc.scalar.activation(
+                v_pool[:, b * SEG : (b + 1) * SEG].bitcast(BF16).rearrange("p (t h) -> p t h", h=2),
+                v_raw[b][:].rearrange("p h t -> p t h"), ACT.Copy,
+            )
+
+        def values(b):
+            pairs = work.tile([P, N], U32, name="v_pairs")
+            nc.vector.tensor_copy(pairs[:], window(v_pool, b).bitcast(U32).indirect(listed(b)))
+            turned = psum.tile([P, PACK, P], F32, name="turned")
+            for t in range(PACK):
+                nc.tensor.transpose(turned[:, t, :], pairs[:].bitcast(F32)[:, t:N:PACK], ident[:])
+            grouped = work.tile([P, DV, PACK], BF16, name="v_grouped", align_bytes=64)
+            nc.scalar.copy(grouped[:], turned[:].rearrange("p t c -> p (t c)").bitcast(BF16).rearrange("p (t e) -> p e t", t=PACK))
+            codes = work.tile([P, DV], U32, name="v_codes", align_bytes=64)
+            plane = work.tile([P, DV], U8, name="v_plane", align_bytes=64)
+            nc.vector.quantize_mx(out=codes[:].bitcast(FP8X4), scales=plane[:], in_=grouped[:].rearrange("p e t -> p (e t)"))
+            return codes, plane
+
+        def weights(turned, vs_cols):
+            grouped = rows.tile([P, P, PACK], BF16, name="w_grouped", align_bytes=64)
+            nc.vector.tensor_tensor(
+                grouped[:], turned[:].rearrange("p t q -> p q t"),
+                vs_cols[:].unsqueeze(1).to_broadcast([P, P, PACK]), ALU.mult,
+            )
+            return grouped
+
+        def finish(b, j, grouped, total, v_codes, v_plane):
+            codes = rows.tile([P, P], U32, name="w_codes", align_bytes=64)
+            plane = rows.tile([P, P], U8, name="w_plane", align_bytes=64)
+            inverse = rows.tile([P, 1], F32, name="inverse")
+            nc.vector.reciprocal(inverse[:], total[:])
+            nc.vector.quantize_mx(out=codes[:].bitcast(FP8X4), scales=plane[:], in_=grouped[:].rearrange("p q t -> p (q t)"))
+            sums = psum.tile([P, DV], F32, name="sums")
+            nc.tensor.matmul_mx(
+                out=sums[:], lhsT=codes[:].bitcast(FP8X4), lhsT_scale=plane[:],
+                rhs=v_codes[:].bitcast(FP8X4), rhs_scale=v_plane[:], start=True, stop=True,
+            )
+            result = rows.tile([P, DV], F32, name="result")
+            nc.scalar.activation(result[:], sums[:], ACT.Copy, scale=inverse[:])
+            nc.sync.dma_start(out[b, j * P : (j + 1) * P, :], result[:])
+
+        tiles = [(b, j) for b in range(B) for j in range(QT)]
+        score, pen, vs_cols, v_mx = [], [], [], []
+        parted = []
+        for b in range(B):
+            cast_values(b)
+            vs_cols.append(token_scales(b))
+            parted.append(keys(b))
+            v_mx.append(values(b))
+        for b in range(B):
+            pos_got = places(b)
+            score.extend(scores(b, j, parted[b]) for j in range(QT))
+            pen.extend(penalty(b, j, pos_got) for j in range(QT))
+        negated = keep.tile([P, B * QT * N], F32, name="negated", tag="v_pool", align_bytes=64)
+        part = [negated[:, u * N : (u + 1) * N] for u in range(B * QT)]
+        soft = []
+        mask(part[0], score[0], pen[0])
+        for u in range(B * QT):
+            if u + 1 < B * QT:
+                mask(part[u + 1], score[u + 1], pen[u + 1])
+            soft.append(softmax(u, part[u]))
+        grouped = [weights(soft[0][0], vs_cols[0])]
+        for u, (b, j) in enumerate(tiles):
+            if u + 1 < B * QT:
+                grouped.append(weights(soft[u + 1][0], vs_cols[tiles[u + 1][0]]))
+            finish(b, j, grouped[u], soft[u][1], *v_mx[b])

@@ -25,7 +25,9 @@ SEG = T // B
 QT = NQ // P
 LIST_COLS = N // 16
 MASKED = 30000.0
-STEEP = 2.0 ** 60
+STEEP = 2.0 ** 80
+NUDGE = 2.0 ** -22
+FLOOR = 2.0 ** 40
 
 
 def tile_attend_soft_draft_segb2q256n512t2048_kernel(tc, q_words, q_scales, k_words, k_scales, vT, vs, pos, qpos, offs, out):
@@ -44,23 +46,31 @@ def tile_attend_soft_draft_segb2q256n512t2048_kernel(tc, q_words, q_scales, k_wo
         q_planes = keep.tile([P, B * PASSES * NQ], U8, name="q_planes", align_bytes=64)
         pos_pool = keep.tile([P, T], F32, name="pos_pool")
         vs_pool = keep.tile([P, T], F32, name="vs_pool")
-        v_raw = [keep.tile([P, 2, SEG], F32, name=f"v_raw{b}") for b in range(B)]
-        v_pool = keep.tile([P, T], I32, name="v_pool", tag="v_pool", align_bytes=64)
+        v_raw = [keep.tile([P, 2, SEG], F32, name=f"v_raw{b}", tag=f"v_raw{b}") for b in range(B)]
+        v_pool = keep.tile([P, B * 2 * SEG], BF16, name="v_pool", align_bytes=64)
         q_place = keep.tile([P, B * QT], F32, name="q_place")
-        q_bias = keep.tile([P, B * QT], F32, name="q_bias")
+        q_up = keep.tile([P, B * QT], F32, name="q_up")
+        q_down = keep.tile([P, B * QT], F32, name="q_down")
+        q_edge = keep.tile([P, B * QT], F32, name="q_edge")
+        total = keep.tile([P, B * QT], F32, name="total")
+        inverse = keep.tile([P, B * QT], F32, name="inverse")
+        ident_bf = keep.tile([P, P], BF16, name="ident_bf")
         ks_got = keep.tile([P, B * N], U8, name="ks_got", align_bytes=64)
         k_planes = keep.tile([P, PASSES * B * N], U8, name="k_planes", align_bytes=64)
         vs_got = keep.tile([P, B * N], F32, name="vs_got")
+        pos_got = keep.tile([P, B * N], F32, name="pos_got")
         ident = keep.tile([P, P], F32, name="ident")
         warm = keep.tile([P, 1], F32, name="warm")
 
-        nc.vector.memset(q_planes[:].bitcast(I32), 0)
         nc.vector.memset(warm[:], 0.0)
         nc.vector.memset(ks_pool[0:96, :].bitcast(I32), 0)
-        nc.vector.memset(k_planes[:].bitcast(I32), 0)
+        nc.vector.memset(vs_pool[0 : P - 1, :], 0.0)
+        nc.gpsimd.memset(pos_pool[0 : P - 1, :], 0.0)
+        nc.gpsimd.memset(q_planes[:].bitcast(I32), 0)
+        nc.gpsimd.memset(k_planes[:].bitcast(I32), 0)
         nc.scalar.activation(warm[:], warm[:], ACT.Exp)
         make_identity(nc, ident[:])
-        nc.gpsimd.memset(vs_pool[0 : P - 1, :], 0.0)
+        make_identity(nc, ident_bf[:])
 
         k_hbm = k_words[0].rearrange("p t r -> p (t r)").bitcast(I32)
         nc.sync.dma_start(offsets[:], offs)
@@ -73,29 +83,27 @@ def tile_attend_soft_draft_segb2q256n512t2048_kernel(tc, q_words, q_scales, k_wo
             nc.sync.dma_start(q_codes[b][:], q_words[b].rearrange("o p q r -> p o (q r)").bitcast(I32))
 
         def load_values(b):
-            nc.sync.dma_start(v_raw[b][:], vT[:, stretch(b)].rearrange("(c h) t -> c h t", h=2))
+            nc.sync.dma_start(v_raw[b][:], vT[:, stretch(b)].rearrange("(h c) t -> c h t", h=2))
 
+        nc.sync.dma_start(pos_pool[P - 1 : P, :], pos[0:1, :])
         nc.sync.dma_start(vs_pool[P - 1 : P, :], vs[0:1, :])
         for b in range(B):
             load_values(b)
-            nc.sync.dma_start(k_pool[:, stretch(b)], k_hbm[:, stretch(b)])
         for b in range(B):
-            nc.sync.dma_start(pos_pool[:, stretch(b)], pos[:, stretch(b)])
+            nc.sync.dma_start(k_pool[:, stretch(b)], k_hbm[:, stretch(b)])
+            load_queries(b)
         with nc.allow_non_contiguous_dma(reason="one place a partition"):
             nc.sync.dma_start(q_place[:], qpos.rearrange("b (j p) o -> p (b j o)", p=P))
-        for b in range(B):
-            load_queries(b)
         for quad in range(4):
             nc.sync.dma_start(
                 q_planes[32 * quad : 32 * quad + 4, :].bitcast(I32).rearrange("j (g q) -> j g q", g=B * PASSES),
                 q_scales[:, :, 4 * quad : 4 * quad + 4, :].rearrange("b o j q -> j (b o) q").bitcast(I32),
             )
-
         nc.vector.tensor_copy(ks_got[:], ks_pool[:].indirect(offsets[:]))
         for quad in range(4):
             nc.sync.dma_start(k_planes[32 * quad : 32 * quad + 4, :].bitcast(I32), ks_got[96 + 8 * quad : 96 + 8 * quad + 8, :].bitcast(I32))
+        nc.vector.tensor_copy(pos_got[:], pos_pool[:].indirect(offsets[:]))
         nc.vector.tensor_copy(vs_got[:], vs_pool[:].indirect(offsets[:]))
-        nc.vector.tensor_scalar(q_bias[:], q_place[:], -STEEP, None, ALU.mult)
 
         def window(pool, b):
             return pool[:, 0 : (b + 1) * SEG]
@@ -113,10 +121,19 @@ def tile_attend_soft_draft_segb2q256n512t2048_kernel(tc, q_words, q_scales, k_wo
             )
             return parted
 
-        def places(b):
-            got = work.tile([P, N], F32, name="pos_got")
-            nc.vector.tensor_copy(got[:], window(pos_pool, b).indirect(listed(b)))
-            return got
+        def place_columns(b, cols):
+            turned = psum.tile([P, PACK, P], F32, name="pos_turned", tag="turned")
+            for c in range(PACK):
+                nc.tensor.transpose(turned[:, c, :], pos_got[:, b * N + c * P : b * N + (c + 1) * P], ident[:])
+            nc.scalar.mul(cols, turned[:, :, P - 1], -STEEP)
+
+        def place_row(b, cols):
+            spread = psum.tile([P, PACK, P], F32, name="pos_spread", tag="turned")
+            for c in range(PACK):
+                nc.tensor.transpose(spread[:, c, :], cols[:, c : c + 1].to_broadcast([P, P]), ident[:])
+            row = keep.tile([P, N], F32, name="pos_row", tag=f"pos_row{b}", align_bytes=64)
+            nc.scalar.copy(row[:], spread[:].rearrange("p c s -> p (c s)"))
+            return row
 
         def scores(b, j, parted):
             bank = banks.tile([P, N], F32, name="scores", tag=f"bank{b * QT + j}")
@@ -133,56 +150,56 @@ def tile_attend_soft_draft_segb2q256n512t2048_kernel(tc, q_words, q_scales, k_wo
                 )
             return bank
 
-        def penalty(b, j, pos_got):
-            tile = rows.tile([P, N], F32, name="penalty")
-            nc.scalar.activation(
-                tile[:].rearrange("p (t c i) -> p c t i", t=PACK, i=4),
-                pos_got[:].rearrange("p (c i t) -> p c t i", t=PACK, i=4),
-                ACT.Relu, bias=q_bias[:, b * QT + j : b * QT + j + 1], scale=STEEP,
-            )
-            return tile
+        def mask(u, bank, pos_row):
+            masked = rows.tile([P, N], F32, name="masked")
+            nc.vector.scalar_tensor_tensor(masked[:], pos_row[:], q_edge[:, u : u + 1], bank[:], ALU.add, ALU.min)
+            return masked
 
-        def mask(negated, bank, pen):
-            nc.vector.tensor_tensor(
-                negated.rearrange("p (t s) -> p t s", t=PACK), pen[:].rearrange("p (t s) -> p t s", t=PACK),
-                bank[:].rearrange("p (s t) -> p t s", t=PACK), ALU.subtract,
-            )
-
-        def softmax(u, negated):
+        def softmax(u, masked):
             capped = rows.tile([P, N], F32, name="capped")
-            low = rows.tile([P, 1], F32, name="low")
-            nc.vector.tensor_scalar(capped[:], negated, MASKED, None, ALU.min, ALU.min, accum_out=low[:])
-            p = rows.tile([P, PACK, P], F32, name="p")
-            total = rows.tile([P, 1], F32, name="total")
-            nc.scalar.activation(p[:].rearrange("p t s -> p (t s)"), capped[:], ACT.Exp, bias=low[:], scale=-1.0, accum_out=total[:])
-            turned = banks.tile([P, PACK, P], F32, name="p_turned", tag=f"bank{u}")
+            top = rows.tile([P, 1], F32, name="top")
+            nc.vector.tensor_scalar(capped[:], masked[:], -MASKED, None, ALU.max, ALU.max, accum_out=top[:])
+            shift = rows.tile([P, 1], F32, name="shift")
+            nc.scalar.mul(shift[:], top[:], -1.0)
+            p = rows.tile([P, N], F32, name="p")
+            nc.scalar.activation(
+                p[:].rearrange("p (t c i) -> p c t i", t=PACK, i=4),
+                capped[:].rearrange("p (c i t) -> p c t i", t=PACK, i=4),
+                ACT.Exp, bias=shift[:], accum_out=total[:, u : u + 1],
+            )
+            if u + 1 < B * QT:
+                turned = banks.tile([P, PACK, P], F32, name="p_turned", tag=f"bank{u}")
+            else:
+                turned = psum.tile([P, PACK, P], F32, name="p_turned", tag="turned")
             for t in range(PACK):
-                nc.tensor.transpose(turned[:, t, :], p[:, t, :], ident[:])
-            return turned, total
+                nc.tensor.transpose(turned[:, t, :], p[:, t * P : (t + 1) * P], ident[:])
+            return turned
 
-        def token_scales(b):
-            turned = psum.tile([P, PACK, P], F32, name="turned")
+        def token_scales(b, turned, cols):
             for t in range(PACK):
                 nc.tensor.transpose(turned[:, t, :], vs_got[:, b * N + t : (b + 1) * N : PACK], ident[:])
-            cols = work.tile([P, PACK], F32, name="vs_cols")
-            nc.scalar.copy(cols[:], turned[:, :, P - 1])
-            return cols
+            nc.scalar.copy(cols, turned[:, :, P - 1])
 
         def cast_values(b):
-            nc.scalar.activation(
-                v_pool[:, b * SEG : (b + 1) * SEG].bitcast(BF16).rearrange("p (t h) -> p t h", h=2),
-                v_raw[b][:].rearrange("p h t -> p t h"), ACT.Copy,
-            )
+            nc.scalar.activation(v_pool[:, 2 * b * SEG : 2 * (b + 1) * SEG], v_raw[b][:].rearrange("p h t -> p (h t)"), ACT.Copy)
 
-        def values(b):
-            pairs = work.tile([P, N], U32, name="v_pairs")
-            nc.vector.tensor_copy(pairs[:], window(v_pool, b).bitcast(U32).indirect(listed(b)))
-            turned = psum.tile([P, PACK, P], F32, name="turned")
-            for t in range(PACK):
-                nc.tensor.transpose(turned[:, t, :], pairs[:].bitcast(F32)[:, t:N:PACK], ident[:])
+        def gather_values(b):
+            got = work.tile([P, 2, PACK, P], BF16, name="v_got")
+            for h in range(2):
+                end = (2 * b + h + 1) * SEG
+                nc.scalar.activation(got[:, h].rearrange("p t s -> p s t"), v_pool[:, end - (b + 1) * SEG : end].indirect(listed(b)), ACT.Copy)
+            return got
+
+        def turn_values(got, turned):
+            for h in range(2):
+                for t in range(PACK):
+                    nc.tensor.transpose(turned[:, t, h, :], got[:, h, t, :], ident_bf[:])
+            return turned
+
+        def quantise_values(b, turned):
             grouped = work.tile([P, DV, PACK], BF16, name="v_grouped", align_bytes=64)
-            nc.scalar.copy(grouped[:], turned[:].rearrange("p t c -> p (t c)").bitcast(BF16).rearrange("p (t e) -> p e t", t=PACK))
-            codes = work.tile([P, DV], U32, name="v_codes", align_bytes=64)
+            nc.scalar.copy(grouped[:], turned[:].rearrange("p t h c -> p (h c) t"))
+            codes = keep.tile([P, DV], U32, name="v_codes", tag=f"pos_row{B - 1 - b}", align_bytes=64)
             plane = work.tile([P, DV], U8, name="v_plane", align_bytes=64)
             nc.vector.quantize_mx(out=codes[:].bitcast(FP8X4), scales=plane[:], in_=grouped[:].rearrange("p e t -> p (e t)"))
             return codes, plane
@@ -191,47 +208,57 @@ def tile_attend_soft_draft_segb2q256n512t2048_kernel(tc, q_words, q_scales, k_wo
             grouped = rows.tile([P, P, PACK], BF16, name="w_grouped", align_bytes=64)
             nc.vector.tensor_tensor(
                 grouped[:], turned[:].rearrange("p t q -> p q t"),
-                vs_cols[:].unsqueeze(1).to_broadcast([P, P, PACK]), ALU.mult,
+                vs_cols.unsqueeze(1).to_broadcast([P, P, PACK]), ALU.mult,
             )
             return grouped
 
-        def finish(b, j, grouped, total, v_codes, v_plane):
+        def finish(b, j, grouped, v_codes, v_plane):
             codes = rows.tile([P, P], U32, name="w_codes", align_bytes=64)
             plane = rows.tile([P, P], U8, name="w_plane", align_bytes=64)
-            inverse = rows.tile([P, 1], F32, name="inverse")
-            nc.vector.reciprocal(inverse[:], total[:])
             nc.vector.quantize_mx(out=codes[:].bitcast(FP8X4), scales=plane[:], in_=grouped[:].rearrange("p q t -> p (q t)"))
-            sums = psum.tile([P, DV], F32, name="sums")
+            sums = psum.tile([P, DV], F32, name="sums", tag="sums" if j == 0 else "turned")
             nc.tensor.matmul_mx(
                 out=sums[:], lhsT=codes[:].bitcast(FP8X4), lhsT_scale=plane[:],
                 rhs=v_codes[:].bitcast(FP8X4), rhs_scale=v_plane[:], start=True, stop=True,
             )
             result = rows.tile([P, DV], F32, name="result")
-            nc.scalar.activation(result[:], sums[:], ACT.Copy, scale=inverse[:])
+            factor = inverse[:, b * QT + j : b * QT + j + 1]
+            if b == B - 1 and j == QT - 1:
+                nc.vector.tensor_scalar(result[:], sums[:], factor, None, ALU.mult)
+            else:
+                nc.scalar.activation(result[:], sums[:], ACT.Copy, scale=factor)
             nc.sync.dma_start(out[b, j * P : (j + 1) * P, :], result[:])
 
         tiles = [(b, j) for b in range(B) for j in range(QT)]
-        score, pen, vs_cols, v_mx = [], [], [], []
-        parted = []
+        cast_values(0)
+        v_got = [gather_values(0)]
+        pos_cols = keep.tile([P, B, PACK], F32, name="pos_cols", tag="v_raw0")
         for b in range(B):
-            cast_values(b)
-            vs_cols.append(token_scales(b))
-            parted.append(keys(b))
-            v_mx.append(values(b))
-        for b in range(B):
-            pos_got = places(b)
-            score.extend(scores(b, j, parted[b]) for j in range(QT))
-            pen.extend(penalty(b, j, pos_got) for j in range(QT))
-        negated = keep.tile([P, B * QT * N], F32, name="negated", tag="v_pool", align_bytes=64)
-        part = [negated[:, u * N : (u + 1) * N] for u in range(B * QT)]
-        soft = []
-        mask(part[0], score[0], pen[0])
-        for u in range(B * QT):
-            if u + 1 < B * QT:
-                mask(part[u + 1], score[u + 1], pen[u + 1])
-            soft.append(softmax(u, part[u]))
-        grouped = [weights(soft[0][0], vs_cols[0])]
+            place_columns(b, pos_cols[:, b, :])
+        cast_values(1)
+        pos_row = [place_row(b, pos_cols[:, b, :]) for b in range(B)]
+        vs_tile = keep.tile([P, B, PACK], F32, name="vs_cols", tag="v_raw1")
+        vs_cols = [vs_tile[:, b, :] for b in range(B)]
+        token_scales(0, psum.tile([P, PACK, P], F32, name="vs_turned", tag="sums"), vs_cols[0])
+        token_scales(1, banks.tile([P, PACK, P], F32, name="vs_turned", tag="bank3"), vs_cols[1])
+        v_got.append(gather_values(1))
+        v_turned = [turn_values(v_got[0], psum.tile([P, PACK, 2, P], BF16, name="v_turned", tag="sums"))]
+        parted = [keys(b) for b in range(B)]
+        nc.vector.tensor_scalar(q_up[:], q_place[:], STEEP * (1.0 + NUDGE), FLOOR, ALU.mult, ALU.add)
+        nc.vector.tensor_scalar(q_down[:], q_place[:], STEEP * (1.0 - NUDGE), FLOOR, ALU.mult, ALU.add)
+        nc.vector.tensor_tensor(q_edge[:], q_up[:], q_down[:], ALU.max)
+        score = [scores(b, j, parted[b]) for b, j in tiles]
+        masked = [mask(0, score[0], pos_row[0])]
+        p_turned = []
+        for u in range(len(tiles)):
+            if u + 1 < len(tiles):
+                masked.append(mask(u + 1, score[u + 1], pos_row[tiles[u + 1][0]]))
+            p_turned.append(softmax(u, masked[u]))
+        v_turned.append(turn_values(v_got[1], banks.tile([P, PACK, 2, P], BF16, name="v_turned", tag="bank3")))
+        v_mx = [quantise_values(b, v_turned[b]) for b in range(B)]
+        nc.vector.reciprocal(inverse[:], total[:])
+        grouped = [weights(p_turned[0], vs_cols[0])]
         for u, (b, j) in enumerate(tiles):
-            if u + 1 < B * QT:
-                grouped.append(weights(soft[u + 1][0], vs_cols[tiles[u + 1][0]]))
-            finish(b, j, grouped[u], soft[u][1], *v_mx[b])
+            if u + 1 < len(tiles):
+                grouped.append(weights(p_turned[u + 1], vs_cols[tiles[u + 1][0]]))
+            finish(b, j, grouped[u], *v_mx[b])

@@ -42,10 +42,9 @@ def tile_attend_soft_draft_segb2q256n512t2048_kernel(tc, q_words, q_scales, k_wo
         offsets = keep.tile([P, B * LIST_COLS], U16, name="offsets")
         k_pool = keep.tile([P, T], I32, name="k_pool", align_bytes=64)
         ks_pool = keep.tile([P, T], U8, name="ks_pool", align_bytes=64)
-        q_codes = [keep.tile([P, PASSES, NQ], I32, name=f"q_codes{b}", align_bytes=64) for b in range(B)]
+        q_codes = keep.tile([P, B * PASSES, NQ], I32, name="q_codes", align_bytes=64)
         q_planes = keep.tile([P, B * PASSES * NQ], U8, name="q_planes", align_bytes=64)
         pos_pool = keep.tile([P, T], F32, name="pos_pool")
-        vs_pool = keep.tile([P, T], F32, name="vs_pool")
         v_raw = [keep.tile([P, 2, SEG], F32, name=f"v_raw{b}", tag=f"v_raw{b}") for b in range(B)]
         v_pool = keep.tile([P, B * 2 * SEG], BF16, name="v_pool", align_bytes=64)
         q_place = keep.tile([P, B * QT], F32, name="q_place")
@@ -60,49 +59,39 @@ def tile_attend_soft_draft_segb2q256n512t2048_kernel(tc, q_words, q_scales, k_wo
         vs_got = keep.tile([P, B * N], F32, name="vs_got")
         pos_got = keep.tile([P, B * N], F32, name="pos_got")
         ident = keep.tile([P, P], F32, name="ident")
-        warm = keep.tile([P, 1], F32, name="warm")
+        warm = keep.tile([P, 1], F32, name="warm", tag="warm")
 
         nc.vector.memset(warm[:], 0.0)
+        nc.vector.memset(ident[:], 0.0)
+        nc.vector.memset(q_planes[:].bitcast(I32), 0)
+        nc.vector.memset(pos_pool[0 : P - 1, :], 0.0)
         nc.vector.memset(ks_pool[0:96, :].bitcast(I32), 0)
-        nc.vector.memset(vs_pool[0 : P - 1, :], 0.0)
-        nc.gpsimd.memset(pos_pool[0 : P - 1, :], 0.0)
-        nc.gpsimd.memset(q_planes[:].bitcast(I32), 0)
-        nc.gpsimd.memset(k_planes[:].bitcast(I32), 0)
+        nc.vector.memset(k_planes[:].bitcast(I32), 0)
         nc.scalar.activation(warm[:], warm[:], ACT.Exp)
-        make_identity(nc, ident[:])
-        make_identity(nc, ident_bf[:])
+        make_identity(nc, ident[:], nomemset=True)
+        nc.vector.tensor_copy(ident_bf[:], ident[:])
+        vs_pool = keep.tile([P, T], F32, name="vs_pool", tag="warm")
+        nc.gpsimd.memset(vs_pool[0 : P - 1, :], 0.0)
+        nc.scalar.dma_start(vs_pool[P - 1 : P, :], vs[0:1, :])
 
-        k_hbm = k_words[0].rearrange("p t r -> p (t r)").bitcast(I32)
         nc.sync.dma_start(offsets[:], offs)
-        nc.sync.dma_start(ks_pool[96:P, :].bitcast(I32), k_scales.rearrange("o f t -> f o t").bitcast(I32))
-
-        def stretch(b):
-            return slice(b * SEG, (b + 1) * SEG)
-
-        def load_queries(b):
-            nc.sync.dma_start(q_codes[b][:], q_words[b].rearrange("o p q r -> p o (q r)").bitcast(I32))
-
-        def load_values(b):
-            nc.sync.dma_start(v_raw[b][:], vT[:, stretch(b)].rearrange("(h c) t -> c h t", h=2))
-
         nc.sync.dma_start(pos_pool[P - 1 : P, :], pos[0:1, :])
-        nc.sync.dma_start(vs_pool[P - 1 : P, :], vs[0:1, :])
-        for b in range(B):
-            load_values(b)
-        for b in range(B):
-            nc.sync.dma_start(k_pool[:, stretch(b)], k_hbm[:, stretch(b)])
-            load_queries(b)
+        nc.sync.dma_start(ks_pool[96:P, :].bitcast(I32), k_scales.rearrange("o f t -> f o t").bitcast(I32))
         with nc.allow_non_contiguous_dma(reason="one place a partition"):
             nc.sync.dma_start(q_place[:], qpos.rearrange("b (j p) o -> p (b j o)", p=P))
+        for b in range(B):
+            nc.sync.dma_start(v_raw[b][:], vT[:, b * SEG : (b + 1) * SEG].rearrange("(h c) t -> c h t", h=2))
+        nc.sync.dma_start(k_pool[:], k_words[0].rearrange("p t r -> p (t r)").bitcast(I32))
         for quad in range(4):
             nc.sync.dma_start(
                 q_planes[32 * quad : 32 * quad + 4, :].bitcast(I32).rearrange("j (g q) -> j g q", g=B * PASSES),
                 q_scales[:, :, 4 * quad : 4 * quad + 4, :].rearrange("b o j q -> j (b o) q").bitcast(I32),
             )
+        nc.sync.dma_start(q_codes[:], q_words.rearrange("b o p q r -> p (b o) (q r)").bitcast(I32))
+        nc.vector.tensor_copy(pos_got[:], pos_pool[:].indirect(offsets[:]))
         nc.vector.tensor_copy(ks_got[:], ks_pool[:].indirect(offsets[:]))
         for quad in range(4):
             nc.sync.dma_start(k_planes[32 * quad : 32 * quad + 4, :].bitcast(I32), ks_got[96 + 8 * quad : 96 + 8 * quad + 8, :].bitcast(I32))
-        nc.vector.tensor_copy(pos_got[:], pos_pool[:].indirect(offsets[:]))
         nc.vector.tensor_copy(vs_got[:], vs_pool[:].indirect(offsets[:]))
 
         def window(pool, b):
@@ -141,7 +130,7 @@ def tile_attend_soft_draft_segb2q256n512t2048_kernel(tc, q_words, q_scales, k_wo
                 first = (b * PASSES + o) * NQ + j * P
                 nc.tensor.matmul_mx(
                     out=bank[:],
-                    lhsT=q_codes[b][:, o, j * P : (j + 1) * P].bitcast(FP8X4),
+                    lhsT=q_codes[:, b * PASSES + o, j * P : (j + 1) * P].bitcast(FP8X4),
                     lhsT_scale=q_planes[:, first : first + P],
                     rhs=parted[:, o * 2 * N : (o + 1) * 2 * N].bitcast(FP4X4),
                     rhs_scale=k_planes[:, (o * B + b) * N : (o * B + b + 1) * N],

@@ -23,6 +23,7 @@ PACK = 4
 PASSES = D // (P * PACK)
 SEG = T // B
 QT = NQ // P
+HALVES = DV // P
 LIST_COLS = N // 16
 MASKED = 30000.0
 STEEP = 2.0 ** 80
@@ -34,75 +35,76 @@ def tile_attend_soft_draft_segb2q256n512t2048_kernel(tc, q_words, q_scales, k_wo
     nc = tc.nc
     with ExitStack() as ctx:
         keep = ctx.enter_context(tc.tile_pool(name="keep", bufs=1))
+        values = ctx.enter_context(tc.tile_pool(name="values", bufs=1))
         work = ctx.enter_context(tc.tile_pool(name="work", bufs=2))
-        psum = ctx.enter_context(tc.psum_pool(name="psum", bufs=2))
         banks = ctx.enter_context(tc.psum_pool(name="banks", bufs=1))
         rows = ctx.enter_context(tc.tile_pool(name="rows", bufs=B * QT))
 
         offsets = keep.tile([P, B * LIST_COLS], U16, name="offsets")
         k_pool = keep.tile([P, T], I32, name="k_pool", align_bytes=64)
-        ks_pool = keep.tile([P, T], U8, name="ks_pool", align_bytes=64)
+        ks_pool = values.tile([P, T], U8, name="ks_pool", offset=4 * T - T // 2)
         q_codes = keep.tile([P, B * PASSES, NQ], I32, name="q_codes", align_bytes=64)
         q_planes = keep.tile([P, B * PASSES * NQ], U8, name="q_planes", align_bytes=64)
         pos_pool = keep.tile([P, T], F32, name="pos_pool")
-        v_raw = [keep.tile([P, 2, SEG], F32, name=f"v_raw{b}", tag=f"v_raw{b}") for b in range(B)]
-        v_pool = keep.tile([P, B * 2 * SEG], BF16, name="v_pool", align_bytes=64)
         q_place = keep.tile([P, B * QT], F32, name="q_place")
         q_up = keep.tile([P, B * QT], F32, name="q_up")
         q_down = keep.tile([P, B * QT], F32, name="q_down")
         q_edge = keep.tile([P, B * QT], F32, name="q_edge")
-        total = keep.tile([P, B * QT], F32, name="total")
-        inverse = keep.tile([P, B * QT], F32, name="inverse")
-        ident_bf = keep.tile([P, P], BF16, name="ident_bf")
         ks_got = keep.tile([P, B * N], U8, name="ks_got", align_bytes=64)
         k_planes = keep.tile([P, PASSES * B * N], U8, name="k_planes", align_bytes=64)
-        vs_got = keep.tile([P, B * N], F32, name="vs_got")
-        pos_got = keep.tile([P, B * N], F32, name="pos_got")
+        pos_got = keep.tile([P, B * N], F32, name="pos_got", tag="pos_got")
         ident = keep.tile([P, P], F32, name="ident")
-        warm = keep.tile([P, 1], F32, name="warm", tag="warm")
+        vs_pool = keep.tile([P, T], F32, name="vs_pool")
 
+        warm = keep.tile([P, 1], F32, name="warm")
         nc.vector.memset(warm[:], 0.0)
-        nc.vector.memset(ident[:], 0.0)
-        nc.vector.memset(q_planes[:].bitcast(I32), 0)
-        nc.vector.memset(pos_pool[0 : P - 1, :], 0.0)
-        nc.vector.memset(ks_pool[0:96, :].bitcast(I32), 0)
-        nc.vector.memset(k_planes[:].bitcast(I32), 0)
         nc.scalar.activation(warm[:], warm[:], ACT.Exp)
-        make_identity(nc, ident[:], nomemset=True)
-        nc.vector.tensor_copy(ident_bf[:], ident[:])
-        vs_pool = keep.tile([P, T], F32, name="vs_pool", tag="warm")
-        nc.gpsimd.memset(vs_pool[0 : P - 1, :], 0.0)
-        nc.scalar.dma_start(vs_pool[P - 1 : P, :], vs[0:1, :])
 
+        def clear(words):
+            cut = words.shape[1] // 2 + 1
+            nc.vector.memset(words[:, 0:cut], 0)
+            nc.vector.memset(words[:, cut:], 0)
+
+        nc.gpsimd.memset(pos_pool[0 : P - 1, :], 0.0)
+        clear(ident[:].bitcast(I32))
+        clear(q_planes[:].bitcast(I32))
+        clear(ks_pool[0:96, :].bitcast(I32))
+        clear(k_planes[:].bitcast(I32))
+        make_identity(nc, ident[:], nomemset=True)
+        nc.gpsimd.memset(vs_pool[0 : P - 1, :], 0.0)
+
+        k_flat = k_words[0].rearrange("p t r -> p (t r)").bitcast(I32)
         nc.sync.dma_start(offsets[:], offs)
-        nc.sync.dma_start(pos_pool[P - 1 : P, :], pos[0:1, :])
         nc.sync.dma_start(ks_pool[96:P, :].bitcast(I32), k_scales.rearrange("o f t -> f o t").bitcast(I32))
-        with nc.allow_non_contiguous_dma(reason="one place a partition"):
-            nc.sync.dma_start(q_place[:], qpos.rearrange("b (j p) o -> p (b j o)", p=P))
-        for b in range(B):
-            nc.sync.dma_start(v_raw[b][:], vT[:, b * SEG : (b + 1) * SEG].rearrange("(h c) t -> c h t", h=2))
-        nc.sync.dma_start(k_pool[:], k_words[0].rearrange("p t r -> p (t r)").bitcast(I32))
+        nc.sync.dma_start(pos_pool[P - 1 : P, :], pos[0:1, :])
+        nc.sync.dma_start(k_pool[:, 0:SEG], k_flat[:, 0:SEG])
         for quad in range(4):
             nc.sync.dma_start(
                 q_planes[32 * quad : 32 * quad + 4, :].bitcast(I32).rearrange("j (g q) -> j g q", g=B * PASSES),
                 q_scales[:, :, 4 * quad : 4 * quad + 4, :].rearrange("b o j q -> j (b o) q").bitcast(I32),
             )
+        nc.sync.dma_start(vs_pool[P - 1 : P, :], vs[0:1, :])
+        nc.sync.dma_start(k_pool[:, SEG:T], k_flat[:, SEG:T])
         nc.sync.dma_start(q_codes[:], q_words.rearrange("b o p q r -> p (b o) (q r)").bitcast(I32))
-        nc.vector.tensor_copy(pos_got[:], pos_pool[:].indirect(offsets[:]))
+        with nc.allow_non_contiguous_dma(reason="one place a partition"):
+            nc.sync.dma_start(q_place[:], qpos.rearrange("b (j p) o -> p (b j o)", p=P))
         nc.vector.tensor_copy(ks_got[:], ks_pool[:].indirect(offsets[:]))
         for quad in range(4):
             nc.sync.dma_start(k_planes[32 * quad : 32 * quad + 4, :].bitcast(I32), ks_got[96 + 8 * quad : 96 + 8 * quad + 8, :].bitcast(I32))
-        nc.vector.tensor_copy(vs_got[:], vs_pool[:].indirect(offsets[:]))
-
-        def window(pool, b):
-            return pool[:, 0 : (b + 1) * SEG]
+        nc.scalar.activation(pos_got[:], pos_pool[:].indirect(offsets[:]), ACT.Copy)
+        v_pool = [values.tile([P, T], F32, name=f"v_pool{h}", offset=4 * T * h) for h in range(HALVES)]
+        for h in range(HALVES):
+            nc.sync.dma_start(v_pool[h][:], vT[h * P : (h + 1) * P, :])
 
         def listed(b):
             return offsets[:, b * LIST_COLS : (b + 1) * LIST_COLS]
 
-        def keys(b):
+        def gather_keys(b):
             both = work.tile([P, N], U32, name="k_both")
-            nc.vector.tensor_copy(both[:], window(k_pool, b).bitcast(U32).indirect(listed(b)))
+            nc.vector.tensor_copy(both[:], k_pool[:, 0 : (b + 1) * SEG].bitcast(U32).indirect(listed(b)))
+            return both
+
+        def part_keys(both):
             parted = work.tile([P, PASSES * 2 * N], U8, name="k_parted", align_bytes=64)
             nc.vector.tensor_copy(
                 parted[:].bitcast(U16).rearrange("p (o n) -> p o n", o=PASSES),
@@ -110,14 +112,15 @@ def tile_attend_soft_draft_segb2q256n512t2048_kernel(tc, q_words, q_scales, k_wo
             )
             return parted
 
-        def place_columns(b, cols):
-            turned = psum.tile([P, PACK, P], F32, name="pos_turned", tag="turned")
-            for c in range(PACK):
-                nc.tensor.transpose(turned[:, c, :], pos_got[:, b * N + c * P : b * N + (c + 1) * P], ident[:])
-            nc.scalar.mul(cols, turned[:, :, P - 1], -STEEP)
+        def columns(sources, cols, tag, factor):
+            turned = banks.tile([P, N], F32, name="cols_turned", tag=tag)
+            count = len(sources)
+            for c in reversed(range(count)):
+                nc.tensor.transpose(turned[:, 2 * c : 2 * c + P], sources[c], ident[:])
+            nc.scalar.mul(cols, turned[:, P - 1 : P - 1 + 2 * count : 2], factor)
 
         def place_row(b, cols):
-            spread = psum.tile([P, PACK, P], F32, name="pos_spread", tag="turned")
+            spread = banks.tile([P, PACK, P], F32, name="pos_spread", tag=f"side{1 + b}")
             for c in range(PACK):
                 nc.tensor.transpose(spread[:, c, :], cols[:, c : c + 1].to_broadcast([P, P]), ident[:])
             row = keep.tile([P, N], F32, name="pos_row", tag=f"pos_row{b}", align_bytes=64)
@@ -144,53 +147,44 @@ def tile_attend_soft_draft_segb2q256n512t2048_kernel(tc, q_words, q_scales, k_wo
             nc.vector.scalar_tensor_tensor(masked[:], pos_row[:], q_edge[:, u : u + 1], bank[:], ALU.add, ALU.min)
             return masked
 
-        def softmax(u, masked):
-            capped = rows.tile([P, N], F32, name="capped")
+        def row_top(u, masked):
+            capped = keep.tile([P, N], F32, name="capped", tag=f"capped{u}")
             top = rows.tile([P, 1], F32, name="top")
             nc.vector.tensor_scalar(capped[:], masked[:], -MASKED, None, ALU.max, ALU.max, accum_out=top[:])
+            return capped, top
+
+        def softmax(u, capped, top, total):
             shift = rows.tile([P, 1], F32, name="shift")
             nc.scalar.mul(shift[:], top[:], -1.0)
             p = rows.tile([P, N], F32, name="p")
             nc.scalar.activation(
                 p[:].rearrange("p (t c i) -> p c t i", t=PACK, i=4),
                 capped[:].rearrange("p (c i t) -> p c t i", t=PACK, i=4),
-                ACT.Exp, bias=shift[:], accum_out=total[:, u : u + 1],
+                ACT.Exp, bias=shift[:], accum_out=total,
             )
-            if u + 1 < B * QT:
-                turned = banks.tile([P, PACK, P], F32, name="p_turned", tag=f"bank{u}")
-            else:
-                turned = psum.tile([P, PACK, P], F32, name="p_turned", tag="turned")
+            turned = banks.tile([P, PACK, P], F32, name="p_turned", tag=f"side{(u + 3) % 4}")
             for t in range(PACK):
                 nc.tensor.transpose(turned[:, t, :], p[:, t * P : (t + 1) * P], ident[:])
             return turned
 
-        def token_scales(b, turned, cols):
-            for t in range(PACK):
-                nc.tensor.transpose(turned[:, t, :], vs_got[:, b * N + t : (b + 1) * N : PACK], ident[:])
-            nc.scalar.copy(cols, turned[:, :, P - 1])
+        def gather_values(b, h, got, turned):
+            nc.scalar.activation(got, v_pool[h][:].indirect(listed(b)), ACT.Copy)
+            pairs = got.bitcast(F32)
+            for u in range(2):
+                nc.tensor.transpose(turned[:, h, u, :], pairs[:, u : N // 2 : 2], ident[:])
 
-        def cast_values(b):
-            nc.scalar.activation(v_pool[:, 2 * b * SEG : 2 * (b + 1) * SEG], v_raw[b][:].rearrange("p h t -> p (h t)"), ACT.Copy)
+        def group_values(turned, copy):
+            grouped = work.tile([P, DV * PACK], BF16, name="v_grouped", align_bytes=64)
+            copy(
+                grouped[:].bitcast(F32).rearrange("p (h c u) -> p h c u", h=HALVES, u=2),
+                turned[:].rearrange("p h u c -> p h c u"),
+            )
+            return grouped
 
-        def gather_values(b):
-            got = work.tile([P, 2, PACK, P], BF16, name="v_got")
-            for h in range(2):
-                end = (2 * b + h + 1) * SEG
-                nc.scalar.activation(got[:, h].rearrange("p t s -> p s t"), v_pool[:, end - (b + 1) * SEG : end].indirect(listed(b)), ACT.Copy)
-            return got
-
-        def turn_values(got, turned):
-            for h in range(2):
-                for t in range(PACK):
-                    nc.tensor.transpose(turned[:, t, h, :], got[:, h, t, :], ident_bf[:])
-            return turned
-
-        def quantise_values(b, turned):
-            grouped = work.tile([P, DV, PACK], BF16, name="v_grouped", align_bytes=64)
-            nc.scalar.copy(grouped[:], turned[:].rearrange("p t h c -> p (h c) t"))
-            codes = keep.tile([P, DV], U32, name="v_codes", tag=f"pos_row{B - 1 - b}", align_bytes=64)
+        def quantise_values(grouped):
+            codes = work.tile([P, DV], U32, name="v_codes", align_bytes=64)
             plane = work.tile([P, DV], U8, name="v_plane", align_bytes=64)
-            nc.vector.quantize_mx(out=codes[:].bitcast(FP8X4), scales=plane[:], in_=grouped[:].rearrange("p e t -> p (e t)"))
+            nc.vector.quantize_mx(out=codes[:].bitcast(FP8X4), scales=plane[:], in_=grouped[:])
             return codes, plane
 
         def weights(turned, vs_cols):
@@ -201,17 +195,19 @@ def tile_attend_soft_draft_segb2q256n512t2048_kernel(tc, q_words, q_scales, k_wo
             )
             return grouped
 
-        def finish(b, j, grouped, v_codes, v_plane):
+        def quantise_weights(grouped):
             codes = rows.tile([P, P], U32, name="w_codes", align_bytes=64)
             plane = rows.tile([P, P], U8, name="w_plane", align_bytes=64)
             nc.vector.quantize_mx(out=codes[:].bitcast(FP8X4), scales=plane[:], in_=grouped[:].rearrange("p q t -> p (q t)"))
-            sums = psum.tile([P, DV], F32, name="sums", tag="sums" if j == 0 else "turned")
+            return codes, plane
+
+        def finish(b, j, w_mx, v_mx, factor):
+            sums = banks.tile([P, DV], F32, name="sums", tag=("bank3", "bank2", "side3", "side0")[b * QT + j])
             nc.tensor.matmul_mx(
-                out=sums[:], lhsT=codes[:].bitcast(FP8X4), lhsT_scale=plane[:],
-                rhs=v_codes[:].bitcast(FP8X4), rhs_scale=v_plane[:], start=True, stop=True,
+                out=sums[:], lhsT=w_mx[0][:].bitcast(FP8X4), lhsT_scale=w_mx[1][:],
+                rhs=v_mx[0][:].bitcast(FP8X4), rhs_scale=v_mx[1][:], start=True, stop=True,
             )
-            result = rows.tile([P, DV], F32, name="result")
-            factor = inverse[:, b * QT + j : b * QT + j + 1]
+            result = keep.tile([P, DV], F32, name="result", tag=("capped3", "capped0", "capped1", "result")[b * QT + j])
             if b == B - 1 and j == QT - 1:
                 nc.vector.tensor_scalar(result[:], sums[:], factor, None, ALU.mult)
             else:
@@ -219,35 +215,64 @@ def tile_attend_soft_draft_segb2q256n512t2048_kernel(tc, q_words, q_scales, k_wo
             nc.sync.dma_start(out[b, j * P : (j + 1) * P, :], result[:])
 
         tiles = [(b, j) for b in range(B) for j in range(QT)]
-        cast_values(0)
-        v_got = [gather_values(0)]
-        pos_cols = keep.tile([P, B, PACK], F32, name="pos_cols", tag="v_raw0")
+        pos_cols = keep.tile([P, B * PACK], F32, name="pos_cols", tag="v_got0")
+        vs_cols = keep.tile([P, B * PACK], F32, name="vs_cols")
+        columns([pos_got[:, c * P : (c + 1) * P] for c in range(B * PACK)], pos_cols[:], "side0", -STEEP)
+        pos_row = [place_row(b, pos_cols[:, b * PACK : (b + 1) * PACK]) for b in range(B)]
+        vs_got = [keep.tile([P, N], F32, name="vs_got", tag=("vs_got", "pos_got")[b]) for b in range(B)]
         for b in range(B):
-            place_columns(b, pos_cols[:, b, :])
-        cast_values(1)
-        pos_row = [place_row(b, pos_cols[:, b, :]) for b in range(B)]
-        vs_tile = keep.tile([P, B, PACK], F32, name="vs_cols", tag="v_raw1")
-        vs_cols = [vs_tile[:, b, :] for b in range(B)]
-        token_scales(0, psum.tile([P, PACK, P], F32, name="vs_turned", tag="sums"), vs_cols[0])
-        token_scales(1, banks.tile([P, PACK, P], F32, name="vs_turned", tag="bank3"), vs_cols[1])
-        v_got.append(gather_values(1))
-        v_turned = [turn_values(v_got[0], psum.tile([P, PACK, 2, P], BF16, name="v_turned", tag="sums"))]
-        parted = [keys(b) for b in range(B)]
+            nc.scalar.activation(vs_got[b][:], vs_pool[:].indirect(listed(b)), ACT.Copy)
+        v_first = keep.tile([P, B * N], BF16, name="v_first", tag="v_got0")
+        both = [gather_keys(0)]
         nc.vector.tensor_scalar(q_up[:], q_place[:], STEEP * (1.0 + NUDGE), FLOOR, ALU.mult, ALU.add)
         nc.vector.tensor_scalar(q_down[:], q_place[:], STEEP * (1.0 - NUDGE), FLOOR, ALU.mult, ALU.add)
+        parted = [part_keys(both[0])]
+        both.append(gather_keys(1))
         nc.vector.tensor_tensor(q_edge[:], q_up[:], q_down[:], ALU.max)
+        parted.append(part_keys(both[1]))
         score = [scores(b, j, parted[b]) for b, j in tiles]
+
+        total = [keep.tile([P, QT], F32, name=f"total{b}") for b in range(B)]
+        inverse = [keep.tile([P, QT], F32, name=f"inverse{b}") for b in range(B)]
         masked = [mask(0, score[0], pos_row[0])]
-        p_turned = []
+        tops = []
         for u in range(len(tiles)):
             if u + 1 < len(tiles):
                 masked.append(mask(u + 1, score[u + 1], pos_row[tiles[u + 1][0]]))
-            p_turned.append(softmax(u, masked[u]))
-        v_turned.append(turn_values(v_got[1], banks.tile([P, PACK, 2, P], BF16, name="v_turned", tag="bank3")))
-        v_mx = [quantise_values(b, v_turned[b]) for b in range(B)]
-        nc.vector.reciprocal(inverse[:], total[:])
-        grouped = [weights(p_turned[0], vs_cols[0])]
-        for u, (b, j) in enumerate(tiles):
-            if u + 1 < len(tiles):
-                grouped.append(weights(p_turned[u + 1], vs_cols[tiles[u + 1][0]]))
-            finish(b, j, grouped[u], *v_mx[b])
+            tops.append(row_top(u, masked[u]))
+        columns([vs_got[b][:, t:N:PACK] for b in range(B) for t in range(PACK)], vs_cols[:], "bank2", 1.0)
+        v_turned = [banks.tile([P, HALVES, 2, P], F32, name="v_turned", tag=f"bank{b}") for b in range(B)]
+
+        def exp_of(u):
+            b, j = tiles[u]
+            return softmax(u, *tops[u], total[b][:, j : j + 1])
+
+        def weights_of(u):
+            b = tiles[u][0]
+            return weights(p_turned[u], vs_cols[:, b * PACK : (b + 1) * PACK])
+
+        for b in range(B):
+            gather_values(b, 0, v_first[:, b * N : (b + 1) * N], v_turned[b])
+        p_turned = [exp_of(0), exp_of(1)]
+        gather_values(0, 1, keep.tile([P, N], BF16, name="v_second0")[:], v_turned[0])
+        p_turned.append(exp_of(2))
+        gather_values(1, 1, keep.tile([P, N], BF16, name="v_second1", tag="capped2")[:], v_turned[1])
+        p_turned.append(exp_of(3))
+        late_values = group_values(v_turned[1], nc.scalar.copy)
+
+        grouped = [weights_of(0)]
+        early_values = group_values(v_turned[0], nc.vector.tensor_copy)
+        grouped.append(weights_of(1))
+        w_mx = [quantise_weights(grouped[0])]
+        v_mx = quantise_values(early_values)
+        w_mx.append(quantise_weights(grouped[1]))
+        nc.vector.reciprocal(inverse[0][:], total[0][:])
+        grouped.extend([weights_of(2), weights_of(3)])
+        for j in range(QT):
+            finish(0, j, w_mx[j], v_mx, inverse[0][:, j : j + 1])
+        nc.vector.reciprocal(inverse[1][:], total[1][:])
+        w_mx = [quantise_weights(grouped[2])]
+        v_mx = quantise_values(late_values)
+        w_mx.append(quantise_weights(grouped[3]))
+        for j in range(QT):
+            finish(1, j, w_mx[j], v_mx, inverse[1][:, j : j + 1])

@@ -1,7 +1,6 @@
 from contextlib import ExitStack
 
 import concourse.mybir as mybir
-from concourse.masks import make_identity
 
 B, N, T, D, DV, NQ = 2, 512, 2048, 1024, 256, 256
 FLOPS = 2 * B * NQ * N * (D + DV)
@@ -29,6 +28,12 @@ MASKED = 30000.0
 STEEP = 2.0 ** 80
 NUDGE = 2.0 ** -22
 FLOOR = 2.0 ** 40
+Q_BYTES = 4 * B * PASSES * NQ
+V_AT = Q_BYTES
+MID_AT = V_AT + 4 * SEG
+LAST_AT = MID_AT + 4 * T
+VS_AT = LAST_AT + 4 * T
+WIDE = DV * PACK + QT * N
 
 
 def tile_attend_soft_draft_segb2q256n512t2048_kernel(tc, q_words, q_scales, k_words, k_scales, vT, vs, pos, qpos, offs, out):
@@ -36,25 +41,28 @@ def tile_attend_soft_draft_segb2q256n512t2048_kernel(tc, q_words, q_scales, k_wo
     with ExitStack() as ctx:
         keep = ctx.enter_context(tc.tile_pool(name="keep", bufs=1))
         values = ctx.enter_context(tc.tile_pool(name="values", bufs=1))
+        ends = ctx.enter_context(tc.tile_pool(name="ends", bufs=1))
+        held = ctx.enter_context(tc.tile_pool(name="held", bufs=1))
+        keys = ctx.enter_context(tc.tile_pool(name="keys", bufs=1))
         work = ctx.enter_context(tc.tile_pool(name="work", bufs=2))
         banks = ctx.enter_context(tc.psum_pool(name="banks", bufs=1))
         rows = ctx.enter_context(tc.tile_pool(name="rows", bufs=B * QT))
 
         offsets = keep.tile([P, B * LIST_COLS], U16, name="offsets")
         k_pool = keep.tile([P, T], I32, name="k_pool", align_bytes=64)
-        ks_pool = values.tile([P, T], U8, name="ks_pool", offset=4 * T - T // 2)
-        q_codes = keep.tile([P, B * PASSES, NQ], I32, name="q_codes", align_bytes=64)
+        ks_pool = values.tile([P, T], U8, name="ks_pool", offset=MID_AT, align_bytes=64)
+        zeros = values.tile([P, P], F32, name="zeros", offset=Q_BYTES - 256)
         q_planes = keep.tile([P, B * PASSES * NQ], U8, name="q_planes", align_bytes=64)
-        pos_pool = keep.tile([P, T], F32, name="pos_pool")
+        pos_pool = values.tile([P, T], F32, name="pos_pool", offset=LAST_AT)
         q_place = keep.tile([P, B * QT], F32, name="q_place")
         q_up = keep.tile([P, B * QT], F32, name="q_up")
         q_down = keep.tile([P, B * QT], F32, name="q_down")
         q_edge = keep.tile([P, B * QT], F32, name="q_edge")
         ks_got = keep.tile([P, B * N], U8, name="ks_got", align_bytes=64)
         k_planes = keep.tile([P, PASSES * B * N], U8, name="k_planes", align_bytes=64)
-        pos_got = keep.tile([P, B * N], F32, name="pos_got", tag="pos_got")
+        pos_got = [keys.tile([P, N], F32, name=f"pos_got{b}", offset=(10 * N, 4 * N)[b]) for b in range(B)]
         ident = keep.tile([P, P], F32, name="ident")
-        vs_pool = keep.tile([P, T], F32, name="vs_pool")
+        vs_pool = values.tile([P, T], F32, name="vs_pool", offset=VS_AT)
 
         warm = keep.tile([P, 1], F32, name="warm")
         nc.vector.memset(warm[:], 0.0)
@@ -66,46 +74,50 @@ def tile_attend_soft_draft_segb2q256n512t2048_kernel(tc, q_words, q_scales, k_wo
             nc.vector.memset(words[:, cut:], 0)
 
         nc.gpsimd.memset(pos_pool[0 : P - 1, :], 0.0)
-        clear(ident[:].bitcast(I32))
+        clear(zeros[:].bitcast(I32))
         clear(q_planes[:].bitcast(I32))
         clear(ks_pool[0:96, :].bitcast(I32))
         clear(k_planes[:].bitcast(I32))
-        make_identity(nc, ident[:], nomemset=True)
+        nc.gpsimd.affine_select(
+            out=ident[:], in_=zeros[:], compare_op=ALU.not_equal, fill=1.0, base=0, pattern=[[-1, P]], channel_multiplier=1,
+        )
+        q_codes = values.tile([P, B * PASSES, NQ], I32, name="q_codes", offset=0)
         nc.gpsimd.memset(vs_pool[0 : P - 1, :], 0.0)
 
         k_flat = k_words[0].rearrange("p t r -> p (t r)").bitcast(I32)
         nc.sync.dma_start(offsets[:], offs)
         nc.sync.dma_start(ks_pool[96:P, :].bitcast(I32), k_scales.rearrange("o f t -> f o t").bitcast(I32))
         nc.sync.dma_start(pos_pool[P - 1 : P, :], pos[0:1, :])
-        nc.sync.dma_start(k_pool[:, 0:SEG], k_flat[:, 0:SEG])
+        nc.sync.dma_start(vs_pool[P - 1 : P, :], vs[0:1, :])
+        for b in range(B):
+            nc.sync.dma_start(k_pool[:, b * SEG : (b + 1) * SEG], k_flat[:, b * SEG : (b + 1) * SEG])
+        with nc.allow_non_contiguous_dma(reason="one place a partition"):
+            nc.sync.dma_start(q_place[:], qpos.rearrange("b (j p) o -> p (b j o)", p=P))
         for quad in range(4):
             nc.sync.dma_start(
                 q_planes[32 * quad : 32 * quad + 4, :].bitcast(I32).rearrange("j (g q) -> j g q", g=B * PASSES),
                 q_scales[:, :, 4 * quad : 4 * quad + 4, :].rearrange("b o j q -> j (b o) q").bitcast(I32),
             )
-        nc.sync.dma_start(vs_pool[P - 1 : P, :], vs[0:1, :])
-        nc.sync.dma_start(k_pool[:, SEG:T], k_flat[:, SEG:T])
         nc.sync.dma_start(q_codes[:], q_words.rearrange("b o p q r -> p (b o) (q r)").bitcast(I32))
-        with nc.allow_non_contiguous_dma(reason="one place a partition"):
-            nc.sync.dma_start(q_place[:], qpos.rearrange("b (j p) o -> p (b j o)", p=P))
+        v_first = values.tile([P, SEG], F32, name="v_first", offset=V_AT)
+        nc.sync.dma_start(v_first[:], vT[0:P, 0:SEG])
         nc.vector.tensor_copy(ks_got[:], ks_pool[:].indirect(offsets[:]))
         for quad in range(4):
             nc.sync.dma_start(k_planes[32 * quad : 32 * quad + 4, :].bitcast(I32), ks_got[96 + 8 * quad : 96 + 8 * quad + 8, :].bitcast(I32))
-        nc.scalar.activation(pos_got[:], pos_pool[:].indirect(offsets[:]), ACT.Copy)
-        v_pool = [values.tile([P, T], F32, name=f"v_pool{h}", offset=4 * T * h) for h in range(HALVES)]
-        for h in range(HALVES):
-            nc.sync.dma_start(v_pool[h][:], vT[h * P : (h + 1) * P, :])
+        v_mid = values.tile([P, T], F32, name="v_mid", offset=MID_AT)
+        nc.sync.dma_start(v_mid[:, 0:SEG], vT[P : 2 * P, 0:SEG])
+        nc.sync.dma_start(v_mid[:, SEG:T], vT[0:P, SEG:T])
 
         def listed(b):
             return offsets[:, b * LIST_COLS : (b + 1) * LIST_COLS]
 
         def gather_keys(b):
-            both = work.tile([P, N], U32, name="k_both")
+            both = keys.tile([P, N], U32, name=f"k_both{b}", offset=(10 * N, 6 * N)[b])
             nc.vector.tensor_copy(both[:], k_pool[:, 0 : (b + 1) * SEG].bitcast(U32).indirect(listed(b)))
             return both
 
-        def part_keys(both):
-            parted = work.tile([P, PASSES * 2 * N], U8, name="k_parted", align_bytes=64)
+        def part_keys(b, both):
+            parted = keys.tile([P, PASSES * 2 * N], U8, name=f"k_parted{b}", offset=(2 * N, 14 * N)[b], align_bytes=64)
             nc.vector.tensor_copy(
                 parted[:].bitcast(U16).rearrange("p (o n) -> p o n", o=PASSES),
                 both[:].bitcast(U16).rearrange("p (n o) -> p o n", o=PASSES),
@@ -117,14 +129,14 @@ def tile_attend_soft_draft_segb2q256n512t2048_kernel(tc, q_words, q_scales, k_wo
             count = len(sources)
             for c in reversed(range(count)):
                 nc.tensor.transpose(turned[:, 2 * c : 2 * c + P], sources[c], ident[:])
-            nc.scalar.mul(cols, turned[:, P - 1 : P - 1 + 2 * count : 2], factor)
+            nc.vector.tensor_scalar(cols, turned[:, P - 1 : P - 1 + 2 * count : 2], factor, None, ALU.mult)
 
-        def place_row(b, cols):
-            spread = banks.tile([P, PACK, P], F32, name="pos_spread", tag=f"side{1 + b}")
+        def place_row(b, cols, at):
+            spread = banks.tile([P, PACK, P], F32, name="pos_spread", tag=("bank1", "bank3")[b])
             for c in range(PACK):
                 nc.tensor.transpose(spread[:, c, :], cols[:, c : c + 1].to_broadcast([P, P]), ident[:])
-            row = keep.tile([P, N], F32, name="pos_row", tag=f"pos_row{b}", align_bytes=64)
-            nc.scalar.copy(row[:], spread[:].rearrange("p c s -> p (c s)"))
+            row = values.tile([P, N], F32, name=f"pos_row{b}", offset=at)
+            nc.scalar.copy(row[:].rearrange("p (t s) -> p t s", t=PACK), spread[:].rearrange("p c (s t) -> p t (c s)", t=PACK))
             return row
 
         def scores(b, j, parted):
@@ -143,136 +155,146 @@ def tile_attend_soft_draft_segb2q256n512t2048_kernel(tc, q_words, q_scales, k_wo
             return bank
 
         def mask(u, bank, pos_row):
-            masked = rows.tile([P, N], F32, name="masked")
-            nc.vector.scalar_tensor_tensor(masked[:], pos_row[:], q_edge[:, u : u + 1], bank[:], ALU.add, ALU.min)
+            masked = held.tile([P, N], F32, name=f"masked{u}", offset=4 * N * (3 - u))
+            nc.vector.scalar_tensor_tensor(
+                masked[:].rearrange("p (t s) -> p t s", t=PACK), pos_row[:].rearrange("p (t s) -> p t s", t=PACK),
+                q_edge[:, u : u + 1], bank[:].rearrange("p (s t) -> p t s", t=PACK), ALU.add, ALU.min,
+            )
             return masked
 
         def row_top(u, masked):
-            capped = keep.tile([P, N], F32, name="capped", tag=f"capped{u}")
+            capped = keep.tile([P, N], F32, name="capped", tag=f"capped{u}") if u < 3 else ends.tile([P, N], F32, name="capped_last", offset=0)
             top = rows.tile([P, 1], F32, name="top")
             nc.vector.tensor_scalar(capped[:], masked[:], -MASKED, None, ALU.max, ALU.max, accum_out=top[:])
             return capped, top
 
         def softmax(u, capped, top, total):
             shift = rows.tile([P, 1], F32, name="shift")
-            nc.scalar.mul(shift[:], top[:], -1.0)
-            p = rows.tile([P, N], F32, name="p")
-            nc.scalar.activation(
-                p[:].rearrange("p (t c i) -> p c t i", t=PACK, i=4),
-                capped[:].rearrange("p (c i t) -> p c t i", t=PACK, i=4),
-                ACT.Exp, bias=shift[:], accum_out=total,
-            )
-            turned = banks.tile([P, PACK, P], F32, name="p_turned", tag=f"side{(u + 3) % 4}")
+            nc.gpsimd.tensor_scalar(shift[:], top[:], -1.0, 0.0, ALU.mult, ALU.add)
+            p = values.tile([P, N], F32, name=f"p{u}", offset=(MID_AT if u < QT else LAST_AT) + 4 * N * (u % QT))
+            nc.scalar.activation(p[:], capped[:], ACT.Exp, bias=shift[:], accum_out=total)
+            turned = banks.tile([P, PACK, P], F32, name="p_turned", tag=f"side{u}")
             for t in range(PACK):
                 nc.tensor.transpose(turned[:, t, :], p[:, t * P : (t + 1) * P], ident[:])
             return turned
 
         def gather_values(b, h, got, turned):
-            nc.scalar.activation(got, v_pool[h][:].indirect(listed(b)), ACT.Copy)
+            nc.scalar.activation(got, v_pool[b, h][:].indirect(listed(b)), ACT.Copy)
+            turn_values(h, got, turned)
+
+        def turn_values(h, got, turned):
             pairs = got.bitcast(F32)
             for u in range(2):
                 nc.tensor.transpose(turned[:, h, u, :], pairs[:, u : N // 2 : 2], ident[:])
 
-        def group_values(turned, copy):
-            grouped = work.tile([P, DV * PACK], BF16, name="v_grouped", align_bytes=64)
+        codes = [keep.tile([P, WIDE // PACK], U32, name=f"codes{b}", align_bytes=64) for b in range(B)]
+        plane = [keep.tile([P, WIDE // PACK], U8, name=f"plane{b}", align_bytes=64) for b in range(B)]
+
+        def group_values(b, turned, copy):
             copy(
-                grouped[:].bitcast(F32).rearrange("p (h c u) -> p h c u", h=HALVES, u=2),
+                grouped[b][:, 0 : DV * PACK].bitcast(F32).rearrange("p (h c u) -> p h c u", h=HALVES, u=2),
                 turned[:].rearrange("p h u c -> p h c u"),
             )
-            return grouped
 
-        def quantise_values(grouped):
-            codes = work.tile([P, DV], U32, name="v_codes", align_bytes=64)
-            plane = work.tile([P, DV], U8, name="v_plane", align_bytes=64)
-            nc.vector.quantize_mx(out=codes[:].bitcast(FP8X4), scales=plane[:], in_=grouped[:])
-            return codes, plane
-
-        def weights(turned, vs_cols):
-            grouped = rows.tile([P, P, PACK], BF16, name="w_grouped", align_bytes=64)
+        def weights(b, j, turned):
+            first = DV * PACK + j * N
             nc.vector.tensor_tensor(
-                grouped[:], turned[:].rearrange("p t q -> p q t"),
-                vs_cols.unsqueeze(1).to_broadcast([P, P, PACK]), ALU.mult,
+                grouped[b][:, first : first + N].rearrange("p (q t) -> p q t", t=PACK), turned[:].rearrange("p t q -> p q t"),
+                vs_cols[b][:].unsqueeze(1).to_broadcast([P, P, PACK]), ALU.mult,
             )
-            return grouped
 
-        def quantise_weights(grouped):
-            codes = rows.tile([P, P], U32, name="w_codes", align_bytes=64)
-            plane = rows.tile([P, P], U8, name="w_plane", align_bytes=64)
-            nc.vector.quantize_mx(out=codes[:].bitcast(FP8X4), scales=plane[:], in_=grouped[:].rearrange("p q t -> p (q t)"))
-            return codes, plane
+        def quantise(b, first, end):
+            words = slice(first // PACK, end // PACK)
+            nc.vector.quantize_mx(out=codes[b][:, words].bitcast(FP8X4), scales=plane[b][:, words], in_=grouped[b][:, first:end])
 
-        def finish(b, j, w_mx, v_mx, factor):
-            sums = banks.tile([P, DV], F32, name="sums", tag=("bank3", "bank2", "side3", "side0")[b * QT + j])
+        def product(b, j, sums):
+            words = slice(DV + j * P, DV + (j + 1) * P)
             nc.tensor.matmul_mx(
-                out=sums[:], lhsT=w_mx[0][:].bitcast(FP8X4), lhsT_scale=w_mx[1][:],
-                rhs=v_mx[0][:].bitcast(FP8X4), rhs_scale=v_mx[1][:], start=True, stop=True,
+                out=sums, lhsT=codes[b][:, words].bitcast(FP8X4), lhsT_scale=plane[b][:, words],
+                rhs=codes[b][:, 0:DV].bitcast(FP8X4), rhs_scale=plane[b][:, 0:DV], start=True, stop=True,
             )
-            result = keep.tile([P, DV], F32, name="result", tag=("capped3", "capped0", "capped1", "result")[b * QT + j])
-            if b == B - 1 and j == QT - 1:
-                nc.vector.tensor_scalar(result[:], sums[:], factor, None, ALU.mult)
+            return sums
+
+        def finish(u, sums):
+            b, j = tiles[u]
+            result = ends.tile([P, DV], F32, name=f"result{u}", offset=4 * DV * u)
+            if u + 1 == len(tiles):
+                nc.vector.tensor_scalar(result[:], sums, inverse[:, u : u + 1], None, ALU.mult)
             else:
-                nc.scalar.activation(result[:], sums[:], ACT.Copy, scale=factor)
+                nc.scalar.activation(result[:], sums, ACT.Copy, scale=inverse[:, u : u + 1])
             nc.sync.dma_start(out[b, j * P : (j + 1) * P, :], result[:])
 
         tiles = [(b, j) for b in range(B) for j in range(QT)]
-        pos_cols = keep.tile([P, B * PACK], F32, name="pos_cols", tag="v_got0")
-        vs_cols = keep.tile([P, B * PACK], F32, name="vs_cols")
-        columns([pos_got[:, c * P : (c + 1) * P] for c in range(B * PACK)], pos_cols[:], "side0", -STEEP)
-        pos_row = [place_row(b, pos_cols[:, b * PACK : (b + 1) * PACK]) for b in range(B)]
-        vs_got = [keep.tile([P, N], F32, name="vs_got", tag=("vs_got", "pos_got")[b]) for b in range(B)]
+        vs_cols = [keep.tile([P, PACK], F32, name=f"vs_cols{b}") for b in range(B)]
+        vs_got = keep.tile([P, B * N], F32, name="vs_got")
         for b in range(B):
-            nc.scalar.activation(vs_got[b][:], vs_pool[:].indirect(listed(b)), ACT.Copy)
-        v_first = keep.tile([P, B * N], BF16, name="v_first", tag="v_got0")
+            nc.scalar.activation(pos_got[b][:], pos_pool[:].indirect(listed(b)), ACT.Copy)
+        v_last = values.tile([P, T], F32, name="v_last", offset=LAST_AT)
+        nc.gpsimd.memset(v_last[:, 0:SEG], 0.0)
+        nc.sync.dma_start(v_last[:, SEG:T], vT[P : 2 * P, SEG:T])
+        v_pool = {(0, 0): v_first, (0, 1): v_mid, (1, 0): v_mid, (1, 1): v_last}
+        pos_cols = [keep.tile([P, PACK], F32, name="pos_cols0")]
+        columns([pos_got[0][:, c * P : (c + 1) * P] for c in range(PACK)], pos_cols[0][:], "bank0", -STEEP)
+        nc.scalar.activation(vs_got[:], vs_pool[:].indirect(offsets[:]), ACT.Copy)
+        for b in range(B):
+            nc.sync.dma_start(vs_cols[b][:], vs_got[P - 1 : P, b * N : (b + 1) * N])
         both = [gather_keys(0)]
-        nc.vector.tensor_scalar(q_up[:], q_place[:], STEEP * (1.0 + NUDGE), FLOOR, ALU.mult, ALU.add)
-        nc.vector.tensor_scalar(q_down[:], q_place[:], STEEP * (1.0 - NUDGE), FLOOR, ALU.mult, ALU.add)
-        parted = [part_keys(both[0])]
+        pos_cols.append(keep.tile([P, PACK], F32, name="pos_cols1"))
+        columns([pos_got[1][:, c * P : (c + 1) * P] for c in range(PACK)], pos_cols[1][:], "bank2", -STEEP)
+        pos_row = [place_row(0, pos_cols[0], VS_AT + 64)]
+        got = [values.tile([P, N], BF16, name=f"got{h}", offset=VS_AT + 4 * SEG + 2 * N * h) for h in range(HALVES)]
+        nc.scalar.activation(got[0][:], v_first[:].indirect(listed(0)), ACT.Copy)
+        pos_row.append(place_row(1, pos_cols[1], V_AT))
+        nc.gpsimd.tensor_scalar(q_up[:], q_place[:], STEEP * (1.0 + NUDGE), FLOOR, ALU.mult, ALU.add)
+        nc.gpsimd.tensor_scalar(q_down[:], q_place[:], STEEP * (1.0 - NUDGE), FLOOR, ALU.mult, ALU.add)
+        for u in range(len(tiles)):
+            nc.gpsimd.tensor_scalar(q_edge[:, u : u + 1], q_up[:, u : u + 1], q_down[:, u : u + 1], None, ALU.max)
+        parted = [part_keys(0, both[0])]
         both.append(gather_keys(1))
-        nc.vector.tensor_tensor(q_edge[:], q_up[:], q_down[:], ALU.max)
-        parted.append(part_keys(both[1]))
+        parted.append(part_keys(1, both[1]))
         score = [scores(b, j, parted[b]) for b, j in tiles]
 
-        total = [keep.tile([P, QT], F32, name=f"total{b}") for b in range(B)]
-        inverse = [keep.tile([P, QT], F32, name=f"inverse{b}") for b in range(B)]
+        total = keep.tile([P, B * QT], F32, name="total")
+        inverse = keep.tile([P, B * QT], F32, name="inverse")
+        sums = []
         masked = [mask(0, score[0], pos_row[0])]
         tops = []
         for u in range(len(tiles)):
             if u + 1 < len(tiles):
                 masked.append(mask(u + 1, score[u + 1], pos_row[tiles[u + 1][0]]))
             tops.append(row_top(u, masked[u]))
-        columns([vs_got[b][:, t:N:PACK] for b in range(B) for t in range(PACK)], vs_cols[:], "bank2", 1.0)
         v_turned = [banks.tile([P, HALVES, 2, P], F32, name="v_turned", tag=f"bank{b}") for b in range(B)]
 
+        grouped = [held.tile([P, WIDE], BF16, name=f"grouped{b}", offset=2 * WIDE * b, align_bytes=64) for b in range(B)]
+
         def exp_of(u):
-            b, j = tiles[u]
-            return softmax(u, *tops[u], total[b][:, j : j + 1])
+            return softmax(u, *tops[u], total[:, u : u + 1])
 
         def weights_of(u):
-            b = tiles[u][0]
-            return weights(p_turned[u], vs_cols[:, b * PACK : (b + 1) * PACK])
+            weights(*tiles[u], p_turned[u])
 
-        for b in range(B):
-            gather_values(b, 0, v_first[:, b * N : (b + 1) * N], v_turned[b])
+        turn_values(0, got[0][:], v_turned[0])
+        gather_values(0, 1, got[1][:], v_turned[0])
+        gather_values(1, 0, keep.tile([P, N], BF16, name="got_third")[:], v_turned[1])
         p_turned = [exp_of(0), exp_of(1)]
-        gather_values(0, 1, keep.tile([P, N], BF16, name="v_second0")[:], v_turned[0])
+        gather_values(1, 1, keep.tile([P, N], BF16, name="got_last", tag="capped1")[:], v_turned[1])
         p_turned.append(exp_of(2))
-        gather_values(1, 1, keep.tile([P, N], BF16, name="v_second1", tag="capped2")[:], v_turned[1])
+        group_values(1, v_turned[1], nc.scalar.copy)
         p_turned.append(exp_of(3))
-        late_values = group_values(v_turned[1], nc.scalar.copy)
+        group_values(0, v_turned[0], nc.vector.tensor_copy)
 
-        grouped = [weights_of(0)]
-        early_values = group_values(v_turned[0], nc.vector.tensor_copy)
-        grouped.append(weights_of(1))
-        w_mx = [quantise_weights(grouped[0])]
-        v_mx = quantise_values(early_values)
-        w_mx.append(quantise_weights(grouped[1]))
-        nc.vector.reciprocal(inverse[0][:], total[0][:])
-        grouped.extend([weights_of(2), weights_of(3)])
+        for u in range(QT):
+            weights_of(u)
+        quantise(0, 0, WIDE)
+        weights_of(2)
+        early = banks.tile([P, QT, DV], F32, name="early", tag="side2")
         for j in range(QT):
-            finish(0, j, w_mx[j], v_mx, inverse[0][:, j : j + 1])
-        nc.vector.reciprocal(inverse[1][:], total[1][:])
-        w_mx = [quantise_weights(grouped[2])]
-        v_mx = quantise_values(late_values)
-        w_mx.append(quantise_weights(grouped[3]))
+            sums.append(product(0, j, early[:, j, :]))
+        quantise(1, 0, WIDE - N)
+        weights_of(3)
+        nc.vector.reciprocal(inverse[:], total[:])
+        quantise(1, WIDE - N, WIDE)
         for j in range(QT):
-            finish(1, j, w_mx[j], v_mx, inverse[1][:, j : j + 1])
+            sums.append(product(1, j, banks.tile([P, DV], F32, name="sums", tag=f"side{j}")[:]))
+        for u in range(len(tiles)):
+            finish(u, sums[u])

@@ -28,10 +28,12 @@ MASKED = 30000.0
 STEEP = 2.0 ** 80
 NUDGE = 2.0 ** -22
 FLOOR = 2.0 ** 40
-Q_BYTES = 4 * B * PASSES * NQ
+Q_BYTES = 4 * PASSES * NQ
 V_AT = Q_BYTES
-MID_AT = V_AT + 4 * SEG
-LAST_AT = MID_AT + 4 * T
+LATE_Q_AT = V_AT + 4 * SEG
+MID_AT = LATE_Q_AT + Q_BYTES
+THIRD_AT = MID_AT + 4 * SEG
+LAST_AT = THIRD_AT + 4 * T
 VS_AT = LAST_AT + 4 * T
 WIDE = DV * PACK + QT * N
 
@@ -50,11 +52,12 @@ def tile_attend_soft_draft_segb2q256n512t2048_kernel(tc, q_words, q_scales, k_wo
 
         offsets = keep.tile([P, B * LIST_COLS], U16, name="offsets")
         k_pool = keep.tile([P, T], I32, name="k_pool", align_bytes=64)
-        ks_pool = values.tile([P, T], U8, name="ks_pool", offset=MID_AT, align_bytes=64)
-        zeros = values.tile([P, P], F32, name="zeros", offset=Q_BYTES - 256)
+        ks_pool = values.tile([P, T + Q_BYTES + 4 * SEG], U8, name="ks_pool", offset=LATE_Q_AT - T // 2, align_bytes=64)
+        zeros = values.tile([P, P], F32, name="zeros", offset=0)
         q_planes = keep.tile([P, B * PASSES * NQ], U8, name="q_planes", align_bytes=64)
         pos_pool = values.tile([P, T], F32, name="pos_pool", offset=LAST_AT)
         q_place = keep.tile([P, B * QT], F32, name="q_place")
+        q_rows = keep.tile([P, P], F32, name="q_rows")
         q_up = keep.tile([P, B * QT], F32, name="q_up")
         q_down = keep.tile([P, B * QT], F32, name="q_down")
         q_edge = keep.tile([P, B * QT], F32, name="q_edge")
@@ -74,39 +77,42 @@ def tile_attend_soft_draft_segb2q256n512t2048_kernel(tc, q_words, q_scales, k_wo
             nc.vector.memset(words[:, cut:], 0)
 
         nc.gpsimd.memset(pos_pool[0 : P - 1, :], 0.0)
-        clear(zeros[:].bitcast(I32))
         clear(q_planes[:].bitcast(I32))
-        clear(ks_pool[0:96, :].bitcast(I32))
+        clear(zeros[:].bitcast(I32))
+        clear(ks_pool[0:96, 0:T].bitcast(I32))
         clear(k_planes[:].bitcast(I32))
+        clear(q_rows[0 : P - B * QT, :].bitcast(I32))
         nc.gpsimd.affine_select(
             out=ident[:], in_=zeros[:], compare_op=ALU.not_equal, fill=1.0, base=0, pattern=[[-1, P]], channel_multiplier=1,
         )
-        q_codes = values.tile([P, B * PASSES, NQ], I32, name="q_codes", offset=0)
+        q_codes = [values.tile([P, PASSES, NQ], I32, name="q_codes0", offset=0)]
         nc.gpsimd.memset(vs_pool[0 : P - 1, :], 0.0)
 
         k_flat = k_words[0].rearrange("p t r -> p (t r)").bitcast(I32)
         nc.sync.dma_start(offsets[:], offs)
-        nc.sync.dma_start(ks_pool[96:P, :].bitcast(I32), k_scales.rearrange("o f t -> f o t").bitcast(I32))
+        nc.sync.dma_start(ks_pool[96:P, 0:T].bitcast(I32), k_scales.rearrange("o f t -> f o t").bitcast(I32))
         nc.sync.dma_start(pos_pool[P - 1 : P, :], pos[0:1, :])
         nc.sync.dma_start(vs_pool[P - 1 : P, :], vs[0:1, :])
-        for b in range(B):
-            nc.sync.dma_start(k_pool[:, b * SEG : (b + 1) * SEG], k_flat[:, b * SEG : (b + 1) * SEG])
-        with nc.allow_non_contiguous_dma(reason="one place a partition"):
-            nc.sync.dma_start(q_place[:], qpos.rearrange("b (j p) o -> p (b j o)", p=P))
+        nc.sync.dma_start(k_pool[:, 0:SEG], k_flat[:, 0:SEG])
+        nc.sync.dma_start(q_rows[P - B * QT : P, :], qpos.rearrange("b (j p) o -> (b j) (p o)", p=P))
         for quad in range(4):
             nc.sync.dma_start(
                 q_planes[32 * quad : 32 * quad + 4, :].bitcast(I32).rearrange("j (g q) -> j g q", g=B * PASSES),
                 q_scales[:, :, 4 * quad : 4 * quad + 4, :].rearrange("b o j q -> j (b o) q").bitcast(I32),
             )
-        nc.sync.dma_start(q_codes[:], q_words.rearrange("b o p q r -> p (b o) (q r)").bitcast(I32))
-        v_first = values.tile([P, SEG], F32, name="v_first", offset=V_AT)
-        nc.sync.dma_start(v_first[:], vT[0:P, 0:SEG])
-        nc.vector.tensor_copy(ks_got[:], ks_pool[:].indirect(offsets[:]))
+        nc.sync.dma_start(k_pool[:, SEG:T], k_flat[:, SEG:T])
+        nc.sync.dma_start(q_codes[0][:], q_words[0].rearrange("o p q r -> p o (q r)").bitcast(I32))
+        nc.vector.tensor_copy(ks_got[:], ks_pool[:, 0:T].indirect(offsets[:]))
         for quad in range(4):
             nc.sync.dma_start(k_planes[32 * quad : 32 * quad + 4, :].bitcast(I32), ks_got[96 + 8 * quad : 96 + 8 * quad + 8, :].bitcast(I32))
-        v_mid = values.tile([P, T], F32, name="v_mid", offset=MID_AT)
-        nc.sync.dma_start(v_mid[:, 0:SEG], vT[P : 2 * P, 0:SEG])
-        nc.sync.dma_start(v_mid[:, SEG:T], vT[0:P, SEG:T])
+        v_first = values.tile([P, SEG], F32, name="v_first", offset=V_AT)
+        nc.sync.dma_start(v_first[:], vT[0:P, 0:SEG])
+        q_codes.append(values.tile([P, PASSES, NQ], I32, name="q_codes1", offset=LATE_Q_AT))
+        nc.sync.dma_start(q_codes[1][:], q_words[1].rearrange("o p q r -> p o (q r)").bitcast(I32))
+        v_second = values.tile([P, SEG], F32, name="v_second", offset=MID_AT)
+        nc.sync.dma_start(v_second[:], vT[P : 2 * P, 0:SEG])
+        v_third = values.tile([P, T], F32, name="v_third", offset=THIRD_AT)
+        nc.sync.dma_start(v_third[:, SEG:T], vT[0:P, SEG:T])
 
         def listed(b):
             return offsets[:, b * LIST_COLS : (b + 1) * LIST_COLS]
@@ -145,7 +151,7 @@ def tile_attend_soft_draft_segb2q256n512t2048_kernel(tc, q_words, q_scales, k_wo
                 first = (b * PASSES + o) * NQ + j * P
                 nc.tensor.matmul_mx(
                     out=bank[:],
-                    lhsT=q_codes[:, b * PASSES + o, j * P : (j + 1) * P].bitcast(FP8X4),
+                    lhsT=q_codes[b][:, o, j * P : (j + 1) * P].bitcast(FP8X4),
                     lhsT_scale=q_planes[:, first : first + P],
                     rhs=parted[:, o * 2 * N : (o + 1) * 2 * N].bitcast(FP4X4),
                     rhs_scale=k_planes[:, (o * B + b) * N : (o * B + b + 1) * N],
@@ -171,7 +177,7 @@ def tile_attend_soft_draft_segb2q256n512t2048_kernel(tc, q_words, q_scales, k_wo
         def softmax(u, capped, top, total):
             shift = rows.tile([P, 1], F32, name="shift")
             nc.gpsimd.tensor_scalar(shift[:], top[:], -1.0, 0.0, ALU.mult, ALU.add)
-            p = values.tile([P, N], F32, name=f"p{u}", offset=(MID_AT if u < QT else LAST_AT) + 4 * N * (u % QT))
+            p = values.tile([P, N], F32, name=f"p{u}", offset=(MID_AT, MID_AT + 4 * N, THIRD_AT, LAST_AT)[u])
             nc.scalar.activation(p[:], capped[:], ACT.Exp, bias=shift[:], accum_out=total)
             turned = banks.tile([P, PACK, P], F32, name="p_turned", tag=f"side{u}")
             for t in range(PACK):
@@ -190,9 +196,9 @@ def tile_attend_soft_draft_segb2q256n512t2048_kernel(tc, q_words, q_scales, k_wo
         codes = [keep.tile([P, WIDE // PACK], U32, name=f"codes{b}", align_bytes=64) for b in range(B)]
         plane = [keep.tile([P, WIDE // PACK], U8, name=f"plane{b}", align_bytes=64) for b in range(B)]
 
-        def group_values(b, turned, copy):
+        def group_values(target, turned, copy):
             copy(
-                grouped[b][:, 0 : DV * PACK].bitcast(F32).rearrange("p (h c u) -> p h c u", h=HALVES, u=2),
+                target[:, 0 : DV * PACK].bitcast(F32).rearrange("p (h c u) -> p h c u", h=HALVES, u=2),
                 turned[:].rearrange("p h u c -> p h c u"),
             )
 
@@ -203,9 +209,9 @@ def tile_attend_soft_draft_segb2q256n512t2048_kernel(tc, q_words, q_scales, k_wo
                 vs_cols[b][:].unsqueeze(1).to_broadcast([P, P, PACK]), ALU.mult,
             )
 
-        def quantise(b, first, end):
+        def quantise(b, source, first, end):
             words = slice(first // PACK, end // PACK)
-            nc.vector.quantize_mx(out=codes[b][:, words].bitcast(FP8X4), scales=plane[b][:, words], in_=grouped[b][:, first:end])
+            nc.vector.quantize_mx(out=codes[b][:, words].bitcast(FP8X4), scales=plane[b][:, words], in_=source[:, first:end])
 
         def product(b, j, sums):
             words = slice(DV + j * P, DV + (j + 1) * P)
@@ -227,12 +233,14 @@ def tile_attend_soft_draft_segb2q256n512t2048_kernel(tc, q_words, q_scales, k_wo
         tiles = [(b, j) for b in range(B) for j in range(QT)]
         vs_cols = [keep.tile([P, PACK], F32, name=f"vs_cols{b}") for b in range(B)]
         vs_got = keep.tile([P, B * N], F32, name="vs_got")
+        q_turned = banks.tile([P, P], F32, name="q_turned", tag="side0")
+        nc.tensor.transpose(q_turned[:], q_rows[:], ident[:])
+        nc.scalar.copy(q_place[:], q_turned[:, P - B * QT : P])
         for b in range(B):
             nc.scalar.activation(pos_got[b][:], pos_pool[:].indirect(listed(b)), ACT.Copy)
         v_last = values.tile([P, T], F32, name="v_last", offset=LAST_AT)
-        nc.gpsimd.memset(v_last[:, 0:SEG], 0.0)
         nc.sync.dma_start(v_last[:, SEG:T], vT[P : 2 * P, SEG:T])
-        v_pool = {(0, 0): v_first, (0, 1): v_mid, (1, 0): v_mid, (1, 1): v_last}
+        v_pool = {(0, 0): v_first, (0, 1): v_second, (1, 0): v_third, (1, 1): v_last}
         pos_cols = [keep.tile([P, PACK], F32, name="pos_cols0")]
         columns([pos_got[0][:, c * P : (c + 1) * P] for c in range(PACK)], pos_cols[0][:], "bank0", -STEEP)
         nc.scalar.activation(vs_got[:], vs_pool[:].indirect(offsets[:]), ACT.Copy)
@@ -242,13 +250,15 @@ def tile_attend_soft_draft_segb2q256n512t2048_kernel(tc, q_words, q_scales, k_wo
         pos_cols.append(keep.tile([P, PACK], F32, name="pos_cols1"))
         columns([pos_got[1][:, c * P : (c + 1) * P] for c in range(PACK)], pos_cols[1][:], "bank2", -STEEP)
         pos_row = [place_row(0, pos_cols[0], VS_AT + 64)]
-        got = [values.tile([P, N], BF16, name=f"got{h}", offset=VS_AT + 4 * SEG + 2 * N * h) for h in range(HALVES)]
+        got = [values.tile([P, N], BF16, name=f"got{h}", offset=VS_AT + 6 * SEG + 2 * N * h) for h in range(HALVES)]
+        pos_row.append(place_row(1, pos_cols[1], VS_AT + 64 + 4 * N))
         nc.scalar.activation(got[0][:], v_first[:].indirect(listed(0)), ACT.Copy)
-        pos_row.append(place_row(1, pos_cols[1], V_AT))
         nc.gpsimd.tensor_scalar(q_up[:], q_place[:], STEEP * (1.0 + NUDGE), FLOOR, ALU.mult, ALU.add)
         nc.gpsimd.tensor_scalar(q_down[:], q_place[:], STEEP * (1.0 - NUDGE), FLOOR, ALU.mult, ALU.add)
         for u in range(len(tiles)):
             nc.gpsimd.tensor_scalar(q_edge[:, u : u + 1], q_up[:, u : u + 1], q_down[:, u : u + 1], None, ALU.max)
+        nc.gpsimd.memset(v_third[:, 0:SEG], 0.0)
+        nc.gpsimd.memset(v_last[:, 0:SEG], 0.0)
         parted = [part_keys(0, both[0])]
         both.append(gather_keys(1))
         parted.append(part_keys(1, both[1]))
@@ -275,25 +285,27 @@ def tile_attend_soft_draft_segb2q256n512t2048_kernel(tc, q_words, q_scales, k_wo
 
         turn_values(0, got[0][:], v_turned[0])
         gather_values(0, 1, got[1][:], v_turned[0])
-        gather_values(1, 0, keep.tile([P, N], BF16, name="got_third")[:], v_turned[1])
         p_turned = [exp_of(0), exp_of(1)]
-        gather_values(1, 1, keep.tile([P, N], BF16, name="got_last", tag="capped1")[:], v_turned[1])
+        gather_values(1, 0, keep.tile([P, N], BF16, name="got_third", tag="capped1")[:], v_turned[1])
         p_turned.append(exp_of(2))
-        group_values(1, v_turned[1], nc.scalar.copy)
+        gather_values(1, 1, keep.tile([P, N], BF16, name="got_last", tag="capped2")[:], v_turned[1])
         p_turned.append(exp_of(3))
-        group_values(0, v_turned[0], nc.vector.tensor_copy)
+        late_values = keep.tile([P, DV * PACK], BF16, name="late_values", align_bytes=64)
+        group_values(late_values, v_turned[1], nc.scalar.copy)
+        group_values(grouped[0], v_turned[0], nc.vector.tensor_copy)
 
         for u in range(QT):
             weights_of(u)
-        quantise(0, 0, WIDE)
+        quantise(0, grouped[0], 0, WIDE)
         weights_of(2)
-        early = banks.tile([P, QT, DV], F32, name="early", tag="side2")
+        early = banks.tile([P, QT, DV], F32, name="early", tag="bank2")
         for j in range(QT):
             sums.append(product(0, j, early[:, j, :]))
-        quantise(1, 0, WIDE - N)
-        weights_of(3)
+        quantise(1, grouped[1], DV * PACK, WIDE - N)
         nc.vector.reciprocal(inverse[:], total[:])
-        quantise(1, WIDE - N, WIDE)
+        weights_of(3)
+        quantise(1, late_values, 0, DV * PACK)
+        quantise(1, grouped[1], WIDE - N, WIDE)
         for j in range(QT):
             sums.append(product(1, j, banks.tile([P, DV], F32, name="sums", tag=f"side{j}")[:]))
         for u in range(len(tiles)):

@@ -51,19 +51,18 @@ def tile_attend_soft_draft_segb2q256n512t2048_kernel(tc, q_words, q_scales, k_wo
         rows = ctx.enter_context(tc.tile_pool(name="rows", bufs=B * QT))
 
         offsets = keep.tile([P, B * LIST_COLS], U16, name="offsets")
-        k_pool = keep.tile([P, T], I32, name="k_pool", align_bytes=64)
+        k_pool = values.tile([P, T], I32, name="k_pool", offset=LAST_AT, align_bytes=64)
         ks_pool = values.tile([P, T + Q_BYTES + 4 * SEG], U8, name="ks_pool", offset=LATE_Q_AT - T // 2, align_bytes=64)
         zeros = values.tile([P, P], F32, name="zeros", offset=0)
         q_planes = keep.tile([P, B * PASSES * NQ], U8, name="q_planes", align_bytes=64)
-        pos_pool = values.tile([P, T], F32, name="pos_pool", offset=LAST_AT)
-        q_place = keep.tile([P, B * QT], F32, name="q_place")
+        pos_pool = keep.tile([P, T], F32, name="pos_pool")
         q_rows = keep.tile([P, P], F32, name="q_rows")
         q_up = keep.tile([P, B * QT], F32, name="q_up")
         q_down = keep.tile([P, B * QT], F32, name="q_down")
         q_edge = keep.tile([P, B * QT], F32, name="q_edge")
         ks_got = keep.tile([P, B * N], U8, name="ks_got", align_bytes=64)
         k_planes = keep.tile([P, PASSES * B * N], U8, name="k_planes", align_bytes=64)
-        pos_got = [keys.tile([P, N], F32, name=f"pos_got{b}", offset=(10 * N, 4 * N)[b]) for b in range(B)]
+        pos_got = [keys.tile([P, N], F32, name=f"pos_got{b}", offset=(0, 12 * N)[b]) for b in range(B)]
         ident = keep.tile([P, P], F32, name="ident")
         vs_pool = values.tile([P, T], F32, name="vs_pool", offset=VS_AT)
 
@@ -118,12 +117,12 @@ def tile_attend_soft_draft_segb2q256n512t2048_kernel(tc, q_words, q_scales, k_wo
             return offsets[:, b * LIST_COLS : (b + 1) * LIST_COLS]
 
         def gather_keys(b):
-            both = keys.tile([P, N], U32, name=f"k_both{b}", offset=(10 * N, 6 * N)[b])
+            both = keys.tile([P, N], U32, name=f"k_both{b}", offset=(0, 14 * N)[b])
             nc.vector.tensor_copy(both[:], k_pool[:, 0 : (b + 1) * SEG].bitcast(U32).indirect(listed(b)))
             return both
 
         def part_keys(b, both):
-            parted = keys.tile([P, PASSES * 2 * N], U8, name=f"k_parted{b}", offset=(2 * N, 14 * N)[b], align_bytes=64)
+            parted = keys.tile([P, PASSES * 2 * N], U8, name=f"k_parted{b}", offset=(10 * N, 4 * N)[b], align_bytes=64)
             nc.vector.tensor_copy(
                 parted[:].bitcast(U16).rearrange("p (o n) -> p o n", o=PASSES),
                 both[:].bitcast(U16).rearrange("p (n o) -> p o n", o=PASSES),
@@ -135,7 +134,7 @@ def tile_attend_soft_draft_segb2q256n512t2048_kernel(tc, q_words, q_scales, k_wo
             count = len(sources)
             for c in reversed(range(count)):
                 nc.tensor.transpose(turned[:, 2 * c : 2 * c + P], sources[c], ident[:])
-            nc.vector.tensor_scalar(cols, turned[:, P - 1 : P - 1 + 2 * count : 2], factor, None, ALU.mult)
+            nc.vector.tensor_scalar(cols, turned[:, P - 1 : P - 1 + 2 * count : 2], factor, FLOOR, ALU.mult, ALU.add)
 
         def place_row(b, cols, at):
             spread = banks.tile([P, PACK, P], F32, name="pos_spread", tag=("bank1", "bank3")[b])
@@ -177,7 +176,7 @@ def tile_attend_soft_draft_segb2q256n512t2048_kernel(tc, q_words, q_scales, k_wo
         def softmax(u, capped, top, total):
             shift = rows.tile([P, 1], F32, name="shift")
             nc.gpsimd.tensor_scalar(shift[:], top[:], -1.0, 0.0, ALU.mult, ALU.add)
-            p = values.tile([P, N], F32, name=f"p{u}", offset=(MID_AT, MID_AT + 4 * N, THIRD_AT, LAST_AT)[u])
+            p = (values if u < 3 else keys).tile([P, N], F32, name=f"p{u}", offset=(MID_AT, MID_AT + 4 * N, THIRD_AT, 14 * N)[u])
             nc.scalar.activation(p[:], capped[:], ACT.Exp, bias=shift[:], accum_out=total)
             turned = banks.tile([P, PACK, P], F32, name="p_turned", tag=f"side{u}")
             for t in range(PACK):
@@ -235,12 +234,12 @@ def tile_attend_soft_draft_segb2q256n512t2048_kernel(tc, q_words, q_scales, k_wo
         vs_got = keep.tile([P, B * N], F32, name="vs_got")
         q_turned = banks.tile([P, P], F32, name="q_turned", tag="side0")
         nc.tensor.transpose(q_turned[:], q_rows[:], ident[:])
-        nc.scalar.copy(q_place[:], q_turned[:, P - B * QT : P])
+        nc.scalar.activation(q_up[:], q_turned[:, P - B * QT : P], ACT.Copy, scale=STEEP)
+        nc.scalar.activation(q_down[:], q_turned[:, P - B * QT : P], ACT.Abs, scale=STEEP * NUDGE)
+        nc.gpsimd.tensor_tensor(q_edge[:], q_up[:], q_down[:], ALU.add)
+        nc.gpsimd.memset(v_third[:, 0:SEG], 0.0)
         for b in range(B):
             nc.scalar.activation(pos_got[b][:], pos_pool[:].indirect(listed(b)), ACT.Copy)
-        v_last = values.tile([P, T], F32, name="v_last", offset=LAST_AT)
-        nc.sync.dma_start(v_last[:, SEG:T], vT[P : 2 * P, SEG:T])
-        v_pool = {(0, 0): v_first, (0, 1): v_second, (1, 0): v_third, (1, 1): v_last}
         pos_cols = [keep.tile([P, PACK], F32, name="pos_cols0")]
         columns([pos_got[0][:, c * P : (c + 1) * P] for c in range(PACK)], pos_cols[0][:], "bank0", -STEEP)
         nc.scalar.activation(vs_got[:], vs_pool[:].indirect(offsets[:]), ACT.Copy)
@@ -253,15 +252,13 @@ def tile_attend_soft_draft_segb2q256n512t2048_kernel(tc, q_words, q_scales, k_wo
         got = [values.tile([P, N], BF16, name=f"got{h}", offset=VS_AT + 6 * SEG + 2 * N * h) for h in range(HALVES)]
         pos_row.append(place_row(1, pos_cols[1], VS_AT + 64 + 4 * N))
         nc.scalar.activation(got[0][:], v_first[:].indirect(listed(0)), ACT.Copy)
-        nc.gpsimd.tensor_scalar(q_up[:], q_place[:], STEEP * (1.0 + NUDGE), FLOOR, ALU.mult, ALU.add)
-        nc.gpsimd.tensor_scalar(q_down[:], q_place[:], STEEP * (1.0 - NUDGE), FLOOR, ALU.mult, ALU.add)
-        for u in range(len(tiles)):
-            nc.gpsimd.tensor_scalar(q_edge[:, u : u + 1], q_up[:, u : u + 1], q_down[:, u : u + 1], None, ALU.max)
-        nc.gpsimd.memset(v_third[:, 0:SEG], 0.0)
-        nc.gpsimd.memset(v_last[:, 0:SEG], 0.0)
         parted = [part_keys(0, both[0])]
         both.append(gather_keys(1))
         parted.append(part_keys(1, both[1]))
+        v_last = keys.tile([P, T], F32, name="v_last", offset=14 * N)
+        nc.gpsimd.memset(v_last[:, 0:SEG], 0.0)
+        nc.sync.dma_start(v_last[:, SEG:T], vT[P : 2 * P, SEG:T])
+        v_pool = {(0, 0): v_first, (0, 1): v_second, (1, 0): v_third, (1, 1): v_last}
         score = [scores(b, j, parted[b]) for b, j in tiles]
 
         total = keep.tile([P, B * QT], F32, name="total")

@@ -32,7 +32,7 @@ Q_BYTES = 4 * PASSES * NQ
 V_AT = Q_BYTES
 LATE_Q_AT = V_AT + 4 * SEG
 MID_AT = LATE_Q_AT + Q_BYTES
-THIRD_AT = MID_AT + 4 * SEG
+THIRD_AT = MID_AT + 4 * SEG + 6 * N
 LAST_AT = THIRD_AT + 4 * T
 VS_AT = LAST_AT + 4 * T
 WIDE = DV * PACK + QT * N
@@ -52,7 +52,7 @@ def tile_attend_soft_draft_segb2q256n512t2048_kernel(tc, q_words, q_scales, k_wo
 
         offsets = keep.tile([P, B * LIST_COLS], U16, name="offsets")
         k_pool = values.tile([P, T], I32, name="k_pool", offset=LAST_AT, align_bytes=64)
-        ks_pool = values.tile([P, T + Q_BYTES + 4 * SEG], U8, name="ks_pool", offset=LATE_Q_AT - T // 2, align_bytes=64)
+        ks_pool = values.tile([P, T + Q_BYTES + 4 * SEG + 6 * N], U8, name="ks_pool", offset=LATE_Q_AT - T // 2, align_bytes=64)
         zeros = values.tile([P, P], F32, name="zeros", offset=0)
         q_planes = keep.tile([P, B * PASSES * NQ], U8, name="q_planes", align_bytes=64)
         pos_pool = keep.tile([P, T], F32, name="pos_pool")
@@ -176,7 +176,7 @@ def tile_attend_soft_draft_segb2q256n512t2048_kernel(tc, q_words, q_scales, k_wo
         def softmax(u, capped, top, total):
             shift = rows.tile([P, 1], F32, name="shift")
             nc.gpsimd.tensor_scalar(shift[:], top[:], -1.0, 0.0, ALU.mult, ALU.add)
-            p = (values if u < 3 else keys).tile([P, N], F32, name=f"p{u}", offset=(MID_AT, MID_AT + 4 * N, THIRD_AT, 14 * N)[u])
+            p = (values if u < 3 else keys).tile([P, N], F32, name=f"p{u}", offset=(MID_AT, MID_AT + 6 * N, MID_AT + 10 * N, 14 * N)[u])
             nc.scalar.activation(p[:], capped[:], ACT.Exp, bias=shift[:], accum_out=total)
             turned = banks.tile([P, PACK, P], F32, name="p_turned", tag=f"side{u}")
             for t in range(PACK):
@@ -283,9 +283,9 @@ def tile_attend_soft_draft_segb2q256n512t2048_kernel(tc, q_words, q_scales, k_wo
         turn_values(0, got[0][:], v_turned[0])
         gather_values(0, 1, got[1][:], v_turned[0])
         p_turned = [exp_of(0), exp_of(1)]
-        gather_values(1, 0, keep.tile([P, N], BF16, name="got_third", tag="capped1")[:], v_turned[1])
+        gather_values(1, 0, keep.tile([P, N], BF16, name="got_third", tag="capped0")[:], v_turned[1])
         p_turned.append(exp_of(2))
-        gather_values(1, 1, keep.tile([P, N], BF16, name="got_last", tag="capped2")[:], v_turned[1])
+        gather_values(1, 1, keep.tile([P, N], BF16, name="got_last", tag="capped1")[:], v_turned[1])
         p_turned.append(exp_of(3))
         late_values = keep.tile([P, DV * PACK], BF16, name="late_values", align_bytes=64)
         group_values(late_values, v_turned[1], nc.scalar.copy)

@@ -33,6 +33,7 @@ V_AT = Q_BYTES
 LATE_Q_AT = V_AT + 4 * SEG
 MID_AT = LATE_Q_AT + Q_BYTES
 THIRD_AT = MID_AT + 4 * SEG + 6 * N
+POS_AT = MID_AT
 LAST_AT = THIRD_AT + 4 * T
 VS_AT = LAST_AT + 4 * T
 WIDE = DV * PACK + QT * N
@@ -43,7 +44,6 @@ def tile_attend_soft_draft_segb2q256n512t2048_kernel(tc, q_words, q_scales, k_wo
     with ExitStack() as ctx:
         keep = ctx.enter_context(tc.tile_pool(name="keep", bufs=1))
         values = ctx.enter_context(tc.tile_pool(name="values", bufs=1))
-        ends = ctx.enter_context(tc.tile_pool(name="ends", bufs=1))
         held = ctx.enter_context(tc.tile_pool(name="held", bufs=1))
         keys = ctx.enter_context(tc.tile_pool(name="keys", bufs=1))
         work = ctx.enter_context(tc.tile_pool(name="work", bufs=2))
@@ -52,10 +52,10 @@ def tile_attend_soft_draft_segb2q256n512t2048_kernel(tc, q_words, q_scales, k_wo
 
         offsets = keep.tile([P, B * LIST_COLS], U16, name="offsets")
         k_pool = values.tile([P, T], I32, name="k_pool", offset=LAST_AT, align_bytes=64)
-        ks_pool = values.tile([P, T + Q_BYTES + 4 * SEG + 6 * N], U8, name="ks_pool", offset=LATE_Q_AT - T // 2, align_bytes=64)
+        ks_pool = values.tile([P, T], U8, name="ks_pool", offset=LATE_Q_AT - T // 2, align_bytes=64)
         zeros = values.tile([P, P], F32, name="zeros", offset=0)
         q_planes = keep.tile([P, B * PASSES * NQ], U8, name="q_planes", align_bytes=64)
-        pos_pool = keep.tile([P, T], F32, name="pos_pool")
+        pos_pool = values.tile([P, T], F32, name="pos_pool", offset=POS_AT)
         q_rows = keep.tile([P, P], F32, name="q_rows")
         q_up = keep.tile([P, B * QT], F32, name="q_up")
         q_down = keep.tile([P, B * QT], F32, name="q_down")
@@ -78,7 +78,7 @@ def tile_attend_soft_draft_segb2q256n512t2048_kernel(tc, q_words, q_scales, k_wo
         nc.gpsimd.memset(pos_pool[0 : P - 1, :], 0.0)
         clear(q_planes[:].bitcast(I32))
         clear(zeros[:].bitcast(I32))
-        clear(ks_pool[0:96, 0:T].bitcast(I32))
+        clear(ks_pool[0:96, :].bitcast(I32))
         clear(k_planes[:].bitcast(I32))
         clear(q_rows[0 : P - B * QT, :].bitcast(I32))
         nc.gpsimd.affine_select(
@@ -89,7 +89,7 @@ def tile_attend_soft_draft_segb2q256n512t2048_kernel(tc, q_words, q_scales, k_wo
 
         k_flat = k_words[0].rearrange("p t r -> p (t r)").bitcast(I32)
         nc.sync.dma_start(offsets[:], offs)
-        nc.sync.dma_start(ks_pool[96:P, 0:T].bitcast(I32), k_scales.rearrange("o f t -> f o t").bitcast(I32))
+        nc.sync.dma_start(ks_pool[96:P, :].bitcast(I32), k_scales.rearrange("o f t -> f o t").bitcast(I32))
         nc.sync.dma_start(pos_pool[P - 1 : P, :], pos[0:1, :])
         nc.sync.dma_start(vs_pool[P - 1 : P, :], vs[0:1, :])
         nc.sync.dma_start(k_pool[:, 0:SEG], k_flat[:, 0:SEG])
@@ -101,17 +101,13 @@ def tile_attend_soft_draft_segb2q256n512t2048_kernel(tc, q_words, q_scales, k_wo
             )
         nc.sync.dma_start(k_pool[:, SEG:T], k_flat[:, SEG:T])
         nc.sync.dma_start(q_codes[0][:], q_words[0].rearrange("o p q r -> p o (q r)").bitcast(I32))
-        nc.vector.tensor_copy(ks_got[:], ks_pool[:, 0:T].indirect(offsets[:]))
+        nc.vector.tensor_copy(ks_got[:], ks_pool[:].indirect(offsets[:]))
         for quad in range(4):
             nc.sync.dma_start(k_planes[32 * quad : 32 * quad + 4, :].bitcast(I32), ks_got[96 + 8 * quad : 96 + 8 * quad + 8, :].bitcast(I32))
         v_first = values.tile([P, SEG], F32, name="v_first", offset=V_AT)
         nc.sync.dma_start(v_first[:], vT[0:P, 0:SEG])
         q_codes.append(values.tile([P, PASSES, NQ], I32, name="q_codes1", offset=LATE_Q_AT))
         nc.sync.dma_start(q_codes[1][:], q_words[1].rearrange("o p q r -> p o (q r)").bitcast(I32))
-        v_second = values.tile([P, SEG], F32, name="v_second", offset=MID_AT)
-        nc.sync.dma_start(v_second[:], vT[P : 2 * P, 0:SEG])
-        v_third = values.tile([P, T], F32, name="v_third", offset=THIRD_AT)
-        nc.sync.dma_start(v_third[:, SEG:T], vT[0:P, SEG:T])
 
         def listed(b):
             return offsets[:, b * LIST_COLS : (b + 1) * LIST_COLS]
@@ -168,7 +164,7 @@ def tile_attend_soft_draft_segb2q256n512t2048_kernel(tc, q_words, q_scales, k_wo
             return masked
 
         def row_top(u, masked):
-            capped = keep.tile([P, N], F32, name="capped", tag=f"capped{u}") if u < 3 else ends.tile([P, N], F32, name="capped_last", offset=0)
+            capped = keys.tile([P, N], F32, name=f"capped{u}", offset=30 * N + 4 * N * u)
             top = rows.tile([P, 1], F32, name="top")
             nc.vector.tensor_scalar(capped[:], masked[:], -MASKED, None, ALU.max, ALU.max, accum_out=top[:])
             return capped, top
@@ -176,7 +172,7 @@ def tile_attend_soft_draft_segb2q256n512t2048_kernel(tc, q_words, q_scales, k_wo
         def softmax(u, capped, top, total):
             shift = rows.tile([P, 1], F32, name="shift")
             nc.gpsimd.tensor_scalar(shift[:], top[:], -1.0, 0.0, ALU.mult, ALU.add)
-            p = (values if u < 3 else keys).tile([P, N], F32, name=f"p{u}", offset=(MID_AT, MID_AT + 6 * N, MID_AT + 10 * N, 14 * N)[u])
+            p = values.tile([P, N], F32, name=f"p{u}", offset=(MID_AT, MID_AT + 6 * N, MID_AT + 10 * N, THIRD_AT)[u])
             nc.scalar.activation(p[:], capped[:], ACT.Exp, bias=shift[:], accum_out=total)
             turned = banks.tile([P, PACK, P], F32, name="p_turned", tag=f"side{u}")
             for t in range(PACK):
@@ -222,7 +218,7 @@ def tile_attend_soft_draft_segb2q256n512t2048_kernel(tc, q_words, q_scales, k_wo
 
         def finish(u, sums):
             b, j = tiles[u]
-            result = ends.tile([P, DV], F32, name=f"result{u}", offset=4 * DV * u)
+            result = keys.tile([P, DV], F32, name=f"result{u}", offset=(38 * N, 40 * N, 14 * N, 16 * N)[u])
             if u + 1 == len(tiles):
                 nc.vector.tensor_scalar(result[:], sums, inverse[:, u : u + 1], None, ALU.mult)
             else:
@@ -237,9 +233,13 @@ def tile_attend_soft_draft_segb2q256n512t2048_kernel(tc, q_words, q_scales, k_wo
         nc.scalar.activation(q_up[:], q_turned[:, P - B * QT : P], ACT.Copy, scale=STEEP)
         nc.scalar.activation(q_down[:], q_turned[:, P - B * QT : P], ACT.Abs, scale=STEEP * NUDGE)
         nc.gpsimd.tensor_tensor(q_edge[:], q_up[:], q_down[:], ALU.add)
-        nc.gpsimd.memset(v_third[:, 0:SEG], 0.0)
         for b in range(B):
             nc.scalar.activation(pos_got[b][:], pos_pool[:].indirect(listed(b)), ACT.Copy)
+        v_second = values.tile([P, SEG], F32, name="v_second", offset=MID_AT)
+        nc.sync.dma_start(v_second[:], vT[P : 2 * P, 0:SEG])
+        v_third = values.tile([P, T], F32, name="v_third", offset=THIRD_AT)
+        nc.sync.dma_start(v_third[:, SEG:T], vT[0:P, SEG:T])
+        nc.gpsimd.memset(v_third[:, 0:SEG], 0.0)
         pos_cols = [keep.tile([P, PACK], F32, name="pos_cols0")]
         columns([pos_got[0][:, c * P : (c + 1) * P] for c in range(PACK)], pos_cols[0][:], "bank0", -STEEP)
         nc.scalar.activation(vs_got[:], vs_pool[:].indirect(offsets[:]), ACT.Copy)
@@ -283,10 +283,10 @@ def tile_attend_soft_draft_segb2q256n512t2048_kernel(tc, q_words, q_scales, k_wo
         turn_values(0, got[0][:], v_turned[0])
         gather_values(0, 1, got[1][:], v_turned[0])
         p_turned = [exp_of(0), exp_of(1)]
-        gather_values(1, 0, keep.tile([P, N], BF16, name="got_third", tag="capped0")[:], v_turned[1])
+        gather_values(1, 0, keys.tile([P, N], BF16, name="got_third", offset=30 * N)[:], v_turned[1])
         p_turned.append(exp_of(2))
-        gather_values(1, 1, keep.tile([P, N], BF16, name="got_last", tag="capped1")[:], v_turned[1])
         p_turned.append(exp_of(3))
+        gather_values(1, 1, keys.tile([P, N], BF16, name="got_last", offset=39 * N)[:], v_turned[1])
         late_values = keep.tile([P, DV * PACK], BF16, name="late_values", align_bytes=64)
         group_values(late_values, v_turned[1], nc.scalar.copy)
         group_values(grouped[0], v_turned[0], nc.vector.tensor_copy)
@@ -294,15 +294,14 @@ def tile_attend_soft_draft_segb2q256n512t2048_kernel(tc, q_words, q_scales, k_wo
         for u in range(QT):
             weights_of(u)
         quantise(0, grouped[0], 0, WIDE)
+        nc.vector.reciprocal(inverse[:], total[:])
         weights_of(2)
         early = banks.tile([P, QT, DV], F32, name="early", tag="bank2")
         for j in range(QT):
             sums.append(product(0, j, early[:, j, :]))
-        quantise(1, grouped[1], DV * PACK, WIDE - N)
-        nc.vector.reciprocal(inverse[:], total[:])
         weights_of(3)
         quantise(1, late_values, 0, DV * PACK)
-        quantise(1, grouped[1], WIDE - N, WIDE)
+        quantise(1, grouped[1], DV * PACK, WIDE)
         for j in range(QT):
             sums.append(product(1, j, banks.tile([P, DV], F32, name="sums", tag=f"side{j}")[:]))
         for u in range(len(tiles)):

@@ -120,8 +120,8 @@ def tile_attend_soft_draft_segb2q256n512t2048_kernel(tc, q_words, q_scales, k_wo
         def part_keys(b, both):
             parted = keys.tile([P, PASSES * 2 * N], U8, name=f"k_parted{b}", offset=(10 * N, 4 * N)[b], align_bytes=64)
             nc.vector.tensor_copy(
-                parted[:].bitcast(U16).rearrange("p (o n) -> p o n", o=PASSES),
-                both[:].bitcast(U16).rearrange("p (n o) -> p o n", o=PASSES),
+                parted[:].bitcast(U16).rearrange("p (o h n) -> p h o n", o=PASSES, h=2),
+                both[:].bitcast(U16).rearrange("p (h n o) -> p h o n", o=PASSES, h=2),
             )
             return parted
 

@@ -28,43 +28,38 @@ MASKED = 30000.0
 STEEP = 2.0 ** 80
 NUDGE = 2.0 ** -22
 FLOOR = 2.0 ** 40
-Q_BYTES = 4 * PASSES * NQ
-V_AT = Q_BYTES
-LATE_Q_AT = V_AT + 4 * SEG
-MID_AT = LATE_Q_AT + Q_BYTES
-THIRD_AT = MID_AT + 4 * SEG + 6 * N
-POS_AT = MID_AT
-LAST_AT = THIRD_AT + 4 * T
-VS_AT = LAST_AT + 4 * T
-WIDE = DV * PACK + QT * N
+KB = 1024
 
 
 def tile_attend_soft_draft_segb2q256n512t2048_kernel(tc, q_words, q_scales, k_words, k_scales, vT, vs, pos, qpos, offs, out):
     nc = tc.nc
     with ExitStack() as ctx:
         keep = ctx.enter_context(tc.tile_pool(name="keep", bufs=1))
-        values = ctx.enter_context(tc.tile_pool(name="values", bufs=1))
-        held = ctx.enter_context(tc.tile_pool(name="held", bufs=1))
+        early_v = ctx.enter_context(tc.tile_pool(name="early_v", bufs=1))
+        late_v = [ctx.enter_context(tc.tile_pool(name=f"late_v{h}", bufs=1)) for h in range(HALVES)]
         keys = ctx.enter_context(tc.tile_pool(name="keys", bufs=1))
-        work = ctx.enter_context(tc.tile_pool(name="work", bufs=2))
+        scales = ctx.enter_context(tc.tile_pool(name="scales", bufs=1))
+        probs = ctx.enter_context(tc.tile_pool(name="probs", bufs=1))
+        held = ctx.enter_context(tc.tile_pool(name="held", bufs=1))
         banks = ctx.enter_context(tc.psum_pool(name="banks", bufs=1))
         rows = ctx.enter_context(tc.tile_pool(name="rows", bufs=B * QT))
 
         offsets = keep.tile([P, B * LIST_COLS], U16, name="offsets")
-        k_pool = values.tile([P, T], I32, name="k_pool", offset=LAST_AT, align_bytes=64)
-        ks_pool = values.tile([P, T], U8, name="ks_pool", offset=LATE_Q_AT - T // 2, align_bytes=64)
-        zeros = values.tile([P, P], F32, name="zeros", offset=0)
+        k_pool = keep.tile([P, T], I32, name="k_pool", align_bytes=64)
+        ks_pool = [early_v.tile([P, (b + 1) * SEG], U8, name=f"ks_pool{b}", offset=4 * KB * b) for b in range(B)]
+        zeros = keep.tile([P, P], F32, name="zeros")
         q_planes = keep.tile([P, B * PASSES * NQ], U8, name="q_planes", align_bytes=64)
-        pos_pool = values.tile([P, T], F32, name="pos_pool", offset=POS_AT)
+        q_codes = keep.tile([P, B * PASSES, NQ], I32, name="q_codes", align_bytes=64)
+        pos_pool = keep.tile([P, T], F32, name="pos_pool")
         q_rows = keep.tile([P, P], F32, name="q_rows")
         q_up = keep.tile([P, B * QT], F32, name="q_up")
         q_down = keep.tile([P, B * QT], F32, name="q_down")
         q_edge = keep.tile([P, B * QT], F32, name="q_edge")
-        ks_got = keep.tile([P, B * N], U8, name="ks_got", align_bytes=64)
-        k_planes = keep.tile([P, PASSES * B * N], U8, name="k_planes", align_bytes=64)
-        pos_got = [keys.tile([P, N], F32, name=f"pos_got{b}", offset=(0, 12 * N)[b]) for b in range(B)]
+        ks_got = [keep.tile([P, N], U8, name=f"ks_got{b}", align_bytes=64) for b in range(B)]
+        k_planes = keep.tile([P, B * PASSES * N], U8, name="k_planes", align_bytes=64)
+        pos_got = [keep.tile([P, N], F32, name="pos_got0"), late_v[1].tile([P, N], F32, name="pos_got1", offset=8 * KB)]
         ident = keep.tile([P, P], F32, name="ident")
-        vs_pool = values.tile([P, T], F32, name="vs_pool", offset=VS_AT)
+        vs_pool = scales.tile([P, T], F32, name="vs_pool", offset=0)
 
         warm = keep.tile([P, 1], F32, name="warm")
         nc.vector.memset(warm[:], 0.0)
@@ -75,24 +70,28 @@ def tile_attend_soft_draft_segb2q256n512t2048_kernel(tc, q_words, q_scales, k_wo
             nc.vector.memset(words[:, 0:cut], 0)
             nc.vector.memset(words[:, cut:], 0)
 
-        nc.gpsimd.memset(pos_pool[0 : P - 1, :], 0.0)
-        clear(q_planes[:].bitcast(I32))
+        for b in range(B):
+            nc.gpsimd.memset(pos_pool[0 : P - 1, b * SEG : (b + 1) * SEG], 0.0)
         clear(zeros[:].bitcast(I32))
-        clear(ks_pool[0:96, :].bitcast(I32))
-        clear(k_planes[:].bitcast(I32))
+        clear(ks_pool[0][0:96, :].bitcast(I32))
+        clear(ks_pool[1][0:96, SEG:T].bitcast(I32))
         clear(q_rows[0 : P - B * QT, :].bitcast(I32))
         nc.gpsimd.affine_select(
             out=ident[:], in_=zeros[:], compare_op=ALU.not_equal, fill=1.0, base=0, pattern=[[-1, P]], channel_multiplier=1,
         )
-        q_codes = [values.tile([P, PASSES, NQ], I32, name="q_codes0", offset=0)]
-        nc.gpsimd.memset(vs_pool[0 : P - 1, :], 0.0)
+        for b in range(B):
+            nc.gpsimd.memset(vs_pool[0 : P - 1, b * SEG : (b + 1) * SEG], 0.0)
 
         k_flat = k_words[0].rearrange("p t r -> p (t r)").bitcast(I32)
         nc.sync.dma_start(offsets[:], offs)
-        nc.sync.dma_start(ks_pool[96:P, :].bitcast(I32), k_scales.rearrange("o f t -> f o t").bitcast(I32))
+        for b in range(B):
+            nc.sync.dma_start(
+                ks_pool[b][96:P, b * SEG : (b + 1) * SEG].bitcast(I32),
+                k_scales[:, :, b * SEG : (b + 1) * SEG].rearrange("o f t -> f o t").bitcast(I32),
+            )
         nc.sync.dma_start(pos_pool[P - 1 : P, :], pos[0:1, :])
-        nc.sync.dma_start(vs_pool[P - 1 : P, :], vs[0:1, :])
         nc.sync.dma_start(k_pool[:, 0:SEG], k_flat[:, 0:SEG])
+        nc.sync.dma_start(vs_pool[P - 1 : P, :], vs[0:1, :])
         nc.sync.dma_start(q_rows[P - B * QT : P, :], qpos.rearrange("b (j p) o -> (b j) (p o)", p=P))
         for quad in range(4):
             nc.sync.dma_start(
@@ -100,25 +99,32 @@ def tile_attend_soft_draft_segb2q256n512t2048_kernel(tc, q_words, q_scales, k_wo
                 q_scales[:, :, 4 * quad : 4 * quad + 4, :].rearrange("b o j q -> j (b o) q").bitcast(I32),
             )
         nc.sync.dma_start(k_pool[:, SEG:T], k_flat[:, SEG:T])
-        nc.sync.dma_start(q_codes[0][:], q_words[0].rearrange("o p q r -> p o (q r)").bitcast(I32))
-        nc.vector.tensor_copy(ks_got[:], ks_pool[:].indirect(offsets[:]))
-        for quad in range(4):
-            nc.sync.dma_start(k_planes[32 * quad : 32 * quad + 4, :].bitcast(I32), ks_got[96 + 8 * quad : 96 + 8 * quad + 8, :].bitcast(I32))
-        v_first = values.tile([P, SEG], F32, name="v_first", offset=V_AT)
-        nc.sync.dma_start(v_first[:], vT[0:P, 0:SEG])
-        q_codes.append(values.tile([P, PASSES, NQ], I32, name="q_codes1", offset=LATE_Q_AT))
-        nc.sync.dma_start(q_codes[1][:], q_words[1].rearrange("o p q r -> p o (q r)").bitcast(I32))
+        nc.sync.dma_start(q_codes[:], q_words.rearrange("b o p q r -> p (b o) (q r)").bitcast(I32))
 
         def listed(b):
             return offsets[:, b * LIST_COLS : (b + 1) * LIST_COLS]
 
+        v_pool = {}
+        for b in range(B):
+            nc.vector.tensor_copy(ks_got[b][:], ks_pool[b][:].indirect(listed(b)))
+            for quad in range(4):
+                nc.sync.dma_start(
+                    k_planes[32 * quad : 32 * quad + 4, b * PASSES * N : (b + 1) * PASSES * N].bitcast(I32),
+                    ks_got[b][96 + 8 * quad : 96 + 8 * quad + 8, :].bitcast(I32),
+                )
+            v_pool[0, b] = early_v.tile([P, SEG], F32, name=f"v_early{b}", offset=4 * KB * b)
+            nc.sync.dma_start(v_pool[0, b][:], vT[b * P : (b + 1) * P, 0:SEG])
+
         def gather_keys(b):
-            both = keys.tile([P, N], U32, name=f"k_both{b}", offset=(0, 14 * N)[b])
+            both = late_v[b].tile([P, N], U32, name=f"k_both{b}", offset=7 * KB)
             nc.vector.tensor_copy(both[:], k_pool[:, 0 : (b + 1) * SEG].bitcast(U32).indirect(listed(b)))
             return both
 
         def part_keys(b, both):
-            parted = keys.tile([P, PASSES * 2 * N], U8, name=f"k_parted{b}", offset=(10 * N, 4 * N)[b], align_bytes=64)
+            if b == 0:
+                parted = late_v[1].tile([P, PASSES * 2 * N], U8, name="k_parted0", offset=9 * KB, align_bytes=64)
+            else:
+                parted = keep.tile([P, PASSES * 2 * N], U8, name="k_parted1", align_bytes=64)
             nc.vector.tensor_copy(
                 parted[:].bitcast(U16).rearrange("p (o h n) -> p h o n", o=PASSES, h=2),
                 both[:].bitcast(U16).rearrange("p (h n o) -> p h o n", o=PASSES, h=2),
@@ -132,31 +138,31 @@ def tile_attend_soft_draft_segb2q256n512t2048_kernel(tc, q_words, q_scales, k_wo
                 nc.tensor.transpose(turned[:, 2 * c : 2 * c + P], sources[c], ident[:])
             nc.vector.tensor_scalar(cols, turned[:, P - 1 : P - 1 + 2 * count : 2], factor, FLOOR, ALU.mult, ALU.add)
 
-        def place_row(b, cols, at):
-            spread = banks.tile([P, PACK, P], F32, name="pos_spread", tag=("bank1", "bank3")[b])
+        def place_row(b, cols):
+            spread = banks.tile([P, PACK, P], F32, name="pos_spread", tag=("bank3", "bank4")[b])
             for c in range(PACK):
                 nc.tensor.transpose(spread[:, c, :], cols[:, c : c + 1].to_broadcast([P, P]), ident[:])
-            row = values.tile([P, N], F32, name=f"pos_row{b}", offset=at)
+            row = scales.tile([P, N], F32, name=f"pos_row{b}", offset=2 * KB * b)
             nc.scalar.copy(row[:].rearrange("p (t s) -> p t s", t=PACK), spread[:].rearrange("p c (s t) -> p t (c s)", t=PACK))
             return row
 
         def scores(b, j, parted):
-            bank = banks.tile([P, N], F32, name="scores", tag=f"bank{b * QT + j}")
+            bank = banks.tile([P, N], F32, name="scores", tag=("bank1", "bank0", "bank5", "bank6")[b * QT + j])
             for o in range(PASSES):
-                first = (b * PASSES + o) * NQ + j * P
+                g = b * PASSES + o
                 nc.tensor.matmul_mx(
                     out=bank[:],
-                    lhsT=q_codes[b][:, o, j * P : (j + 1) * P].bitcast(FP8X4),
-                    lhsT_scale=q_planes[:, first : first + P],
+                    lhsT=q_codes[:, g, j * P : (j + 1) * P].bitcast(FP8X4),
+                    lhsT_scale=q_planes[:, g * NQ + j * P : g * NQ + (j + 1) * P],
                     rhs=parted[:, o * 2 * N : (o + 1) * 2 * N].bitcast(FP4X4),
-                    rhs_scale=k_planes[:, (o * B + b) * N : (o * B + b + 1) * N],
+                    rhs_scale=k_planes[:, g * N : (g + 1) * N],
                     start=(o == 0),
                     stop=(o == PASSES - 1),
                 )
             return bank
 
         def mask(u, bank, pos_row):
-            masked = held.tile([P, N], F32, name=f"masked{u}", offset=4 * N * (3 - u))
+            masked = held.tile([P, N], F32, name=f"masked{u}", offset=2 * KB * u)
             nc.vector.scalar_tensor_tensor(
                 masked[:].rearrange("p (t s) -> p t s", t=PACK), pos_row[:].rearrange("p (t s) -> p t s", t=PACK),
                 q_edge[:, u : u + 1], bank[:].rearrange("p (s t) -> p t s", t=PACK), ALU.add, ALU.min,
@@ -164,7 +170,7 @@ def tile_attend_soft_draft_segb2q256n512t2048_kernel(tc, q_words, q_scales, k_wo
             return masked
 
         def row_top(u, masked):
-            capped = keys.tile([P, N], F32, name=f"capped{u}", offset=30 * N + 4 * N * u)
+            capped = keys.tile([P, N], F32, name=f"capped{u}", offset=2 * KB * u)
             top = rows.tile([P, 1], F32, name="top")
             nc.vector.tensor_scalar(capped[:], masked[:], -MASKED, None, ALU.max, ALU.max, accum_out=top[:])
             return capped, top
@@ -172,53 +178,48 @@ def tile_attend_soft_draft_segb2q256n512t2048_kernel(tc, q_words, q_scales, k_wo
         def softmax(u, capped, top, total):
             shift = rows.tile([P, 1], F32, name="shift")
             nc.gpsimd.tensor_scalar(shift[:], top[:], -1.0, 0.0, ALU.mult, ALU.add)
-            p = values.tile([P, N], F32, name=f"p{u}", offset=(MID_AT, MID_AT + 6 * N, MID_AT + 10 * N, THIRD_AT)[u])
+            p = probs.tile([P, N], F32, name=f"p{u}", offset=2 * KB * u)
             nc.scalar.activation(p[:], capped[:], ACT.Exp, bias=shift[:], accum_out=total)
-            turned = banks.tile([P, PACK, P], F32, name="p_turned", tag=f"side{u}")
+            turned = banks.tile([P, PACK, P], F32, name="p_turned", tag=("bank2", "bank3", "bank4", "bank7")[u])
             for t in range(PACK):
                 nc.tensor.transpose(turned[:, t, :], p[:, t * P : (t + 1) * P], ident[:])
             return turned
 
         def gather_values(b, h, got, turned):
             nc.scalar.activation(got, v_pool[b, h][:].indirect(listed(b)), ACT.Copy)
-            turn_values(h, got, turned)
-
-        def turn_values(h, got, turned):
             pairs = got.bitcast(F32)
             for u in range(2):
                 nc.tensor.transpose(turned[:, h, u, :], pairs[:, u : N // 2 : 2], ident[:])
 
-        codes = [keep.tile([P, WIDE // PACK], U32, name=f"codes{b}", align_bytes=64) for b in range(B)]
-        plane = [keep.tile([P, WIDE // PACK], U8, name=f"plane{b}", align_bytes=64) for b in range(B)]
-
         def group_values(target, turned, copy):
             copy(
-                target[:, 0 : DV * PACK].bitcast(F32).rearrange("p (h c u) -> p h c u", h=HALVES, u=2),
+                target[:].bitcast(F32).rearrange("p (h c u) -> p h c u", h=HALVES, u=2),
                 turned[:].rearrange("p h u c -> p h c u"),
             )
 
-        def weights(b, j, turned):
-            first = DV * PACK + j * N
+        def weights(target, b, turned):
             nc.vector.tensor_tensor(
-                grouped[b][:, first : first + N].rearrange("p (q t) -> p q t", t=PACK), turned[:].rearrange("p t q -> p q t"),
+                target.rearrange("p (q t) -> p q t", t=PACK), turned[:].rearrange("p t q -> p q t"),
                 vs_cols[b][:].unsqueeze(1).to_broadcast([P, P, PACK]), ALU.mult,
             )
 
-        def quantise(b, source, first, end):
-            words = slice(first // PACK, end // PACK)
-            nc.vector.quantize_mx(out=codes[b][:, words].bitcast(FP8X4), scales=plane[b][:, words], in_=source[:, first:end])
+        def quantise(name, source):
+            words = source.shape[1] // PACK
+            codes = keep.tile([P, words], U32, name=f"{name}_codes", align_bytes=64)
+            plane = keep.tile([P, words], U8, name=f"{name}_plane", align_bytes=64)
+            nc.vector.quantize_mx(out=codes[:].bitcast(FP8X4), scales=plane[:], in_=source)
+            return codes, plane
 
-        def product(b, j, sums):
-            words = slice(DV + j * P, DV + (j + 1) * P)
+        def product(sums, w, first, v):
             nc.tensor.matmul_mx(
-                out=sums, lhsT=codes[b][:, words].bitcast(FP8X4), lhsT_scale=plane[b][:, words],
-                rhs=codes[b][:, 0:DV].bitcast(FP8X4), rhs_scale=plane[b][:, 0:DV], start=True, stop=True,
+                out=sums, lhsT=w[0][:, first : first + P].bitcast(FP8X4), lhsT_scale=w[1][:, first : first + P],
+                rhs=v[0][:].bitcast(FP8X4), rhs_scale=v[1][:], start=True, stop=True,
             )
             return sums
 
         def finish(u, sums):
             b, j = tiles[u]
-            result = keys.tile([P, DV], F32, name=f"result{u}", offset=(38 * N, 40 * N, 14 * N, 16 * N)[u])
+            result = keep.tile([P, DV], F32, name=f"result{u}")
             if u + 1 == len(tiles):
                 nc.vector.tensor_scalar(result[:], sums, inverse[:, u : u + 1], None, ALU.mult)
             else:
@@ -226,83 +227,73 @@ def tile_attend_soft_draft_segb2q256n512t2048_kernel(tc, q_words, q_scales, k_wo
             nc.sync.dma_start(out[b, j * P : (j + 1) * P, :], result[:])
 
         tiles = [(b, j) for b in range(B) for j in range(QT)]
-        vs_cols = [keep.tile([P, PACK], F32, name=f"vs_cols{b}") for b in range(B)]
-        vs_got = keep.tile([P, B * N], F32, name="vs_got")
-        q_turned = banks.tile([P, P], F32, name="q_turned", tag="side0")
+        vs_got = [probs.tile([P, N], F32, name=f"vs_got{b}", offset=KB + 4 * KB * b) for b in range(B)]
+        nc.scalar.activation(pos_got[0][:], pos_pool[:, 0:SEG].indirect(listed(0)), ACT.Copy)
+        nc.scalar.activation(pos_got[1][:], pos_pool[:].indirect(listed(1)), ACT.Copy)
+        q_turned = banks.tile([P, P], F32, name="q_turned", tag="bank2")
         nc.tensor.transpose(q_turned[:], q_rows[:], ident[:])
         nc.scalar.activation(q_up[:], q_turned[:, P - B * QT : P], ACT.Copy, scale=STEEP)
         nc.scalar.activation(q_down[:], q_turned[:, P - B * QT : P], ACT.Abs, scale=STEEP * NUDGE)
         nc.gpsimd.tensor_tensor(q_edge[:], q_up[:], q_down[:], ALU.add)
-        for b in range(B):
-            nc.scalar.activation(pos_got[b][:], pos_pool[:].indirect(listed(b)), ACT.Copy)
-        v_second = values.tile([P, SEG], F32, name="v_second", offset=MID_AT)
-        nc.sync.dma_start(v_second[:], vT[P : 2 * P, 0:SEG])
-        v_third = values.tile([P, T], F32, name="v_third", offset=THIRD_AT)
-        nc.sync.dma_start(v_third[:, SEG:T], vT[0:P, SEG:T])
-        nc.gpsimd.memset(v_third[:, 0:SEG], 0.0)
-        pos_cols = [keep.tile([P, PACK], F32, name="pos_cols0")]
+        nc.scalar.activation(vs_got[0][:], vs_pool[:, 0:SEG].indirect(listed(0)), ACT.Copy)
+        nc.scalar.activation(vs_got[1][:], vs_pool[:].indirect(listed(1)), ACT.Copy)
+        pos_cols = [keep.tile([P, PACK], F32, name=f"pos_cols{b}") for b in range(B)]
         columns([pos_got[0][:, c * P : (c + 1) * P] for c in range(PACK)], pos_cols[0][:], "bank0", -STEEP)
-        nc.scalar.activation(vs_got[:], vs_pool[:].indirect(offsets[:]), ACT.Copy)
-        for b in range(B):
-            nc.sync.dma_start(vs_cols[b][:], vs_got[P - 1 : P, b * N : (b + 1) * N])
         both = [gather_keys(0)]
-        pos_cols.append(keep.tile([P, PACK], F32, name="pos_cols1"))
-        columns([pos_got[1][:, c * P : (c + 1) * P] for c in range(PACK)], pos_cols[1][:], "bank2", -STEEP)
-        pos_row = [place_row(0, pos_cols[0], VS_AT + 64)]
-        got = [values.tile([P, N], BF16, name=f"got{h}", offset=VS_AT + 6 * SEG + 2 * N * h) for h in range(HALVES)]
-        pos_row.append(place_row(1, pos_cols[1], VS_AT + 64 + 4 * N))
-        nc.scalar.activation(got[0][:], v_first[:].indirect(listed(0)), ACT.Copy)
+        columns([pos_got[1][:, c * P : (c + 1) * P] for c in range(PACK)], pos_cols[1][:], "bank1", -STEEP)
+        pos_row = [place_row(b, pos_cols[b]) for b in range(B)]
         parted = [part_keys(0, both[0])]
         both.append(gather_keys(1))
         parted.append(part_keys(1, both[1]))
-        v_last = keys.tile([P, T], F32, name="v_last", offset=14 * N)
-        nc.gpsimd.memset(v_last[:, 0:SEG], 0.0)
-        nc.sync.dma_start(v_last[:, SEG:T], vT[P : 2 * P, SEG:T])
-        v_pool = {(0, 0): v_first, (0, 1): v_second, (1, 0): v_third, (1, 1): v_last}
+        vs_cols = []
+        for h in range(HALVES):
+            v_pool[1, h] = late_v[h].tile([P, T], F32, name=f"v_late{h}", offset=0)
+            nc.sync.dma_start(v_pool[1, h][:, SEG:T], vT[h * P : (h + 1) * P, SEG:T])
+            vs_cols.append(late_v[h].tile([P, PACK], F32, name=f"vs_cols{h}", offset=8 * KB))
+            nc.sync.dma_start(vs_cols[h][:], vs_got[h][P - 1 : P, :])
         score = [scores(b, j, parted[b]) for b, j in tiles]
 
         total = keep.tile([P, B * QT], F32, name="total")
         inverse = keep.tile([P, B * QT], F32, name="inverse")
-        sums = []
         masked = [mask(0, score[0], pos_row[0])]
         tops = []
         for u in range(len(tiles)):
             if u + 1 < len(tiles):
                 masked.append(mask(u + 1, score[u + 1], pos_row[tiles[u + 1][0]]))
             tops.append(row_top(u, masked[u]))
-        v_turned = [banks.tile([P, HALVES, 2, P], F32, name="v_turned", tag=f"bank{b}") for b in range(B)]
-
-        grouped = [held.tile([P, WIDE], BF16, name=f"grouped{b}", offset=2 * WIDE * b, align_bytes=64) for b in range(B)]
+        v_turned = [banks.tile([P, HALVES, 2, P], F32, name="v_turned", tag=("bank5", "bank0")[b]) for b in range(B)]
 
         def exp_of(u):
             return softmax(u, *tops[u], total[:, u : u + 1])
 
-        def weights_of(u):
-            weights(*tiles[u], p_turned[u])
-
-        turn_values(0, got[0][:], v_turned[0])
-        gather_values(0, 1, got[1][:], v_turned[0])
+        for h in range(HALVES):
+            gather_values(0, h, scales.tile([P, N], BF16, name=f"got0{h}", offset=4 * KB + KB * h)[:], v_turned[0])
+        gather_values(1, 0, keep.tile([P, N], BF16, name="got10")[:], v_turned[1])
         p_turned = [exp_of(0), exp_of(1)]
-        gather_values(1, 0, keys.tile([P, N], BF16, name="got_third", offset=30 * N)[:], v_turned[1])
+        gather_values(1, 1, keys.tile([P, N], BF16, name="got11", offset=0)[:], v_turned[1])
         p_turned.append(exp_of(2))
         p_turned.append(exp_of(3))
-        gather_values(1, 1, keys.tile([P, N], BF16, name="got_last", offset=39 * N)[:], v_turned[1])
-        late_values = keep.tile([P, DV * PACK], BF16, name="late_values", align_bytes=64)
-        group_values(late_values, v_turned[1], nc.scalar.copy)
-        group_values(grouped[0], v_turned[0], nc.vector.tensor_copy)
+        v_grouped = [
+            held.tile([P, DV * PACK], BF16, name="v_grouped0", offset=4 * KB, align_bytes=64),
+            keys.tile([P, DV * PACK], BF16, name="v_grouped1", offset=4 * KB, align_bytes=64),
+        ]
+        group_values(v_grouped[1], v_turned[1], nc.scalar.copy)
+        group_values(v_grouped[0], v_turned[0], nc.vector.tensor_copy)
 
-        for u in range(QT):
-            weights_of(u)
-        quantise(0, grouped[0], 0, WIDE)
+        w_first = [keep.tile([P, N], BF16, name=f"w_first{j}", align_bytes=64) for j in range(QT)]
+        w_last = keep.tile([P, QT * N], BF16, name="w_last", align_bytes=64)
+        weights(w_first[0][:], 0, p_turned[0])
+        v_first = quantise("v0", v_grouped[0][:])
+        weights(w_first[1][:], 0, p_turned[1])
+        w_codes = [quantise(f"w{j}", w_first[j][:]) for j in range(QT)]
         nc.vector.reciprocal(inverse[:], total[:])
-        weights_of(2)
-        early = banks.tile([P, QT, DV], F32, name="early", tag="bank2")
         for j in range(QT):
-            sums.append(product(0, j, early[:, j, :]))
-        weights_of(3)
-        quantise(1, late_values, 0, DV * PACK)
-        quantise(1, grouped[1], DV * PACK, WIDE)
+            weights(w_last[:, j * N : (j + 1) * N], 1, p_turned[QT + j])
+        early = banks.tile([P, QT, DV], F32, name="early", tag="bank4")
+        sums = [product(early[:, j, :], w_codes[j], 0, v_first) for j in range(QT)]
+        v_last = quantise("v1", v_grouped[1][:])
+        w_both = quantise("w23", w_last[:])
         for j in range(QT):
-            sums.append(product(1, j, banks.tile([P, DV], F32, name="sums", tag=f"side{j}")[:]))
+            sums.append(product(banks.tile([P, DV], F32, name="sums", tag=("bank6", "bank2")[j])[:], w_both, j * P, v_last))
         for u in range(len(tiles)):
             finish(u, sums[u])

@@ -29,16 +29,16 @@ STEEP = 2.0 ** 80
 NUDGE = 2.0 ** -22
 FLOOR = 2.0 ** 40
 KB = 1024
+VS_SHARE = 512
 
 
 def tile_attend_soft_draft_segb2q256n512t2048_kernel(tc, q_words, q_scales, k_words, k_scales, vT, vs, pos, qpos, offs, out):
     nc = tc.nc
     with ExitStack() as ctx:
         keep = ctx.enter_context(tc.tile_pool(name="keep", bufs=1))
-        early_v = ctx.enter_context(tc.tile_pool(name="early_v", bufs=1))
+        early_v = [ctx.enter_context(tc.tile_pool(name=f"early_v{h}", bufs=1)) for h in range(HALVES)]
         late_v = [ctx.enter_context(tc.tile_pool(name=f"late_v{h}", bufs=1)) for h in range(HALVES)]
         keys = ctx.enter_context(tc.tile_pool(name="keys", bufs=1))
-        scales = ctx.enter_context(tc.tile_pool(name="scales", bufs=1))
         probs = ctx.enter_context(tc.tile_pool(name="probs", bufs=1))
         held = ctx.enter_context(tc.tile_pool(name="held", bufs=1))
         banks = ctx.enter_context(tc.psum_pool(name="banks", bufs=1))
@@ -46,20 +46,18 @@ def tile_attend_soft_draft_segb2q256n512t2048_kernel(tc, q_words, q_scales, k_wo
 
         offsets = keep.tile([P, B * LIST_COLS], U16, name="offsets")
         k_pool = keep.tile([P, T], I32, name="k_pool", align_bytes=64)
-        ks_pool = [early_v.tile([P, (b + 1) * SEG], U8, name=f"ks_pool{b}", offset=4 * KB * b) for b in range(B)]
+        ks_pool = early_v[0].tile([P, T], U8, name="ks_pool", offset=3 * KB)
         zeros = keep.tile([P, P], F32, name="zeros")
         q_planes = keep.tile([P, B * PASSES * NQ], U8, name="q_planes", align_bytes=64)
-        q_codes = keep.tile([P, B * PASSES, NQ], I32, name="q_codes", align_bytes=64)
         pos_pool = keep.tile([P, T], F32, name="pos_pool")
-        q_rows = keep.tile([P, P], F32, name="q_rows")
-        q_up = keep.tile([P, B * QT], F32, name="q_up")
+        q_rows = probs.tile([P, P], F32, name="q_rows", offset=4 * KB)
         q_down = keep.tile([P, B * QT], F32, name="q_down")
         q_edge = keep.tile([P, B * QT], F32, name="q_edge")
         ks_got = [keep.tile([P, N], U8, name=f"ks_got{b}", align_bytes=64) for b in range(B)]
-        k_planes = keep.tile([P, B * PASSES * N], U8, name="k_planes", align_bytes=64)
-        pos_got = [keep.tile([P, N], F32, name="pos_got0"), late_v[1].tile([P, N], F32, name="pos_got1", offset=8 * KB)]
+        k_planes = [keep.tile([P, PASSES * N], U8, name=f"k_planes{b}", align_bytes=64) for b in range(B)]
+        pos_got = [probs.tile([P, N], F32, name="pos_got0", offset=2 * KB), late_v[0].tile([P, N], F32, name="pos_got1", offset=8 * KB)]
         ident = keep.tile([P, P], F32, name="ident")
-        vs_pool = scales.tile([P, T], F32, name="vs_pool", offset=0)
+        vs_pool = keep.tile([P, T], F32, name="vs_pool")
 
         warm = keep.tile([P, 1], F32, name="warm")
         nc.vector.memset(warm[:], 0.0)
@@ -72,57 +70,60 @@ def tile_attend_soft_draft_segb2q256n512t2048_kernel(tc, q_words, q_scales, k_wo
 
         for b in range(B):
             nc.gpsimd.memset(pos_pool[0 : P - 1, b * SEG : (b + 1) * SEG], 0.0)
+        clear(q_rows[:].bitcast(I32))
         clear(zeros[:].bitcast(I32))
-        clear(ks_pool[0][0:96, :].bitcast(I32))
-        clear(ks_pool[1][0:96, SEG:T].bitcast(I32))
-        clear(q_rows[0 : P - B * QT, :].bitcast(I32))
+        clear(ks_pool[0:96, :].bitcast(I32))
+        clear(vs_pool[0 : P - 1, 0:VS_SHARE].bitcast(I32))
+        nc.gpsimd.memset(vs_pool[0 : P - 1, VS_SHARE:SEG], 0.0)
         nc.gpsimd.affine_select(
             out=ident[:], in_=zeros[:], compare_op=ALU.not_equal, fill=1.0, base=0, pattern=[[-1, P]], channel_multiplier=1,
         )
-        for b in range(B):
-            nc.gpsimd.memset(vs_pool[0 : P - 1, b * SEG : (b + 1) * SEG], 0.0)
+        nc.gpsimd.memset(vs_pool[0 : P - 1, SEG:T], 0.0)
 
-        k_flat = k_words[0].rearrange("p t r -> p (t r)").bitcast(I32)
-        nc.sync.dma_start(offsets[:], offs)
-        for b in range(B):
-            nc.sync.dma_start(
-                ks_pool[b][96:P, b * SEG : (b + 1) * SEG].bitcast(I32),
-                k_scales[:, :, b * SEG : (b + 1) * SEG].rearrange("o f t -> f o t").bitcast(I32),
-            )
-        nc.sync.dma_start(pos_pool[P - 1 : P, :], pos[0:1, :])
-        nc.sync.dma_start(k_pool[:, 0:SEG], k_flat[:, 0:SEG])
-        nc.sync.dma_start(vs_pool[P - 1 : P, :], vs[0:1, :])
-        nc.sync.dma_start(q_rows[P - B * QT : P, :], qpos.rearrange("b (j p) o -> (b j) (p o)", p=P))
-        for quad in range(4):
+        def load_query_scales(quad):
             nc.sync.dma_start(
                 q_planes[32 * quad : 32 * quad + 4, :].bitcast(I32).rearrange("j (g q) -> j g q", g=B * PASSES),
                 q_scales[:, :, 4 * quad : 4 * quad + 4, :].rearrange("b o j q -> j (b o) q").bitcast(I32),
             )
+
+        def load_queries(b, codes):
+            nc.sync.dma_start(codes[:], q_words[b].rearrange("o p q r -> p o (q r)").bitcast(I32))
+            return codes
+
+        k_flat = k_words[0].rearrange("p t r -> p (t r)").bitcast(I32)
+        nc.sync.dma_start(offsets[:], offs)
+        nc.sync.dma_start(ks_pool[96:P, :].bitcast(I32), k_scales.rearrange("o f t -> f o t").bitcast(I32))
+        nc.sync.dma_start(pos_pool[P - 1 : P, :], pos[0:1, :])
+        nc.sync.dma_start(k_pool[:, 0:SEG], k_flat[:, 0:SEG])
+        nc.sync.dma_start(vs_pool[P - 1 : P, :], vs[0:1, :])
+        nc.sync.dma_start(q_rows[P - 2 * B * QT + 1 : P : 2, :], qpos.rearrange("b (j p) o -> (b j) (p o)", p=P))
+        for quad in range(3):
+            load_query_scales(quad)
         nc.sync.dma_start(k_pool[:, SEG:T], k_flat[:, SEG:T])
-        nc.sync.dma_start(q_codes[:], q_words.rearrange("b o p q r -> p (b o) (q r)").bitcast(I32))
+        load_query_scales(3)
+        q_codes = [load_queries(0, keep.tile([P, PASSES, NQ], I32, name="q_codes0", align_bytes=64))]
 
         def listed(b):
             return offsets[:, b * LIST_COLS : (b + 1) * LIST_COLS]
 
-        v_pool = {}
-        for b in range(B):
-            nc.vector.tensor_copy(ks_got[b][:], ks_pool[b][:].indirect(listed(b)))
+        def gather_key_scales(b):
+            nc.vector.tensor_copy(ks_got[b][:], ks_pool[:, 0 : (b + 1) * SEG].indirect(listed(b)))
+
+        def move_key_scales(b):
             for quad in range(4):
                 nc.sync.dma_start(
-                    k_planes[32 * quad : 32 * quad + 4, b * PASSES * N : (b + 1) * PASSES * N].bitcast(I32),
+                    k_planes[b][32 * quad : 32 * quad + 4, :].bitcast(I32),
                     ks_got[b][96 + 8 * quad : 96 + 8 * quad + 8, :].bitcast(I32),
                 )
-            v_pool[0, b] = early_v.tile([P, SEG], F32, name=f"v_early{b}", offset=4 * KB * b)
-            nc.sync.dma_start(v_pool[0, b][:], vT[b * P : (b + 1) * P, 0:SEG])
 
         def gather_keys(b):
-            both = late_v[b].tile([P, N], U32, name=f"k_both{b}", offset=7 * KB)
+            both = (early_v[1], late_v[0])[b].tile([P, N], U32, name=f"k_both{b}", offset=7 * KB)
             nc.vector.tensor_copy(both[:], k_pool[:, 0 : (b + 1) * SEG].bitcast(U32).indirect(listed(b)))
             return both
 
         def part_keys(b, both):
             if b == 0:
-                parted = late_v[1].tile([P, PASSES * 2 * N], U8, name="k_parted0", offset=9 * KB, align_bytes=64)
+                parted = late_v[0].tile([P, PASSES * 2 * N], U8, name="k_parted0", offset=9 * KB, align_bytes=64)
             else:
                 parted = keep.tile([P, PASSES * 2 * N], U8, name="k_parted1", align_bytes=64)
             nc.vector.tensor_copy(
@@ -131,38 +132,45 @@ def tile_attend_soft_draft_segb2q256n512t2048_kernel(tc, q_words, q_scales, k_wo
             )
             return parted
 
-        def columns(sources, cols, tag, factor):
+        def turn_columns(sources, last, count, tag):
             turned = banks.tile([P, N], F32, name="cols_turned", tag=tag)
-            count = len(sources)
-            for c in reversed(range(count)):
+            if last is not None:
+                shift = 2 * (count - 1)
+                nc.tensor.transpose(turned[:, shift : shift + P], last, ident[:])
+            for c in reversed(range(len(sources))):
                 nc.tensor.transpose(turned[:, 2 * c : 2 * c + P], sources[c], ident[:])
-            nc.vector.tensor_scalar(cols, turned[:, P - 1 : P - 1 + 2 * count : 2], factor, FLOOR, ALU.mult, ALU.add)
+            return turned
 
-        def place_row(b, cols):
-            spread = banks.tile([P, PACK, P], F32, name="pos_spread", tag=("bank3", "bank4")[b])
+        def copy_columns(cols, turned):
+            nc.vector.tensor_scalar(cols, turned[:, P - 1 : P - 1 + 2 * cols.shape[1] : 2], STEEP, None, ALU.mult)
+
+        def place_row(b, cols, row):
+            spread = banks.tile([P, PACK, P], F32, name="pos_spread", tag=("bank3", "bank7")[b])
             for c in range(PACK):
                 nc.tensor.transpose(spread[:, c, :], cols[:, c : c + 1].to_broadcast([P, P]), ident[:])
-            row = scales.tile([P, N], F32, name=f"pos_row{b}", offset=2 * KB * b)
-            nc.scalar.copy(row[:].rearrange("p (t s) -> p t s", t=PACK), spread[:].rearrange("p c (s t) -> p t (c s)", t=PACK))
+            nc.scalar.activation(
+                row[:].rearrange("p (t s) -> p t s", t=PACK), spread[:].rearrange("p c (s t) -> p t (c s)", t=PACK),
+                ACT.Copy, bias=FLOOR, scale=-1.0,
+            )
             return row
 
         def scores(b, j, parted):
-            bank = banks.tile([P, N], F32, name="scores", tag=("bank1", "bank0", "bank5", "bank6")[b * QT + j])
+            bank = banks.tile([P, N], F32, name="scores", tag=("bank1", "bank0", "bank2", "bank4")[b * QT + j])
             for o in range(PASSES):
                 g = b * PASSES + o
                 nc.tensor.matmul_mx(
                     out=bank[:],
-                    lhsT=q_codes[:, g, j * P : (j + 1) * P].bitcast(FP8X4),
+                    lhsT=q_codes[b][:, o, j * P : (j + 1) * P].bitcast(FP8X4),
                     lhsT_scale=q_planes[:, g * NQ + j * P : g * NQ + (j + 1) * P],
                     rhs=parted[:, o * 2 * N : (o + 1) * 2 * N].bitcast(FP4X4),
-                    rhs_scale=k_planes[:, g * N : (g + 1) * N],
+                    rhs_scale=k_planes[b][:, o * N : (o + 1) * N],
                     start=(o == 0),
                     stop=(o == PASSES - 1),
                 )
             return bank
 
         def mask(u, bank, pos_row):
-            masked = held.tile([P, N], F32, name=f"masked{u}", offset=2 * KB * u)
+            masked = (held if u else late_v[1]).tile([P, N], F32, name=f"masked{u}", offset=2 * KB * u if u else 7 * KB)
             nc.vector.scalar_tensor_tensor(
                 masked[:].rearrange("p (t s) -> p t s", t=PACK), pos_row[:].rearrange("p (t s) -> p t s", t=PACK),
                 q_edge[:, u : u + 1], bank[:].rearrange("p (s t) -> p t s", t=PACK), ALU.add, ALU.min,
@@ -170,32 +178,32 @@ def tile_attend_soft_draft_segb2q256n512t2048_kernel(tc, q_words, q_scales, k_wo
             return masked
 
         def row_top(u, masked):
-            capped = keys.tile([P, N], F32, name=f"capped{u}", offset=2 * KB * u)
-            top = rows.tile([P, 1], F32, name="top")
+            capped = keys.tile([P, N], F32, name=f"capped{u}", offset=32 + (2 * KB + 32) * u)
+            top = keys.tile([P, 1], F32, name=f"top{u}", offset=(2 * KB + 32) * (u - 1) if u == 3 else 10 * KB + 32 * u)
             nc.vector.tensor_scalar(capped[:], masked[:], -MASKED, None, ALU.max, ALU.max, accum_out=top[:])
             return capped, top
 
         def softmax(u, capped, top, total):
             shift = rows.tile([P, 1], F32, name="shift")
             nc.gpsimd.tensor_scalar(shift[:], top[:], -1.0, 0.0, ALU.mult, ALU.add)
-            p = probs.tile([P, N], F32, name=f"p{u}", offset=2 * KB * u)
+            p = probs.tile([P, N], F32, name=f"p{u}", offset=(0, 2 * KB, 6 * KB - 64, 8 * KB)[u])
             nc.scalar.activation(p[:], capped[:], ACT.Exp, bias=shift[:], accum_out=total)
-            turned = banks.tile([P, PACK, P], F32, name="p_turned", tag=("bank2", "bank3", "bank4", "bank7")[u])
+            turned = banks.tile([P, PACK, P], F32, name="p_turned", tag=("bank3", "bank5", "bank6", "bank1")[u])
             for t in range(PACK):
                 nc.tensor.transpose(turned[:, t, :], p[:, t * P : (t + 1) * P], ident[:])
             return turned
 
-        def gather_values(b, h, got, turned):
+        def gather_values(b, h, got):
             nc.scalar.activation(got, v_pool[b, h][:].indirect(listed(b)), ACT.Copy)
+            return got
+
+        def turn_values(got, turned):
             pairs = got.bitcast(F32)
             for u in range(2):
-                nc.tensor.transpose(turned[:, h, u, :], pairs[:, u : N // 2 : 2], ident[:])
+                nc.tensor.transpose(turned[:, u, :], pairs[:, u : N // 2 : 2], ident[:])
 
         def group_values(target, turned, copy):
-            copy(
-                target[:].bitcast(F32).rearrange("p (h c u) -> p h c u", h=HALVES, u=2),
-                turned[:].rearrange("p h u c -> p h c u"),
-            )
+            copy(target.bitcast(F32).rearrange("p (h c u) -> p h c u", c=P, u=2), turned.rearrange("p h u c -> p h c u"))
 
         def weights(target, b, turned):
             nc.vector.tensor_tensor(
@@ -210,90 +218,107 @@ def tile_attend_soft_draft_segb2q256n512t2048_kernel(tc, q_words, q_scales, k_wo
             nc.vector.quantize_mx(out=codes[:].bitcast(FP8X4), scales=plane[:], in_=source)
             return codes, plane
 
-        def product(sums, w, first, v):
+        def product(tag, w, first, v):
+            sums = banks.tile([P, v[1].shape[1]], F32, name="sums", tag=tag)
             nc.tensor.matmul_mx(
-                out=sums, lhsT=w[0][:, first : first + P].bitcast(FP8X4), lhsT_scale=w[1][:, first : first + P],
+                out=sums[:], lhsT=w[0][:, first : first + P].bitcast(FP8X4), lhsT_scale=w[1][:, first : first + P],
                 rhs=v[0][:].bitcast(FP8X4), rhs_scale=v[1][:], start=True, stop=True,
             )
             return sums
 
-        def finish(u, sums):
+        def finish(u, parts):
             b, j = tiles[u]
             result = keep.tile([P, DV], F32, name=f"result{u}")
-            if u + 1 == len(tiles):
-                nc.vector.tensor_scalar(result[:], sums, inverse[:, u : u + 1], None, ALU.mult)
-            else:
-                nc.scalar.activation(result[:], sums, ACT.Copy, scale=inverse[:, u : u + 1])
+            width = DV // len(parts)
+            for h, sums in enumerate(parts):
+                target = result[:, h * width : (h + 1) * width]
+                if u + 1 == len(tiles):
+                    nc.vector.tensor_scalar(target, sums[:], inverse[:, u : u + 1], None, ALU.mult)
+                else:
+                    nc.scalar.activation(target, sums[:], ACT.Copy, scale=inverse[:, u : u + 1])
             nc.sync.dma_start(out[b, j * P : (j + 1) * P, :], result[:])
 
         tiles = [(b, j) for b in range(B) for j in range(QT)]
-        vs_got = [probs.tile([P, N], F32, name=f"vs_got{b}", offset=KB + 4 * KB * b) for b in range(B)]
         nc.scalar.activation(pos_got[0][:], pos_pool[:, 0:SEG].indirect(listed(0)), ACT.Copy)
         nc.scalar.activation(pos_got[1][:], pos_pool[:].indirect(listed(1)), ACT.Copy)
-        q_turned = banks.tile([P, P], F32, name="q_turned", tag="bank2")
-        nc.tensor.transpose(q_turned[:], q_rows[:], ident[:])
-        nc.scalar.activation(q_up[:], q_turned[:, P - B * QT : P], ACT.Copy, scale=STEEP)
-        nc.scalar.activation(q_down[:], q_turned[:, P - B * QT : P], ACT.Abs, scale=STEEP * NUDGE)
-        nc.gpsimd.tensor_tensor(q_edge[:], q_up[:], q_down[:], ALU.add)
-        nc.scalar.activation(vs_got[0][:], vs_pool[:, 0:SEG].indirect(listed(0)), ACT.Copy)
-        nc.scalar.activation(vs_got[1][:], vs_pool[:].indirect(listed(1)), ACT.Copy)
-        pos_cols = [keep.tile([P, PACK], F32, name=f"pos_cols{b}") for b in range(B)]
-        columns([pos_got[0][:, c * P : (c + 1) * P] for c in range(PACK)], pos_cols[0][:], "bank0", -STEEP)
+        gather_key_scales(0)
+        move_key_scales(0)
+        gather_key_scales(1)
+        v_pool = {(0, 0): early_v[0].tile([P, SEG], F32, name="v_early0", offset=0)}
+        nc.sync.dma_start(v_pool[0, 0][:], vT[0:P, 0:SEG])
+        v_pool[0, 1] = early_v[0].tile([P, SEG], F32, name="v_early1", offset=4 * KB)
+        nc.sync.dma_start(v_pool[0, 1][:], vT[P : 2 * P, 0:SEG])
+        move_key_scales(1)
+        first_cols = keep.tile([P, PACK + B * QT], F32, name="first_cols")[:]
+        first_turned = turn_columns([pos_got[0][:, c * P : (c + 1) * P] for c in range(PACK)], q_rows[:], PACK + B * QT, "bank0")
+        nc.scalar.activation(first_cols, first_turned[:, P - 1 : P - 1 + 2 * (PACK + B * QT) : 2], ACT.Copy, scale=STEEP)
+        nc.scalar.activation(q_down[:], first_turned[:, P - 1 + 2 * PACK : P - 1 + 2 * (PACK + B * QT) : 2], ACT.Abs, scale=STEEP * NUDGE)
+        vs_got = probs.tile([P, B * N], F32, name="vs_got", offset=2 * KB - 32)
+        nc.scalar.activation(vs_got[:], vs_pool[:].indirect(offsets[:]), ACT.Copy)
+        second_turned = turn_columns([pos_got[1][:, c * P : (c + 1) * P] for c in range(PACK)], None, PACK, "bank1")
+        nc.gpsimd.tensor_tensor(q_edge[:], first_cols[:, PACK:], q_down[:], ALU.add)
         both = [gather_keys(0)]
-        columns([pos_got[1][:, c * P : (c + 1) * P] for c in range(PACK)], pos_cols[1][:], "bank1", -STEEP)
-        pos_row = [place_row(b, pos_cols[b]) for b in range(B)]
+        second_cols = keys.tile([P, 16], F32, name="second_cols", offset=12 * KB)[:, 0:PACK]
+        copy_columns(second_cols, second_turned)
+        pos_row = [place_row(b, (first_cols, second_cols)[b], keep.tile([P, N], F32, name=f"pos_row{b}")) for b in range(B)]
         parted = [part_keys(0, both[0])]
+        q_codes.append(load_queries(1, early_v[1].tile([P, PASSES, NQ], I32, name="q_codes1", offset=8 * KB + 512, align_bytes=64)))
+        v_pool[1, 0] = early_v[1].tile([P, T], F32, name="v_late0", offset=0)
+        nc.sync.dma_start(v_pool[1, 0][:, SEG:T], vT[0:P, SEG:T])
+        vs_cols = []
+        for b in range(B):
+            vs_cols.append(early_v[1].tile([P, PACK], F32, name=f"vs_cols{b}", offset=8 * KB + 32 * b))
+            nc.sync.dma_start(vs_cols[b][:], vs_got[P - 1 : P, b * N : (b + 1) * N])
         both.append(gather_keys(1))
         parted.append(part_keys(1, both[1]))
-        vs_cols = []
-        for h in range(HALVES):
-            v_pool[1, h] = late_v[h].tile([P, T], F32, name=f"v_late{h}", offset=0)
-            nc.sync.dma_start(v_pool[1, h][:, SEG:T], vT[h * P : (h + 1) * P, SEG:T])
-            vs_cols.append(late_v[h].tile([P, PACK], F32, name=f"vs_cols{h}", offset=8 * KB))
-            nc.sync.dma_start(vs_cols[h][:], vs_got[h][P - 1 : P, :])
-        score = [scores(b, j, parted[b]) for b, j in tiles]
+        got = {(0, h): gather_values(0, h, keys.tile([P, N], BF16, name=f"got0{h}", offset=11 * KB + KB * h + 32)[:]) for h in range(HALVES)}
 
         total = keep.tile([P, B * QT], F32, name="total")
         inverse = keep.tile([P, B * QT], F32, name="inverse")
-        masked = [mask(0, score[0], pos_row[0])]
         tops = []
-        for u in range(len(tiles)):
-            if u + 1 < len(tiles):
-                masked.append(mask(u + 1, score[u + 1], pos_row[tiles[u + 1][0]]))
-            tops.append(row_top(u, masked[u]))
-        v_turned = [banks.tile([P, HALVES, 2, P], F32, name="v_turned", tag=("bank5", "bank0")[b]) for b in range(B)]
+        for b in range(B):
+            score = [scores(b, j, parted[b]) for j in range(QT)]
+            masked = [mask(b * QT + j, score[j], pos_row[b]) for j in range(QT)]
+            tops.extend(row_top(b * QT + j, masked[j]) for j in range(QT))
+            if b == 0:
+                v_pool[1, 1] = late_v[1].tile([P, T], F32, name="v_late1", offset=0)
+                nc.sync.dma_start(v_pool[1, 1][:, SEG:T], vT[P : 2 * P, SEG:T])
 
         def exp_of(u):
             return softmax(u, *tops[u], total[:, u : u + 1])
 
+        v_turned = banks.tile([P, HALVES, 2, P], F32, name="v_turned", tag="bank2")
         for h in range(HALVES):
-            gather_values(0, h, scales.tile([P, N], BF16, name=f"got0{h}", offset=4 * KB + KB * h)[:], v_turned[0])
-        gather_values(1, 0, keep.tile([P, N], BF16, name="got10")[:], v_turned[1])
-        p_turned = [exp_of(0), exp_of(1)]
-        gather_values(1, 1, keys.tile([P, N], BF16, name="got11", offset=0)[:], v_turned[1])
-        p_turned.append(exp_of(2))
-        p_turned.append(exp_of(3))
-        v_grouped = [
-            held.tile([P, DV * PACK], BF16, name="v_grouped0", offset=4 * KB, align_bytes=64),
-            keys.tile([P, DV * PACK], BF16, name="v_grouped1", offset=4 * KB, align_bytes=64),
+            turn_values(got[0, h], v_turned[:, h, :, :])
+        late_turned = [banks.tile([P, 1, 2, P], F32, name="late_turned", tag=("bank4", "bank7")[h]) for h in range(HALVES)]
+        turn_values(gather_values(1, 0, early_v[0].tile([P, N], BF16, name="got10", offset=0)[:]), late_turned[0][:, 0, :, :])
+        p_turned = [exp_of(u) for u in range(B * QT)]
+        turn_values(gather_values(1, 1, keys.tile([P, N], BF16, name="got11", offset=2 * (2 * KB + 32))[:]), late_turned[1][:, 0, :, :])
+        v_grouped = keys.tile([P, DV * PACK], BF16, name="v_grouped", offset=6 * KB + 128, align_bytes=64)
+        group_values(v_grouped[:], v_turned[:], nc.scalar.copy)
+        late_grouped = [
+            late_v[1].tile([P, N], BF16, name="late_grouped0", offset=4 * KB, align_bytes=64),
+            keep.tile([P, N], BF16, name="late_grouped1", align_bytes=64),
         ]
-        group_values(v_grouped[1], v_turned[1], nc.scalar.copy)
-        group_values(v_grouped[0], v_turned[0], nc.vector.tensor_copy)
+        for h in range(HALVES):
+            group_values(late_grouped[h][:], late_turned[h][:], nc.scalar.copy)
 
-        w_first = [keep.tile([P, N], BF16, name=f"w_first{j}", align_bytes=64) for j in range(QT)]
+        w_first = held.tile([P, QT * N], BF16, name="w_first", offset=4 * KB, align_bytes=64)
         w_last = keep.tile([P, QT * N], BF16, name="w_last", align_bytes=64)
-        weights(w_first[0][:], 0, p_turned[0])
-        v_first = quantise("v0", v_grouped[0][:])
-        weights(w_first[1][:], 0, p_turned[1])
-        w_codes = [quantise(f"w{j}", w_first[j][:]) for j in range(QT)]
+        for j in range(QT):
+            weights(w_first[:, j * N : (j + 1) * N], 0, p_turned[j])
+        weights(w_last[:, 0:N], 1, p_turned[QT])
+        w_codes = quantise("w01", w_first[:])
+        weights(w_last[:, N : 2 * N], 1, p_turned[QT + 1])
         nc.vector.reciprocal(inverse[:], total[:])
-        for j in range(QT):
-            weights(w_last[:, j * N : (j + 1) * N], 1, p_turned[QT + j])
-        early = banks.tile([P, QT, DV], F32, name="early", tag="bank4")
-        sums = [product(early[:, j, :], w_codes[j], 0, v_first) for j in range(QT)]
-        v_last = quantise("v1", v_grouped[1][:])
+        v_first = quantise("v0", v_grouped[:])
+        sums = [[product(("bank5", "bank1")[j], w_codes, j * P, v_first)] for j in range(QT)]
+        v_last = [quantise("v10", late_grouped[0][:])]
         w_both = quantise("w23", w_last[:])
-        for j in range(QT):
-            sums.append(product(banks.tile([P, DV], F32, name="sums", tag=("bank6", "bank2")[j])[:], w_both, j * P, v_last))
+        v_last.append(quantise("v11", late_grouped[1][:]))
+        sums.extend([] for j in range(QT))
+        for h in range(HALVES):
+            for j in range(QT):
+                sums[QT + j].append(product((("bank0", "bank3"), ("bank2", "bank6"))[h][j], w_both, j * P, v_last[h]))
         for u in range(len(tiles)):
             finish(u, sums[u])

@@ -46,16 +46,16 @@ def tile_attend_soft_draft_segb2q256n512t2048_kernel(tc, q_words, q_scales, k_wo
 
         offsets = keep.tile([P, B * LIST_COLS], U16, name="offsets")
         k_pool = keep.tile([P, T], I32, name="k_pool", align_bytes=64)
-        ks_pool = early_v[0].tile([P, T], U8, name="ks_pool", offset=3 * KB)
+        ks_pool = early_v[0].tile([P, T], U8, name="ks_pool", offset=0, align_bytes=64)
         zeros = keep.tile([P, P], F32, name="zeros")
         q_planes = keep.tile([P, B * PASSES * NQ], U8, name="q_planes", align_bytes=64)
         pos_pool = keep.tile([P, T], F32, name="pos_pool")
-        q_rows = probs.tile([P, P], F32, name="q_rows", offset=4 * KB)
+        q_rows = early_v[0].tile([P, P], F32, name="q_rows", offset=2 * KB)
         q_down = keep.tile([P, B * QT], F32, name="q_down")
         q_edge = keep.tile([P, B * QT], F32, name="q_edge")
         ks_got = [keep.tile([P, N], U8, name=f"ks_got{b}", align_bytes=64) for b in range(B)]
         k_planes = [keep.tile([P, PASSES * N], U8, name=f"k_planes{b}", align_bytes=64) for b in range(B)]
-        pos_got = [probs.tile([P, N], F32, name="pos_got0", offset=2 * KB), late_v[0].tile([P, N], F32, name="pos_got1", offset=8 * KB)]
+        pos_got = [probs.tile([P, N], F32, name="pos_got0", offset=2 * KB), late_v[0].tile([P, T], F32, name="pos_got1", offset=8 * KB)[:, 0:N]]
         ident = keep.tile([P, P], F32, name="ident")
         vs_pool = keep.tile([P, T], F32, name="vs_pool")
 
@@ -117,13 +117,13 @@ def tile_attend_soft_draft_segb2q256n512t2048_kernel(tc, q_words, q_scales, k_wo
                 )
 
         def gather_keys(b):
-            both = (early_v[1], late_v[0])[b].tile([P, N], U32, name=f"k_both{b}", offset=7 * KB)
+            both = (early_v[1], late_v[0])[b].tile([P, N], U32, name=f"k_both{b}", offset=(7, 9)[b] * KB)
             nc.vector.tensor_copy(both[:], k_pool[:, 0 : (b + 1) * SEG].bitcast(U32).indirect(listed(b)))
             return both
 
         def part_keys(b, both):
             if b == 0:
-                parted = late_v[0].tile([P, PASSES * 2 * N], U8, name="k_parted0", offset=9 * KB, align_bytes=64)
+                parted = late_v[0].tile([P, PASSES * 2 * N], U8, name="k_parted0", offset=11 * KB, align_bytes=64)
             else:
                 parted = keep.tile([P, PASSES * 2 * N], U8, name="k_parted1", align_bytes=64)
             nc.vector.tensor_copy(
@@ -186,9 +186,9 @@ def tile_attend_soft_draft_segb2q256n512t2048_kernel(tc, q_words, q_scales, k_wo
         def softmax(u, capped, top, total):
             shift = rows.tile([P, 1], F32, name="shift")
             nc.gpsimd.tensor_scalar(shift[:], top[:], -1.0, 0.0, ALU.mult, ALU.add)
-            p = probs.tile([P, N], F32, name=f"p{u}", offset=(0, 2 * KB, 6 * KB - 64, 8 * KB)[u])
+            p = probs.tile([P, N], F32, name=f"p{u}", offset=2 * KB * u)
             nc.scalar.activation(p[:], capped[:], ACT.Exp, bias=shift[:], accum_out=total)
-            turned = banks.tile([P, PACK, P], F32, name="p_turned", tag=("bank3", "bank5", "bank6", "bank1")[u])
+            turned = banks.tile([P, PACK, P], F32, name="p_turned", tag=("bank7", "bank5", "bank6", "bank1")[u])
             for t in range(PACK):
                 nc.tensor.transpose(turned[:, t, :], p[:, t * P : (t + 1) * P], ident[:])
             return turned
@@ -240,29 +240,29 @@ def tile_attend_soft_draft_segb2q256n512t2048_kernel(tc, q_words, q_scales, k_wo
 
         tiles = [(b, j) for b in range(B) for j in range(QT)]
         nc.scalar.activation(pos_got[0][:], pos_pool[:, 0:SEG].indirect(listed(0)), ACT.Copy)
-        nc.scalar.activation(pos_got[1][:], pos_pool[:].indirect(listed(1)), ACT.Copy)
+        nc.scalar.activation(pos_got[1], pos_pool[:].indirect(listed(1)), ACT.Copy)
         gather_key_scales(0)
         move_key_scales(0)
-        gather_key_scales(1)
-        v_pool = {(0, 0): early_v[0].tile([P, SEG], F32, name="v_early0", offset=0)}
+        first_turned = turn_columns([pos_got[0][:, c * P : (c + 1) * P] for c in range(PACK)], q_rows[:], PACK + B * QT, "bank0")
+        v_pool = {(0, 0): early_v[0].tile([P, SEG], F32, name="v_early0", offset=2 * KB)}
         nc.sync.dma_start(v_pool[0, 0][:], vT[0:P, 0:SEG])
-        v_pool[0, 1] = early_v[0].tile([P, SEG], F32, name="v_early1", offset=4 * KB)
-        nc.sync.dma_start(v_pool[0, 1][:], vT[P : 2 * P, 0:SEG])
+        gather_key_scales(1)
+        q_codes.append(load_queries(1, early_v[0].tile([P, PASSES, NQ], I32, name="q_codes1", offset=0, align_bytes=64)))
         move_key_scales(1)
         first_cols = keep.tile([P, PACK + B * QT], F32, name="first_cols")[:]
-        first_turned = turn_columns([pos_got[0][:, c * P : (c + 1) * P] for c in range(PACK)], q_rows[:], PACK + B * QT, "bank0")
         nc.scalar.activation(first_cols, first_turned[:, P - 1 : P - 1 + 2 * (PACK + B * QT) : 2], ACT.Copy, scale=STEEP)
         nc.scalar.activation(q_down[:], first_turned[:, P - 1 + 2 * PACK : P - 1 + 2 * (PACK + B * QT) : 2], ACT.Abs, scale=STEEP * NUDGE)
-        vs_got = probs.tile([P, B * N], F32, name="vs_got", offset=2 * KB - 32)
-        nc.scalar.activation(vs_got[:], vs_pool[:].indirect(offsets[:]), ACT.Copy)
+        vs_got = probs.tile([P, T], F32, name="vs_got", offset=2 * KB - 32)[:, 0 : B * N]
+        nc.scalar.activation(vs_got, vs_pool[:].indirect(offsets[:]), ACT.Copy)
         second_turned = turn_columns([pos_got[1][:, c * P : (c + 1) * P] for c in range(PACK)], None, PACK, "bank1")
+        v_pool[0, 1] = late_v[0].tile([P, SEG], F32, name="v_early1", offset=4 * KB + 32)
+        nc.sync.dma_start(v_pool[0, 1][:], vT[P : 2 * P, 0:SEG])
         nc.gpsimd.tensor_tensor(q_edge[:], first_cols[:, PACK:], q_down[:], ALU.add)
         both = [gather_keys(0)]
         second_cols = keys.tile([P, 16], F32, name="second_cols", offset=12 * KB)[:, 0:PACK]
         copy_columns(second_cols, second_turned)
         pos_row = [place_row(b, (first_cols, second_cols)[b], keep.tile([P, N], F32, name=f"pos_row{b}")) for b in range(B)]
         parted = [part_keys(0, both[0])]
-        q_codes.append(load_queries(1, early_v[1].tile([P, PASSES, NQ], I32, name="q_codes1", offset=8 * KB + 512, align_bytes=64)))
         v_pool[1, 0] = early_v[1].tile([P, T], F32, name="v_late0", offset=0)
         nc.sync.dma_start(v_pool[1, 0][:, SEG:T], vT[0:P, SEG:T])
         vs_cols = []
@@ -287,11 +287,11 @@ def tile_attend_soft_draft_segb2q256n512t2048_kernel(tc, q_words, q_scales, k_wo
         def exp_of(u):
             return softmax(u, *tops[u], total[:, u : u + 1])
 
-        v_turned = banks.tile([P, HALVES, 2, P], F32, name="v_turned", tag="bank2")
-        for h in range(HALVES):
+        v_turned = banks.tile([P, HALVES, 2, P], F32, name="v_turned", tag="bank3")
+        for h in reversed(range(HALVES)):
             turn_values(got[0, h], v_turned[:, h, :, :])
-        late_turned = [banks.tile([P, 1, 2, P], F32, name="late_turned", tag=("bank4", "bank7")[h]) for h in range(HALVES)]
-        turn_values(gather_values(1, 0, early_v[0].tile([P, N], BF16, name="got10", offset=0)[:]), late_turned[0][:, 0, :, :])
+        late_turned = [banks.tile([P, 1, 2, P], F32, name="late_turned", tag=("bank2", "bank4")[h]) for h in range(HALVES)]
+        turn_values(gather_values(1, 0, early_v[0].tile([P, N], BF16, name="got10", offset=2 * KB)[:]), late_turned[0][:, 0, :, :])
         p_turned = [exp_of(u) for u in range(B * QT)]
         turn_values(gather_values(1, 1, keys.tile([P, N], BF16, name="got11", offset=2 * (2 * KB + 32))[:]), late_turned[1][:, 0, :, :])
         v_grouped = keys.tile([P, DV * PACK], BF16, name="v_grouped", offset=6 * KB + 128, align_bytes=64)
@@ -319,6 +319,6 @@ def tile_attend_soft_draft_segb2q256n512t2048_kernel(tc, q_words, q_scales, k_wo
         sums.extend([] for j in range(QT))
         for h in range(HALVES):
             for j in range(QT):
-                sums[QT + j].append(product((("bank0", "bank3"), ("bank2", "bank6"))[h][j], w_both, j * P, v_last[h]))
+                sums[QT + j].append(product((("bank0", "bank7"), ("bank3", "bank6"))[h][j], w_both, j * P, v_last[h]))
         for u in range(len(tiles)):
             finish(u, sums[u])

@@ -29,7 +29,7 @@ STEEP = 2.0 ** 80
 NUDGE = 2.0 ** -22
 FLOOR = 2.0 ** 40
 KB = 1024
-VS_SHARE = 512
+VS_SHARE = 1280
 
 
 def tile_attend_soft_draft_segb2q256n512t2048_kernel(tc, q_words, q_scales, k_words, k_scales, vT, vs, pos, qpos, offs, out):
@@ -74,11 +74,10 @@ def tile_attend_soft_draft_segb2q256n512t2048_kernel(tc, q_words, q_scales, k_wo
         clear(zeros[:].bitcast(I32))
         clear(ks_pool[0:96, :].bitcast(I32))
         clear(vs_pool[0 : P - 1, 0:VS_SHARE].bitcast(I32))
-        nc.gpsimd.memset(vs_pool[0 : P - 1, VS_SHARE:SEG], 0.0)
         nc.gpsimd.affine_select(
             out=ident[:], in_=zeros[:], compare_op=ALU.not_equal, fill=1.0, base=0, pattern=[[-1, P]], channel_multiplier=1,
         )
-        nc.gpsimd.memset(vs_pool[0 : P - 1, SEG:T], 0.0)
+        nc.gpsimd.memset(vs_pool[0 : P - 1, VS_SHARE:T], 0.0)
 
         def load_query_scales(quad):
             nc.sync.dma_start(

from contextlib import ExitStack

import concourse.mybir as mybir

B, N, T, D, DV, NQ = 2, 512, 2048, 1024, 256, 256
FLOPS = 2 * B * NQ * N * (D + DV)
BYTES = B * D * NQ + B * D * NQ // 32 + D * T // 2 + D * T // 32 + 4 * DV * T + 2 * 4 * T + 4 * B * NQ + 2 * 128 * 64 + 4 * B * NQ * DV

F32 = mybir.dt.float32
BF16 = mybir.dt.bfloat16
I32 = mybir.dt.int32
U32 = mybir.dt.uint32
U16 = mybir.dt.uint16
U8 = mybir.dt.uint8
FP8X4 = mybir.dt.float8_e4m3fn_x4
FP4X4 = mybir.dt.float4_e2m1fn_x4
ALU = mybir.AluOpType
ACT = mybir.ActivationFunctionType

P = 128
PACK = 4
PASSES = D // (P * PACK)
SEG = T // B
QT = NQ // P
HALVES = DV // P
LIST_COLS = N // 16
MASKED = 30000.0
STEEP = 2.0 ** 80
NUDGE = 2.0 ** -22
FLOOR = 2.0 ** 40
KB = 1024
VS_SHARE = 1280


def tile_attend_soft_draft_segb2q256n512t2048_kernel(tc, q_words, q_scales, k_words, k_scales, vT, vs, pos, qpos, offs, out):
    nc = tc.nc
    with ExitStack() as ctx:
        keep = ctx.enter_context(tc.tile_pool(name="keep", bufs=1))
        early_v = [ctx.enter_context(tc.tile_pool(name=f"early_v{h}", bufs=1)) for h in range(HALVES)]
        late_v = [ctx.enter_context(tc.tile_pool(name=f"late_v{h}", bufs=1)) for h in range(HALVES)]
        keys = ctx.enter_context(tc.tile_pool(name="keys", bufs=1))
        probs = ctx.enter_context(tc.tile_pool(name="probs", bufs=1))
        held = ctx.enter_context(tc.tile_pool(name="held", bufs=1))
        banks = ctx.enter_context(tc.psum_pool(name="banks", bufs=1))
        rows = ctx.enter_context(tc.tile_pool(name="rows", bufs=B * QT))

        offsets = keep.tile([P, B * LIST_COLS], U16, name="offsets")
        k_pool = keep.tile([P, T], I32, name="k_pool", align_bytes=64)
        ks_pool = early_v[0].tile([P, T], U8, name="ks_pool", offset=0, align_bytes=64)
        zeros = keep.tile([P, P], F32, name="zeros")
        q_planes = keep.tile([P, B * PASSES * NQ], U8, name="q_planes", align_bytes=64)
        pos_pool = keep.tile([P, T], F32, name="pos_pool")
        q_rows = early_v[0].tile([P, P], F32, name="q_rows", offset=2 * KB)
        q_down = keep.tile([P, B * QT], F32, name="q_down")
        q_edge = keep.tile([P, B * QT], F32, name="q_edge")
        ks_got = [keep.tile([P, N], U8, name=f"ks_got{b}", align_bytes=64) for b in range(B)]
        k_planes = [keep.tile([P, PASSES * N], U8, name=f"k_planes{b}", align_bytes=64) for b in range(B)]
        pos_got = [probs.tile([P, N], F32, name="pos_got0", offset=2 * KB), late_v[0].tile([P, T], F32, name="pos_got1", offset=8 * KB)[:, 0:N]]
        ident = keep.tile([P, P], F32, name="ident")
        vs_pool = keep.tile([P, T], F32, name="vs_pool")

        warm = keep.tile([P, 1], F32, name="warm")
        nc.vector.memset(warm[:], 0.0)
        nc.scalar.activation(warm[:], warm[:], ACT.Exp)

        def clear(words):
            cut = words.shape[1] // 2 + 1
            nc.vector.memset(words[:, 0:cut], 0)
            nc.vector.memset(words[:, cut:], 0)

        for b in range(B):
            nc.gpsimd.memset(pos_pool[0 : P - 1, b * SEG : (b + 1) * SEG], 0.0)
        clear(q_rows[:].bitcast(I32))
        clear(zeros[:].bitcast(I32))
        clear(ks_pool[0:96, :].bitcast(I32))
        clear(vs_pool[0 : P - 1, 0:VS_SHARE].bitcast(I32))
        nc.gpsimd.affine_select(
            out=ident[:], in_=zeros[:], compare_op=ALU.not_equal, fill=1.0, base=0, pattern=[[-1, P]], channel_multiplier=1,
        )
        nc.gpsimd.memset(vs_pool[0 : P - 1, VS_SHARE:T], 0.0)

        def load_query_scales(quad):
            nc.sync.dma_start(
                q_planes[32 * quad : 32 * quad + 4, :].bitcast(I32).rearrange("j (g q) -> j g q", g=B * PASSES),
                q_scales[:, :, 4 * quad : 4 * quad + 4, :].rearrange("b o j q -> j (b o) q").bitcast(I32),
            )

        def load_queries(b, codes):
            nc.sync.dma_start(codes[:], q_words[b].rearrange("o p q r -> p o (q r)").bitcast(I32))
            return codes

        k_flat = k_words[0].rearrange("p t r -> p (t r)").bitcast(I32)
        nc.sync.dma_start(offsets[:], offs)
        nc.sync.dma_start(ks_pool[96:P, :].bitcast(I32), k_scales.rearrange("o f t -> f o t").bitcast(I32))
        nc.sync.dma_start(pos_pool[P - 1 : P, :], pos[0:1, :])
        nc.sync.dma_start(k_pool[:, 0:SEG], k_flat[:, 0:SEG])
        nc.sync.dma_start(vs_pool[P - 1 : P, :], vs[0:1, :])
        nc.sync.dma_start(q_rows[P - 2 * B * QT + 1 : P : 2, :], qpos.rearrange("b (j p) o -> (b j) (p o)", p=P))
        for quad in range(3):
            load_query_scales(quad)
        nc.sync.dma_start(k_pool[:, SEG:T], k_flat[:, SEG:T])
        load_query_scales(3)
        q_codes = [load_queries(0, keep.tile([P, PASSES, NQ], I32, name="q_codes0", align_bytes=64))]

        def listed(b):
            return offsets[:, b * LIST_COLS : (b + 1) * LIST_COLS]

        def gather_key_scales(b):
            nc.vector.tensor_copy(ks_got[b][:], ks_pool[:, 0 : (b + 1) * SEG].indirect(listed(b)))

        def move_key_scales(b):
            for quad in range(4):
                nc.sync.dma_start(
                    k_planes[b][32 * quad : 32 * quad + 4, :].bitcast(I32),
                    ks_got[b][96 + 8 * quad : 96 + 8 * quad + 8, :].bitcast(I32),
                )

        def gather_keys(b):
            both = (early_v[1], late_v[0])[b].tile([P, N], U32, name=f"k_both{b}", offset=(7, 9)[b] * KB)
            nc.vector.tensor_copy(both[:], k_pool[:, 0 : (b + 1) * SEG].bitcast(U32).indirect(listed(b)))
            return both

        def part_keys(b, both):
            if b == 0:
                parted = late_v[0].tile([P, PASSES * 2 * N], U8, name="k_parted0", offset=11 * KB, align_bytes=64)
            else:
                parted = keep.tile([P, PASSES * 2 * N], U8, name="k_parted1", align_bytes=64)
            nc.vector.tensor_copy(
                parted[:].bitcast(U16).rearrange("p (o h n) -> p h o n", o=PASSES, h=2),
                both[:].bitcast(U16).rearrange("p (h n o) -> p h o n", o=PASSES, h=2),
            )
            return parted

        def turn_columns(sources, last, count, tag):
            turned = banks.tile([P, N], F32, name="cols_turned", tag=tag)
            if last is not None:
                shift = 2 * (count - 1)
                nc.tensor.transpose(turned[:, shift : shift + P], last, ident[:])
            for c in reversed(range(len(sources))):
                nc.tensor.transpose(turned[:, 2 * c : 2 * c + P], sources[c], ident[:])
            return turned

        def copy_columns(cols, turned):
            nc.vector.tensor_scalar(cols, turned[:, P - 1 : P - 1 + 2 * cols.shape[1] : 2], STEEP, None, ALU.mult)

        def place_row(b, cols, row):
            spread = banks.tile([P, PACK, P], F32, name="pos_spread", tag=("bank3", "bank7")[b])
            for c in range(PACK):
                nc.tensor.transpose(spread[:, c, :], cols[:, c : c + 1].to_broadcast([P, P]), ident[:])
            nc.scalar.activation(
                row[:].rearrange("p (t s) -> p t s", t=PACK), spread[:].rearrange("p c (s t) -> p t (c s)", t=PACK),
                ACT.Copy, bias=FLOOR, scale=-1.0,
            )
            return row

        def scores(b, j, parted):
            bank = banks.tile([P, N], F32, name="scores", tag=("bank1", "bank0", "bank2", "bank4")[b * QT + j])
            for o in range(PASSES):
                g = b * PASSES + o
                nc.tensor.matmul_mx(
                    out=bank[:],
                    lhsT=q_codes[b][:, o, j * P : (j + 1) * P].bitcast(FP8X4),
                    lhsT_scale=q_planes[:, g * NQ + j * P : g * NQ + (j + 1) * P],
                    rhs=parted[:, o * 2 * N : (o + 1) * 2 * N].bitcast(FP4X4),
                    rhs_scale=k_planes[b][:, o * N : (o + 1) * N],
                    start=(o == 0),
                    stop=(o == PASSES - 1),
                )
            return bank

        def mask(u, bank, pos_row):
            masked = (held if u else late_v[1]).tile([P, N], F32, name=f"masked{u}", offset=2 * KB * u if u else 7 * KB)
            nc.vector.scalar_tensor_tensor(
                masked[:].rearrange("p (t s) -> p t s", t=PACK), pos_row[:].rearrange("p (t s) -> p t s", t=PACK),
                q_edge[:, u : u + 1], bank[:].rearrange("p (s t) -> p t s", t=PACK), ALU.add, ALU.min,
            )
            return masked

        def row_top(u, masked):
            capped = keys.tile([P, N], F32, name=f"capped{u}", offset=32 + (2 * KB + 32) * u)
            top = keys.tile([P, 1], F32, name=f"top{u}", offset=(2 * KB + 32) * (u - 1) if u == 3 else 10 * KB + 32 * u)
            nc.vector.tensor_scalar(capped[:], masked[:], -MASKED, None, ALU.max, ALU.max, accum_out=top[:])
            return capped, top

        def softmax(u, capped, top, total):
            shift = rows.tile([P, 1], F32, name="shift")
            nc.gpsimd.tensor_scalar(shift[:], top[:], -1.0, 0.0, ALU.mult, ALU.add)
            p = probs.tile([P, N], F32, name=f"p{u}", offset=2 * KB * u)
            nc.scalar.activation(p[:], capped[:], ACT.Exp, bias=shift[:], accum_out=total)
            turned = banks.tile([P, PACK, P], F32, name="p_turned", tag=("bank7", "bank5", "bank6", "bank1")[u])
            for t in range(PACK):
                nc.tensor.transpose(turned[:, t, :], p[:, t * P : (t + 1) * P], ident[:])
            return turned

        def gather_values(b, h, got):
            nc.scalar.activation(got, v_pool[b, h][:].indirect(listed(b)), ACT.Copy)
            return got

        def turn_values(got, turned):
            pairs = got.bitcast(F32)
            for u in range(2):
                nc.tensor.transpose(turned[:, u, :], pairs[:, u : N // 2 : 2], ident[:])

        def group_values(target, turned, copy):
            copy(target.bitcast(F32).rearrange("p (h c u) -> p h c u", c=P, u=2), turned.rearrange("p h u c -> p h c u"))

        def weights(target, b, turned):
            nc.vector.tensor_tensor(
                target.rearrange("p (q t) -> p q t", t=PACK), turned[:].rearrange("p t q -> p q t"),
                vs_cols[b][:].unsqueeze(1).to_broadcast([P, P, PACK]), ALU.mult,
            )

        def quantise(name, source):
            words = source.shape[1] // PACK
            codes = keep.tile([P, words], U32, name=f"{name}_codes", align_bytes=64)
            plane = keep.tile([P, words], U8, name=f"{name}_plane", align_bytes=64)
            nc.vector.quantize_mx(out=codes[:].bitcast(FP8X4), scales=plane[:], in_=source)
            return codes, plane

        def product(tag, w, first, v):
            sums = banks.tile([P, v[1].shape[1]], F32, name="sums", tag=tag)
            nc.tensor.matmul_mx(
                out=sums[:], lhsT=w[0][:, first : first + P].bitcast(FP8X4), lhsT_scale=w[1][:, first : first + P],
                rhs=v[0][:].bitcast(FP8X4), rhs_scale=v[1][:], start=True, stop=True,
            )
            return sums

        def finish(u, parts):
            b, j = tiles[u]
            result = keep.tile([P, DV], F32, name=f"result{u}")
            width = DV // len(parts)
            for h, sums in enumerate(parts):
                target = result[:, h * width : (h + 1) * width]
                if u + 1 == len(tiles):
                    nc.vector.tensor_scalar(target, sums[:], inverse[:, u : u + 1], None, ALU.mult)
                else:
                    nc.scalar.activation(target, sums[:], ACT.Copy, scale=inverse[:, u : u + 1])
            nc.sync.dma_start(out[b, j * P : (j + 1) * P, :], result[:])

        tiles = [(b, j) for b in range(B) for j in range(QT)]
        nc.scalar.activation(pos_got[0][:], pos_pool[:, 0:SEG].indirect(listed(0)), ACT.Copy)
        nc.scalar.activation(pos_got[1], pos_pool[:].indirect(listed(1)), ACT.Copy)
        gather_key_scales(0)
        move_key_scales(0)
        first_turned = turn_columns([pos_got[0][:, c * P : (c + 1) * P] for c in range(PACK)], q_rows[:], PACK + B * QT, "bank0")
        v_pool = {(0, 0): early_v[0].tile([P, SEG], F32, name="v_early0", offset=2 * KB)}
        nc.sync.dma_start(v_pool[0, 0][:], vT[0:P, 0:SEG])
        gather_key_scales(1)
        q_codes.append(load_queries(1, early_v[0].tile([P, PASSES, NQ], I32, name="q_codes1", offset=0, align_bytes=64)))
        move_key_scales(1)
        first_cols = keep.tile([P, PACK + B * QT], F32, name="first_cols")[:]
        nc.scalar.activation(first_cols, first_turned[:, P - 1 : P - 1 + 2 * (PACK + B * QT) : 2], ACT.Copy, scale=STEEP)
        nc.scalar.activation(q_down[:], first_turned[:, P - 1 + 2 * PACK : P - 1 + 2 * (PACK + B * QT) : 2], ACT.Abs, scale=STEEP * NUDGE)
        vs_got = probs.tile([P, T], F32, name="vs_got", offset=2 * KB - 32)[:, 0 : B * N]
        nc.scalar.activation(vs_got, vs_pool[:].indirect(offsets[:]), ACT.Copy)
        second_turned = turn_columns([pos_got[1][:, c * P : (c + 1) * P] for c in range(PACK)], None, PACK, "bank1")
        v_pool[0, 1] = late_v[0].tile([P, SEG], F32, name="v_early1", offset=4 * KB + 32)
        nc.sync.dma_start(v_pool[0, 1][:], vT[P : 2 * P, 0:SEG])
        nc.gpsimd.tensor_tensor(q_edge[:], first_cols[:, PACK:], q_down[:], ALU.add)
        both = [gather_keys(0)]
        second_cols = keys.tile([P, 16], F32, name="second_cols", offset=12 * KB)[:, 0:PACK]
        copy_columns(second_cols, second_turned)
        pos_row = [place_row(b, (first_cols, second_cols)[b], keep.tile([P, N], F32, name=f"pos_row{b}")) for b in range(B)]
        parted = [part_keys(0, both[0])]
        v_pool[1, 0] = early_v[1].tile([P, T], F32, name="v_late0", offset=0)
        nc.sync.dma_start(v_pool[1, 0][:, SEG:T], vT[0:P, SEG:T])
        vs_cols = []
        for b in range(B):
            vs_cols.append(early_v[1].tile([P, PACK], F32, name=f"vs_cols{b}", offset=8 * KB + 32 * b))
            nc.sync.dma_start(vs_cols[b][:], vs_got[P - 1 : P, b * N : (b + 1) * N])
        both.append(gather_keys(1))
        parted.append(part_keys(1, both[1]))
        got = {(0, h): gather_values(0, h, keys.tile([P, N], BF16, name=f"got0{h}", offset=11 * KB + KB * h + 32)[:]) for h in range(HALVES)}

        total = keep.tile([P, B * QT], F32, name="total")
        inverse = keep.tile([P, B * QT], F32, name="inverse")
        tops = []
        for b in range(B):
            score = [scores(b, j, parted[b]) for j in range(QT)]
            masked = [mask(b * QT + j, score[j], pos_row[b]) for j in range(QT)]
            tops.extend(row_top(b * QT + j, masked[j]) for j in range(QT))
            if b == 0:
                v_pool[1, 1] = late_v[1].tile([P, T], F32, name="v_late1", offset=0)
                nc.sync.dma_start(v_pool[1, 1][:, SEG:T], vT[P : 2 * P, SEG:T])

        def exp_of(u):
            return softmax(u, *tops[u], total[:, u : u + 1])

        v_turned = banks.tile([P, HALVES, 2, P], F32, name="v_turned", tag="bank3")
        for h in reversed(range(HALVES)):
            turn_values(got[0, h], v_turned[:, h, :, :])
        late_turned = [banks.tile([P, 1, 2, P], F32, name="late_turned", tag=("bank2", "bank4")[h]) for h in range(HALVES)]
        turn_values(gather_values(1, 0, early_v[0].tile([P, N], BF16, name="got10", offset=2 * KB)[:]), late_turned[0][:, 0, :, :])
        p_turned = [exp_of(u) for u in range(B * QT)]
        turn_values(gather_values(1, 1, keys.tile([P, N], BF16, name="got11", offset=2 * (2 * KB + 32))[:]), late_turned[1][:, 0, :, :])
        v_grouped = keys.tile([P, DV * PACK], BF16, name="v_grouped", offset=6 * KB + 128, align_bytes=64)
        group_values(v_grouped[:], v_turned[:], nc.scalar.copy)
        late_grouped = [
            late_v[1].tile([P, N], BF16, name="late_grouped0", offset=4 * KB, align_bytes=64),
            keep.tile([P, N], BF16, name="late_grouped1", align_bytes=64),
        ]
        for h in range(HALVES):
            group_values(late_grouped[h][:], late_turned[h][:], nc.scalar.copy)

        w_first = held.tile([P, QT * N], BF16, name="w_first", offset=4 * KB, align_bytes=64)
        w_last = keep.tile([P, QT * N], BF16, name="w_last", align_bytes=64)
        for j in range(QT):
            weights(w_first[:, j * N : (j + 1) * N], 0, p_turned[j])
        weights(w_last[:, 0:N], 1, p_turned[QT])
        w_codes = quantise("w01", w_first[:])
        weights(w_last[:, N : 2 * N], 1, p_turned[QT + 1])
        nc.vector.reciprocal(inverse[:], total[:])
        v_first = quantise("v0", v_grouped[:])
        sums = [[product(("bank5", "bank1")[j], w_codes, j * P, v_first)] for j in range(QT)]
        v_last = [quantise("v10", late_grouped[0][:])]
        w_both = quantise("w23", w_last[:])
        v_last.append(quantise("v11", late_grouped[1][:]))
        sums.extend([] for j in range(QT))
        for h in range(HALVES):
            for j in range(QT):
                sums[QT + j].append(product((("bank0", "bank7"), ("bank3", "bank6"))[h][j], w_both, j * P, v_last[h]))
        for u in range(len(tiles)):
            finish(u, sums[u])
